import numpy as np
import ml_dtypes


def mxq(x, axis, fmt="e4m3"):
    dtype, down = {"e4m3": (ml_dtypes.float8_e4m3fn, 7), "e5m2": (ml_dtypes.float8_e5m2, 14)}[fmt]
    v = np.moveaxis(np.asarray(x, np.float32).astype(ml_dtypes.bfloat16).astype(np.float64), axis, -1)
    blocks = v.reshape(v.shape[:-1] + (-1, 32))
    amax = np.abs(blocks).max(-1, keepdims=True)
    byte = np.maximum(np.where(amax > 0, np.frexp(amax)[1] - 1 + 127, 0) - down, 1)
    scale = np.exp2(byte - 127.0)
    codes = (blocks / scale).astype(np.float32).astype(dtype).astype(np.float64)
    return np.moveaxis((codes * scale).reshape(v.shape), -1, axis)


WIDE = False


def mx_kscale(k):
    if not WIDE:
        return np.ones(k)
    levels = np.array([10, -10, 5, -5, 0])
    if k % 512:
        return np.exp2(np.random.permutation(np.resize(levels, k // 32))).repeat(32)
    a = np.empty((k // 512, 16))
    for p in range(k // 512):
        a[p, :8] = np.random.permutation(np.resize(levels, 8))
        for g in range(8):
            far = levels[np.abs(levels - a[p, g]) >= 10]
            a[p, g + 8] = far[np.random.randint(len(far))]
    return np.exp2(a.ravel()).repeat(32)


def f64(x):
    return np.asarray(x).astype(np.float64)


def striped(idx):
    return np.tile(idx.reshape(-1, 16).T, (8, 1)).astype(np.uint16)


def unstriped(offs):
    return offs[:16].T.reshape(-1).astype(np.int64)


def striped8(idx):
    return np.concatenate([x.reshape(-1, 16).T for x in idx]).astype(np.uint16)


def runs(offs, k):
    lists = np.stack([offs[16 * r : 16 * r + 16].T.reshape(-1) for r in range(8)]).astype(np.int64)
    return lists[np.arange(k) % 512 // 64]


def pack_weight(w):
    k, n = w.shape
    w = f64(np.asarray(w, np.float32).astype(ml_dtypes.bfloat16)).reshape(k // 32, 32, n)
    amax = np.abs(w).max(1)
    byte = np.clip(np.where(amax > 0, np.frexp(amax)[1] - 1 + 127 - 7, 1), 1, 254)
    scaled = (w * np.exp2(127.0 - byte)[:, None, :]).reshape(k, n).astype(np.float32)
    words = np.ascontiguousarray(scaled.reshape(k // 512, 128, 4, n).transpose(0, 1, 3, 2)).astype(ml_dtypes.float8_e4m3fn).view(np.uint8)
    return words, np.ascontiguousarray(byte.astype(np.uint8).reshape(k // 512, 16, n))


def unpack_weight(words, scales):
    g, p, n, _ = words.shape
    vals = np.ascontiguousarray(words).view(ml_dtypes.float8_e4m3fn).astype(np.float64) * np.repeat(np.exp2(scales.astype(np.float64) - 127.0), 8, axis=1)[..., None]
    return vals.transpose(0, 1, 3, 2).reshape(g * 512, n)


def sigmoid(v):
    return 1.0 / (1.0 + np.exp(-np.maximum(v, -700.0)))


K, T, S, V, N, H = 512, 2048, 512, 256, 512, 512


def setup_inputs():
    n = np.random.standard_normal
    s = mx_kscale(K)[:, None]
    u = mx_kscale(H)
    packed_xT = pack_weight(n((K, T)) * s)
    perm = np.stack([np.random.permutation(S) for _ in range(8)])
    return {
        "x_words": packed_xT[0],
        "x_scales": packed_xT[1],
        "w1": (n((K, H)) / np.sqrt(K) / s).astype(np.float32),
        "gn": (np.random.uniform(0.5, 1.5, (H, 1)) * u[:, None]).astype(np.float32),
        "w2": (n((H, N)) / np.sqrt(H) / u[:, None]).astype(np.float32),
        "offs": striped(np.random.permutation(T)[:S]),
        "la": striped8(perm[:, :V]),
        "lb": striped8(perm[:, V:]),
    }


def reference(x_words, x_scales, w1, gn, w2, offs, la, lb):
    xq = unpack_weight(x_words, x_scales)[:, unstriped(offs)]
    y = mxq(f64(w1), 0, "e4m3").T @ xq
    b = y[np.arange(H)[:, None], runs(lb, H)]
    a = y[np.arange(H)[:, None], runs(la, H)]
    mn = b + a * sigmoid(a)
    h = y.copy()
    h[np.arange(H)[:, None], runs(lb, H)] = mn
    z = f64(gn) * h
    o = mxq(f64(w2), 0, "e4m3").T @ mxq(z, 0, "e4m3")
    return o

@@ -1,0 +1,148 @@
+from contextlib import ExitStack
+
+import concourse.mybir as mybir
+
+K, T, S, V, N, H = 512, 2048, 512, 256, 512, 512
+FLOPS = 2 * K * H * S + 2 * H * N * S
+
+F32 = mybir.dt.float32
+BF16 = mybir.dt.bfloat16
+I32 = mybir.dt.int32
+U32 = mybir.dt.uint32
+U16 = mybir.dt.uint16
+U8 = mybir.dt.uint8
+FP8X4 = mybir.dt.float8_e4m3fn_x4
+ACT = mybir.ActivationFunctionType
+ALU = mybir.AluOpType
+
+P = 128
+PACK = 4
+HALF = S // 2
+ORDER = (2, 0, 1, 3)
+
+
+def tile_picked_revcoup_none_p_kernel(tc, x_words, x_scales, w1, gn, w2, offs, la, lb, out):
+    nc = tc.nc
+    with ExitStack() as ctx:
+        keep = ctx.enter_context(tc.tile_pool(name="keep", bufs=1))
+        psum = ctx.enter_context(tc.psum_pool(name="psum", bufs=1))
+
+        offs_t = keep.tile([P, S // 16], U16, name="offs_t")
+        la_t = keep.tile([P, V // 16], U16, name="la_t")
+        lb_t = keep.tile([P, V // 16], U16, name="lb_t")
+        xw = keep.tile([P, T], U32, name="xw", align_bytes=64)
+        xs = keep.tile([P, T], U8, name="xs", align_bytes=64)
+        w1_raw = keep.tile([P, PACK, H], F32, name="w1_raw", align_bytes=64)
+        w2_raw = keep.tile([P, PACK, N], F32, name="w2_raw", align_bytes=64)
+        gn_t = keep.tile([P, PACK], F32, name="gn_t")
+        banks = [psum.tile([P, 512], F32, name=f"bank{b}") for b in range(8)]
+
+        nc.vector.memset(xs[:].bitcast(I32), 0)
+        nc.sync.dma_start(out=w1_raw[:], in_=w1.rearrange("(p j) c -> p j c", j=PACK))
+        for q in range(4):
+            nc.sync.dma_start(out=xs[32 * q : 32 * q + 4, :].bitcast(I32), in_=x_scales[0, 4 * q : 4 * q + 4, :].bitcast(I32))
+        nc.sync.dma_start(offs_t[:], offs)
+        nc.sync.dma_start(out=xw[:].bitcast(I32), in_=x_words[0].rearrange("p n t -> p (n t)").bitcast(I32))
+        nc.sync.dma_start(la_t[:], la)
+        nc.sync.dma_start(lb_t[:], lb)
+        nc.sync.dma_start(out=gn_t[:], in_=gn.rearrange("(p t) o -> p (t o)", t=PACK))
+        nc.sync.dma_start(out=w2_raw[:], in_=w2.rearrange("(p j) c -> p j c", j=PACK))
+
+        xs_g = keep.tile([P, S], U8, name="xs_g", align_bytes=64)
+        nc.vector.tensor_copy(xs_g[:], xs[:].indirect(offs_t[:]))
+
+        w1_a = keep.tile([P, 3, P, PACK], BF16, name="w1_a", align_bytes=64)
+        w1_b = keep.tile([P, P, PACK], BF16, name="w1_b", align_bytes=64)
+        w1_by_t = w1_raw[:].rearrange("p j (m t) -> p m j t", t=PACK)
+        nc.vector.tensor_copy(out=w1_a[:].rearrange("p t m j -> p m j t"), in_=w1_by_t[:, :, :, 0:3])
+        nc.scalar.copy(out=w1_b[:], in_=w1_by_t[:, :, :, 3])
+        w1_codes = [keep.tile([P, P], U32, name=f"w1_codes{t}", align_bytes=64) for t in range(PACK)]
+        w1_scales = [keep.tile([P, P], U8, name=f"w1_scales{t}", align_bytes=64) for t in range(PACK)]
+        for t in ORDER:
+            src = w1_a[:, t, :, :] if t < 3 else w1_b[:]
+            nc.vector.quantize_mx(out=w1_codes[t][:].bitcast(FP8X4), scales=w1_scales[t][:], in_=src.rearrange("p m j -> p (m j)"))
+
+        xw_g = keep.tile([P, S], U32, name="xw_g", align_bytes=64)
+        for u in range(2):
+            nc.vector.tensor_copy(xw_g[:, u * HALF : (u + 1) * HALF], xw[:].indirect(offs_t[:, u * 16 : (u + 1) * 16]))
+
+        def product1(t, bank, cols):
+            nc.tensor.matmul_mx(out=bank, lhsT=w1_codes[t][:].bitcast(FP8X4), lhsT_scale=w1_scales[t][:],
+                                rhs=xw_g[:, cols].bitcast(FP8X4), rhs_scale=xs_g[:, cols], start=True, stop=True)
+
+        hw = [keep.tile([P, S], F32, name=f"h{t}", align_bytes=64) for t in range(PACK)]
+        first = ORDER[0]
+        s_first = keep.tile([P, S], F32, name="s_first", align_bytes=64)
+        for u in range(2):
+            cols = slice(u * HALF, (u + 1) * HALF)
+            product1(first, banks[u][:, 0:HALF], cols)
+            nc.scalar.activation(out=s_first[:, cols], in_=banks[u][:, 0:HALF], func=ACT.Silu)
+            nc.scalar.copy(out=hw[first][:, cols], in_=banks[u][:, 0:HALF])
+        for i, t in enumerate(ORDER[1:]):
+            product1(t, banks[2 + i][:], slice(0, S))
+            nc.scalar.copy(out=hw[t][:], in_=banks[2 + i][:])
+
+        a_g = [keep.tile([P, V], F32, name=f"a_g{t}", align_bytes=64) for t in range(PACK)]
+        s_g = [keep.tile([P, V], F32, name=f"s_g{t}", align_bytes=64) for t in range(PACK)]
+        b_g = [keep.tile([P, V], F32, name=f"b_g{t}", align_bytes=64) for t in range(PACK)]
+        z_g = [keep.tile([P, HALF, PACK], BF16, name=f"z_g{u}", align_bytes=64) for u in range(2)]
+        w2_g = keep.tile([P, N, PACK], BF16, name="w2_g", align_bytes=64)
+        w2_codes = keep.tile([P, N], U32, name="w2_codes", align_bytes=64)
+        w2_scales = keep.tile([P, N], U8, name="w2_scales", align_bytes=64)
+
+        def gather_a(t):
+            if t == first:
+                nc.vector.tensor_copy(s_g[t][:], s_first[:].indirect(la_t[:]))
+            else:
+                nc.vector.tensor_copy(a_g[t][:], hw[t][:].indirect(la_t[:]))
+                nc.scalar.activation(out=s_g[t][:], in_=a_g[t][:], func=ACT.Silu)
+
+        def gather_b(t):
+            nc.vector.tensor_copy(b_g[t][:], hw[t][:].indirect(lb_t[:]))
+
+        def scatter(t):
+            nc.vector.tensor_tensor(hw[t][:].indirect(lb_t[:]), b_g[t][:], s_g[t][:], ALU.add)
+
+        def plane(t, u, on_vector):
+            src = hw[t][:, u * HALF : (u + 1) * HALF]
+            if on_vector:
+                nc.vector.tensor_scalar(out=z_g[u][:, :, t], in0=src, scalar1=gn_t[:, t : t + 1], scalar2=None, op0=ALU.mult)
+            else:
+                nc.scalar.activation(out=z_g[u][:, :, t], in_=src, func=ACT.Copy, scale=gn_t[:, t : t + 1])
+
+        def w2_piece(c):
+            cols = slice(c * P, (c + 1) * P)
+            nc.scalar.copy(out=w2_g[:, cols, :].rearrange("p (b i) j -> p b j i", i=4),
+                           in_=w2_raw[:, :, cols].rearrange("p j (b i) -> p b j i", i=4))
+
+        gather_a(first)
+        gather_b(first)
+        for t in ORDER[1:]:
+            gather_a(t)
+        for c in range(4):
+            w2_piece(c)
+        for i, t in enumerate(ORDER):
+            if i + 1 < PACK:
+                gather_b(ORDER[i + 1])
+            else:
+                nc.vector.quantize_mx(out=w2_codes[:].bitcast(FP8X4), scales=w2_scales[:], in_=w2_g[:].rearrange("p n j -> p (n j)"))
+            scatter(t)
+            for u in range(2):
+                plane(t, u, i == 3 and u == 0)
+
+        z_codes = [keep.tile([P, HALF], U32, name=f"z_codes{u}", align_bytes=64) for u in range(2)]
+        z_scales = [keep.tile([P, HALF], U8, name=f"z_scales{u}", align_bytes=64) for u in range(2)]
+        for u in range(2):
+            nc.vector.quantize_mx(out=z_codes[u][:].bitcast(FP8X4), scales=z_scales[u][:], in_=z_g[u][:].rearrange("p n j -> p (n j)"))
+        for u in range(2):
+            for m in range(4):
+                rows = slice(m * P, (m + 1) * P)
+                bank = banks[4 * u + m]
+                nc.tensor.matmul_mx(out=bank[:, 0:HALF], lhsT=w2_codes[:, rows].bitcast(FP8X4), lhsT_scale=w2_scales[:, rows],
+                                    rhs=z_codes[u][:].bitcast(FP8X4), rhs_scale=z_scales[u][:], start=True, stop=True)
+                res = keep.tile([P, HALF], F32, name=f"res{u}{m}", align_bytes=64)
+                if m % 2 == 0:
+                    nc.vector.tensor_copy(out=res[:], in_=bank[:, 0:HALF])
+                else:
+                    nc.scalar.copy(out=res[:], in_=bank[:, 0:HALF])
+                nc.sync.dma_start(out=out[rows, u * HALF : (u + 1) * HALF], in_=res[:])

@@ -18,13 +18,15 @@ ALU = mybir.AluOpType
 P = 128
 PACK = 4
 HALF = S // 2
-ORDER = (2, 0, 1, 3)
+ORDER = (0, 1, 2, 3)
+CHUNKS = ((0, 0, 128), (0, 128, 256), (1, 0, 256))
 
 
 def tile_picked_revcoup_none_p_kernel(tc, x_words, x_scales, w1, gn, w2, offs, la, lb, out):
     nc = tc.nc
     with ExitStack() as ctx:
         keep = ctx.enter_context(tc.tile_pool(name="keep", bufs=1))
+        ring = ctx.enter_context(tc.tile_pool(name="ring", bufs=2))
         psum = ctx.enter_context(tc.psum_pool(name="psum", bufs=1))
 
         offs_t = keep.tile([P, S // 16], U16, name="offs_t")
@@ -33,33 +35,38 @@ def tile_picked_revcoup_none_p_kernel(tc, x_words, x_scales, w1, gn, w2, offs, l
         xw = keep.tile([P, T], U32, name="xw", align_bytes=64)
         xs = keep.tile([P, T], U8, name="xs", align_bytes=64)
         w1_raw = keep.tile([P, PACK, H], F32, name="w1_raw", align_bytes=64)
-        w2_raw = keep.tile([P, PACK, N], F32, name="w2_raw", align_bytes=64)
+        w2_raw = [keep.tile([P, PACK, N // 2], F32, name=f"w2_raw{u}", tag=f"stage{u}", align_bytes=64) for u in range(2)]
         gn_t = keep.tile([P, PACK], F32, name="gn_t")
         banks = [psum.tile([P, 512], F32, name=f"bank{b}") for b in range(8)]
 
         nc.vector.memset(xs[:].bitcast(I32), 0)
-        nc.sync.dma_start(out=w1_raw[:], in_=w1.rearrange("(p j) c -> p j c", j=PACK))
+        warm = keep.tile([P, 2], F32, name="warm")
+        nc.gpsimd.memset(warm[:, 0:1], 0.0)
+        nc.scalar.activation(out=warm[:, 1:2], in_=warm[:, 0:1], func=ACT.Silu)
+        w1_rows = w1.rearrange("(p j) c -> p j c", j=PACK)
+        nc.sync.dma_start(out=w1_raw[:, 0:2, :], in_=w1_rows[:, 0:2, :])
         for q in range(4):
             nc.sync.dma_start(out=xs[32 * q : 32 * q + 4, :].bitcast(I32), in_=x_scales[0, 4 * q : 4 * q + 4, :].bitcast(I32))
         nc.sync.dma_start(offs_t[:], offs)
+        nc.sync.dma_start(out=w1_raw[:, 2:4, :], in_=w1_rows[:, 2:4, :])
         nc.sync.dma_start(out=xw[:].bitcast(I32), in_=x_words[0].rearrange("p n t -> p (n t)").bitcast(I32))
         nc.sync.dma_start(la_t[:], la)
         nc.sync.dma_start(lb_t[:], lb)
         nc.sync.dma_start(out=gn_t[:], in_=gn.rearrange("(p t) o -> p (t o)", t=PACK))
-        nc.sync.dma_start(out=w2_raw[:], in_=w2.rearrange("(p j) c -> p j c", j=PACK))
+        w2_rows = w2.rearrange("(p j) c -> p j c", j=PACK)
+        for u in range(2):
+            nc.sync.dma_start(out=w2_raw[u][:], in_=w2_rows[:, :, u * (N // 2) : (u + 1) * (N // 2)])
 
         xs_g = keep.tile([P, S], U8, name="xs_g", align_bytes=64)
         nc.vector.tensor_copy(xs_g[:], xs[:].indirect(offs_t[:]))
 
-        w1_a = keep.tile([P, 3, P, PACK], BF16, name="w1_a", align_bytes=64)
-        w1_b = keep.tile([P, P, PACK], BF16, name="w1_b", align_bytes=64)
+        w1_a = keep.tile([P, PACK, P, PACK], BF16, name="w1_a", align_bytes=64)
         w1_by_t = w1_raw[:].rearrange("p j (m t) -> p m j t", t=PACK)
-        nc.vector.tensor_copy(out=w1_a[:].rearrange("p t m j -> p m j t"), in_=w1_by_t[:, :, :, 0:3])
-        nc.scalar.copy(out=w1_b[:], in_=w1_by_t[:, :, :, 3])
+        nc.vector.tensor_copy(out=w1_a[:].rearrange("p t m j -> p m j t"), in_=w1_by_t)
         w1_codes = [keep.tile([P, P], U32, name=f"w1_codes{t}", align_bytes=64) for t in range(PACK)]
         w1_scales = [keep.tile([P, P], U8, name=f"w1_scales{t}", align_bytes=64) for t in range(PACK)]
         for t in ORDER:
-            src = w1_a[:, t, :, :] if t < 3 else w1_b[:]
+            src = w1_a[:, t, :, :]
             nc.vector.quantize_mx(out=w1_codes[t][:].bitcast(FP8X4), scales=w1_scales[t][:], in_=src.rearrange("p m j -> p (m j)"))
 
         xw_g = keep.tile([P, S], U32, name="xw_g", align_bytes=64)
@@ -72,77 +79,71 @@ def tile_picked_revcoup_none_p_kernel(tc, x_words, x_scales, w1, gn, w2, offs, l
 
         hw = [keep.tile([P, S], F32, name=f"h{t}", align_bytes=64) for t in range(PACK)]
         first = ORDER[0]
-        s_first = keep.tile([P, S], F32, name="s_first", align_bytes=64)
         for u in range(2):
             cols = slice(u * HALF, (u + 1) * HALF)
             product1(first, banks[u][:, 0:HALF], cols)
-            nc.scalar.activation(out=s_first[:, cols], in_=banks[u][:, 0:HALF], func=ACT.Silu)
             nc.scalar.copy(out=hw[first][:, cols], in_=banks[u][:, 0:HALF])
         for i, t in enumerate(ORDER[1:]):
             product1(t, banks[2 + i][:], slice(0, S))
             nc.scalar.copy(out=hw[t][:], in_=banks[2 + i][:])
 
-        a_g = [keep.tile([P, V], F32, name=f"a_g{t}", align_bytes=64) for t in range(PACK)]
+        a_g = [keep.tile([P, V], F32, name=f"a_g{t}", tag=f"looked{t + 1}", align_bytes=64) for t in range(PACK)]
         s_g = [keep.tile([P, V], F32, name=f"s_g{t}", align_bytes=64) for t in range(PACK)]
-        b_g = [keep.tile([P, V], F32, name=f"b_g{t}", align_bytes=64) for t in range(PACK)]
-        z_g = [keep.tile([P, HALF, PACK], BF16, name=f"z_g{u}", align_bytes=64) for u in range(2)]
         w2_g = keep.tile([P, N, PACK], BF16, name="w2_g", align_bytes=64)
         w2_codes = keep.tile([P, N], U32, name="w2_codes", align_bytes=64)
         w2_scales = keep.tile([P, N], U8, name="w2_scales", align_bytes=64)
 
-        def gather_a(t):
-            if t == first:
-                nc.vector.tensor_copy(s_g[t][:], s_first[:].indirect(la_t[:]))
-            else:
-                nc.vector.tensor_copy(a_g[t][:], hw[t][:].indirect(la_t[:]))
-                nc.scalar.activation(out=s_g[t][:], in_=a_g[t][:], func=ACT.Silu)
-
         def gather_b(t):
-            nc.vector.tensor_copy(b_g[t][:], hw[t][:].indirect(lb_t[:]))
+            b = keep.tile([P, V], F32, name=f"b_g{t}", tag=f"looked{t}", align_bytes=64)
+            nc.vector.tensor_copy(b[:], hw[t][:].indirect(lb_t[:]))
+            return b
 
-        def scatter(t):
-            nc.vector.tensor_tensor(hw[t][:].indirect(lb_t[:]), b_g[t][:], s_g[t][:], ALU.add)
-
-        def plane(t, u, on_vector):
-            src = hw[t][:, u * HALF : (u + 1) * HALF]
-            if on_vector:
-                nc.vector.tensor_scalar(out=z_g[u][:, :, t], in0=src, scalar1=gn_t[:, t : t + 1], scalar2=None, op0=ALU.mult)
-            else:
-                nc.scalar.activation(out=z_g[u][:, :, t], in_=src, func=ACT.Copy, scale=gn_t[:, t : t + 1])
+        def plane(t, u, lo, hi):
+            src = hw[t][:, u * HALF + lo : u * HALF + hi]
+            nc.scalar.activation(out=z_g[u][:, lo:hi, t], in_=src, func=ACT.Copy, scale=gn_t[:, t : t + 1])
 
         def w2_piece(c):
             cols = slice(c * P, (c + 1) * P)
             nc.scalar.copy(out=w2_g[:, cols, :].rearrange("p (b i) j -> p b j i", i=4),
-                           in_=w2_raw[:, :, cols].rearrange("p j (b i) -> p b j i", i=4))
+                           in_=w2_raw[c // 2][:, :, (c % 2) * P : (c % 2 + 1) * P].rearrange("p j (b i) -> p b j i", i=4))
 
-        gather_a(first)
-        gather_b(first)
-        for t in ORDER[1:]:
-            gather_a(t)
+        b_g = []
+        for t in range(PACK):
+            nc.vector.tensor_copy(a_g[t][:], hw[t][:].indirect(la_t[:]))
+            if t == 0:
+                b_g.append(gather_b(0))
+        for t in range(PACK):
+            nc.scalar.activation(out=s_g[t][:], in_=a_g[t][:], func=ACT.Silu)
         for c in range(4):
             w2_piece(c)
-        for i, t in enumerate(ORDER):
-            if i + 1 < PACK:
-                gather_b(ORDER[i + 1])
-            else:
-                nc.vector.quantize_mx(out=w2_codes[:].bitcast(FP8X4), scales=w2_scales[:], in_=w2_g[:].rearrange("p n j -> p (n j)"))
-            scatter(t)
-            for u in range(2):
-                plane(t, u, i == 3 and u == 0)
+        z_g = [keep.tile([P, HALF, PACK], BF16, name=f"z_g{u}", tag=f"stage{u}", align_bytes=64) for u in range(2)]
+        for t in range(PACK):
+            if t + 1 < PACK:
+                b_g.append(gather_b(t + 1))
+            nc.vector.tensor_tensor(hw[t][:].indirect(lb_t[:]), b_g[t][:], s_g[t][:], ALU.add)
+            for u, lo, hi in CHUNKS if t == PACK - 1 else ((0, 0, HALF), (1, 0, HALF)):
+                plane(t, u, lo, hi)
+        nc.vector.quantize_mx(out=w2_codes[:].bitcast(FP8X4), scales=w2_scales[:], in_=w2_g[:].rearrange("p n j -> p (n j)"))
 
-        z_codes = [keep.tile([P, HALF], U32, name=f"z_codes{u}", align_bytes=64) for u in range(2)]
-        z_scales = [keep.tile([P, HALF], U8, name=f"z_scales{u}", align_bytes=64) for u in range(2)]
-        for u in range(2):
-            nc.vector.quantize_mx(out=z_codes[u][:].bitcast(FP8X4), scales=z_scales[u][:], in_=z_g[u][:].rearrange("p n j -> p (n j)"))
-        for u in range(2):
-            for m in range(4):
-                rows = slice(m * P, (m + 1) * P)
-                bank = banks[4 * u + m]
-                nc.tensor.matmul_mx(out=bank[:, 0:HALF], lhsT=w2_codes[:, rows].bitcast(FP8X4), lhsT_scale=w2_scales[:, rows],
-                                    rhs=z_codes[u][:].bitcast(FP8X4), rhs_scale=z_scales[u][:], start=True, stop=True)
-                res = keep.tile([P, HALF], F32, name=f"res{u}{m}", align_bytes=64)
-                if m % 2 == 0:
+        n = 0
+        for u, lo, hi in CHUNKS:
+            cols = slice(u * HALF + lo, u * HALF + hi)
+            width = hi - lo
+            per_bank = HALF // width
+            z_codes = ring.tile([P, width], U32, name="z_codes", align_bytes=64)
+            z_scales = ring.tile([P, width], U8, name="z_scales", align_bytes=64)
+            nc.vector.quantize_mx(out=z_codes[:].bitcast(FP8X4), scales=z_scales[:], in_=z_g[u][:, lo:hi, :].rearrange("p n j -> p (n j)"))
+            for m0 in range(0, 4, per_bank):
+                bank = banks[n]
+                for i in range(per_bank):
+                    rows = slice((m0 + i) * P, (m0 + i + 1) * P)
+                    nc.tensor.matmul_mx(out=bank[:, i * width : (i + 1) * width], lhsT=w2_codes[:, rows].bitcast(FP8X4), lhsT_scale=w2_scales[:, rows],
+                                        rhs=z_codes[:].bitcast(FP8X4), rhs_scale=z_scales[:], start=True, stop=True)
+                res = keep.tile([P, HALF], F32, name=f"res{n}", align_bytes=64)
+                if n % 2 == 0:
                     nc.vector.tensor_copy(out=res[:], in_=bank[:, 0:HALF])
                 else:
                     nc.scalar.copy(out=res[:], in_=bank[:, 0:HALF])
-                nc.sync.dma_start(out=out[rows, u * HALF : (u + 1) * HALF], in_=res[:])
+                nc.sync.dma_start(out=out[m0 * P : (m0 + per_bank) * P, cols].rearrange("(i p) c -> p i c", p=P),
+                                  in_=res[:].rearrange("p (i c) -> p i c", i=per_bank))
+                n = n + 1

@@ -60,13 +60,14 @@ def tile_picked_revcoup_none_p_kernel(tc, x_words, x_scales, w1, gn, w2, offs, l
         xs_g = keep.tile([P, S], U8, name="xs_g", align_bytes=64)
         nc.vector.tensor_copy(xs_g[:], xs[:].indirect(offs_t[:]))
 
-        w1_a = keep.tile([P, PACK, P, PACK], BF16, name="w1_a", align_bytes=64)
+        w1_g = [keep.tile([P, 2, P, PACK], BF16, name=f"w1_g{u}", align_bytes=64) for u in range(2)]
         w1_by_t = w1_raw[:].rearrange("p j (m t) -> p m j t", t=PACK)
-        nc.vector.tensor_copy(out=w1_a[:].rearrange("p t m j -> p m j t"), in_=w1_by_t)
+        nc.vector.tensor_copy(out=w1_g[0][:].rearrange("p t m j -> p m j t"), in_=w1_by_t[:, :, :, 0:2])
+        nc.scalar.copy(out=w1_g[1][:].rearrange("p t m j -> p m j t"), in_=w1_by_t[:, :, :, 2:4])
         w1_codes = [keep.tile([P, P], U32, name=f"w1_codes{t}", align_bytes=64) for t in range(PACK)]
         w1_scales = [keep.tile([P, P], U8, name=f"w1_scales{t}", align_bytes=64) for t in range(PACK)]
         for t in ORDER:
-            src = w1_a[:, t, :, :]
+            src = w1_g[t // 2][:, t % 2, :, :]
             nc.vector.quantize_mx(out=w1_codes[t][:].bitcast(FP8X4), scales=w1_scales[t][:], in_=src.rearrange("p m j -> p (m j)"))
 
         xw_g = keep.tile([P, S], U32, name="xw_g", align_bytes=64)
@@ -78,14 +79,10 @@ def tile_picked_revcoup_none_p_kernel(tc, x_words, x_scales, w1, gn, w2, offs, l
                                 rhs=xw_g[:, cols].bitcast(FP8X4), rhs_scale=xs_g[:, cols], start=True, stop=True)
 
         hw = [keep.tile([P, S], F32, name=f"h{t}", align_bytes=64) for t in range(PACK)]
-        first = ORDER[0]
-        for u in range(2):
-            cols = slice(u * HALF, (u + 1) * HALF)
-            product1(first, banks[u][:, 0:HALF], cols)
-            nc.scalar.copy(out=hw[first][:, cols], in_=banks[u][:, 0:HALF])
-        for i, t in enumerate(ORDER[1:]):
-            product1(t, banks[2 + i][:], slice(0, S))
-            nc.scalar.copy(out=hw[t][:], in_=banks[2 + i][:])
+        for n, (t, cols) in enumerate(((0, slice(0, HALF)), (1, slice(0, HALF)), (0, slice(HALF, S)), (1, slice(HALF, S)), (2, slice(0, S)), (3, slice(0, S)))):
+            width = cols.stop - cols.start
+            product1(t, banks[n][:, 0:width], cols)
+            nc.scalar.copy(out=hw[t][:, cols], in_=banks[n][:, 0:width])
 
         a_g = [keep.tile([P, V], F32, name=f"a_g{t}", tag=f"looked{t + 1}", align_bytes=64) for t in range(PACK)]
         s_g = [keep.tile([P, V], F32, name=f"s_g{t}", align_bytes=64) for t in range(PACK)]

@@ -19,7 +19,7 @@ P = 128
 PACK = 4
 HALF = S // 2
 ORDER = (0, 1, 2, 3)
-CHUNKS = ((0, 0, 128), (0, 128, 256), (1, 0, 256))
+CHUNKS = ((0, 128), (128, 256), (256, 512))
 
 
 def tile_picked_revcoup_none_p_kernel(tc, x_words, x_scales, w1, gn, w2, offs, la, lb, out):
@@ -33,9 +33,8 @@ def tile_picked_revcoup_none_p_kernel(tc, x_words, x_scales, w1, gn, w2, offs, l
         la_t = keep.tile([P, V // 16], U16, name="la_t")
         lb_t = keep.tile([P, V // 16], U16, name="lb_t")
         xw = keep.tile([P, T], U32, name="xw", align_bytes=64)
-        xs = keep.tile([P, T], U8, name="xs", align_bytes=64)
+        xs = keep.tile([P, T], U8, name="xs", tag="stage", align_bytes=64)
         w1_raw = keep.tile([P, PACK, H], F32, name="w1_raw", align_bytes=64)
-        w2_raw = [keep.tile([P, PACK, N // 2], F32, name=f"w2_raw{u}", tag=f"stage{u}", align_bytes=64) for u in range(2)]
         gn_t = keep.tile([P, PACK], F32, name="gn_t")
         banks = [psum.tile([P, 512], F32, name=f"bank{b}") for b in range(8)]
 
@@ -45,20 +44,22 @@ def tile_picked_revcoup_none_p_kernel(tc, x_words, x_scales, w1, gn, w2, offs, l
         nc.scalar.activation(out=warm[:, 1:2], in_=warm[:, 0:1], func=ACT.Silu)
         w1_rows = w1.rearrange("(p j) c -> p j c", j=PACK)
         nc.sync.dma_start(out=w1_raw[:, 0:2, :], in_=w1_rows[:, 0:2, :])
-        for q in range(4):
-            nc.sync.dma_start(out=xs[32 * q : 32 * q + 4, :].bitcast(I32), in_=x_scales[0, 4 * q : 4 * q + 4, :].bitcast(I32))
+        nc.sync.dma_start(out=xs[0:P:8, :].bitcast(I32), in_=x_scales[0].bitcast(I32))
         nc.sync.dma_start(offs_t[:], offs)
         nc.sync.dma_start(out=w1_raw[:, 2:4, :], in_=w1_rows[:, 2:4, :])
         nc.sync.dma_start(out=xw[:].bitcast(I32), in_=x_words[0].rearrange("p n t -> p (n t)").bitcast(I32))
         nc.sync.dma_start(la_t[:], la)
         nc.sync.dma_start(lb_t[:], lb)
         nc.sync.dma_start(out=gn_t[:], in_=gn.rearrange("(p t) o -> p (t o)", t=PACK))
-        w2_rows = w2.rearrange("(p j) c -> p j c", j=PACK)
-        for u in range(2):
-            nc.sync.dma_start(out=w2_raw[u][:], in_=w2_rows[:, :, u * (N // 2) : (u + 1) * (N // 2)])
 
+        xs_p = keep.tile([P, S], U8, name="xs_p", align_bytes=64)
+        nc.vector.tensor_copy(xs_p[:], xs[:].indirect(offs_t[:]))
         xs_g = keep.tile([P, S], U8, name="xs_g", align_bytes=64)
-        nc.vector.tensor_copy(xs_g[:], xs[:].indirect(offs_t[:]))
+        nc.gpsimd.memset(xs_g[:].bitcast(I32), 0)
+        for r in range(4):
+            nc.sync.dma_start(out=xs_g[r:P:32, :].bitcast(I32), in_=xs_p[8 * r : P : 32, :].bitcast(I32))
+        w2_raw = keep.tile([P, PACK, N], F32, name="w2_raw", tag="stage", align_bytes=64)
+        nc.sync.dma_start(out=w2_raw[:], in_=w2.rearrange("(p j) c -> p j c", j=PACK))
 
         w1_g = [keep.tile([P, 2, P, PACK], BF16, name=f"w1_g{u}", align_bytes=64) for u in range(2)]
         w1_by_t = w1_raw[:].rearrange("p j (m t) -> p m j t", t=PACK)
@@ -95,14 +96,14 @@ def tile_picked_revcoup_none_p_kernel(tc, x_words, x_scales, w1, gn, w2, offs, l
             nc.vector.tensor_copy(b[:], hw[t][:].indirect(lb_t[:]))
             return b
 
-        def plane(t, u, lo, hi):
-            src = hw[t][:, u * HALF + lo : u * HALF + hi]
-            nc.scalar.activation(out=z_g[u][:, lo:hi, t], in_=src, func=ACT.Copy, scale=gn_t[:, t : t + 1])
+        def plane(t, lo, hi):
+            src = hw[t][:, lo:hi]
+            nc.scalar.activation(out=z_g[:, lo:hi, t], in_=src, func=ACT.Copy, scale=gn_t[:, t : t + 1])
 
         def w2_piece(c):
             cols = slice(c * P, (c + 1) * P)
             nc.scalar.copy(out=w2_g[:, cols, :].rearrange("p (b i) j -> p b j i", i=4),
-                           in_=w2_raw[c // 2][:, :, (c % 2) * P : (c % 2 + 1) * P].rearrange("p j (b i) -> p b j i", i=4))
+                           in_=w2_raw[:, :, cols].rearrange("p j (b i) -> p b j i", i=4))
 
         b_g = []
         for t in range(PACK):
@@ -113,23 +114,23 @@ def tile_picked_revcoup_none_p_kernel(tc, x_words, x_scales, w1, gn, w2, offs, l
             nc.scalar.activation(out=s_g[t][:], in_=a_g[t][:], func=ACT.Silu)
         for c in range(4):
             w2_piece(c)
-        z_g = [keep.tile([P, HALF, PACK], BF16, name=f"z_g{u}", tag=f"stage{u}", align_bytes=64) for u in range(2)]
+        z_g = keep.tile([P, S, PACK], BF16, name="z_g", tag="stage", align_bytes=64)
         for t in range(PACK):
             if t + 1 < PACK:
                 b_g.append(gather_b(t + 1))
             nc.vector.tensor_tensor(hw[t][:].indirect(lb_t[:]), b_g[t][:], s_g[t][:], ALU.add)
-            for u, lo, hi in CHUNKS if t == PACK - 1 else ((0, 0, HALF), (1, 0, HALF)):
-                plane(t, u, lo, hi)
+            for lo, hi in CHUNKS if t == PACK - 1 else ((0, S),):
+                plane(t, lo, hi)
         nc.vector.quantize_mx(out=w2_codes[:].bitcast(FP8X4), scales=w2_scales[:], in_=w2_g[:].rearrange("p n j -> p (n j)"))
 
         n = 0
-        for u, lo, hi in CHUNKS:
-            cols = slice(u * HALF + lo, u * HALF + hi)
+        for lo, hi in CHUNKS:
+            cols = slice(lo, hi)
             width = hi - lo
             per_bank = HALF // width
             z_codes = ring.tile([P, width], U32, name="z_codes", align_bytes=64)
             z_scales = ring.tile([P, width], U8, name="z_scales", align_bytes=64)
-            nc.vector.quantize_mx(out=z_codes[:].bitcast(FP8X4), scales=z_scales[:], in_=z_g[u][:, lo:hi, :].rearrange("p n j -> p (n j)"))
+            nc.vector.quantize_mx(out=z_codes[:].bitcast(FP8X4), scales=z_scales[:], in_=z_g[:, lo:hi, :].rearrange("p n j -> p (n j)"))
             for m0 in range(0, 4, per_bank):
                 bank = banks[n]
                 for i in range(per_bank):

@@ -34,8 +34,7 @@ def tile_picked_revcoup_none_p_kernel(tc, x_words, x_scales, w1, gn, w2, offs, l
         lb_t = keep.tile([P, V // 16], U16, name="lb_t")
         xw = keep.tile([P, T], U32, name="xw", align_bytes=64)
         xs = keep.tile([P, T], U8, name="xs", tag="stage", align_bytes=64)
-        w1_raw = keep.tile([P, PACK, H], F32, name="w1_raw", align_bytes=64)
-        gn_t = keep.tile([P, PACK], F32, name="gn_t")
+        w1_raw = [keep.tile([P, 2, H], F32, name=f"w1_raw{u}", tag=f"w1_raw{u}", align_bytes=64) for u in range(2)]
         banks = [psum.tile([P, 512], F32, name=f"bank{b}") for b in range(8)]
 
         nc.vector.memset(xs[:].bitcast(I32), 0)
@@ -43,50 +42,58 @@ def tile_picked_revcoup_none_p_kernel(tc, x_words, x_scales, w1, gn, w2, offs, l
         nc.gpsimd.memset(warm[:, 0:1], 0.0)
         nc.scalar.activation(out=warm[:, 1:2], in_=warm[:, 0:1], func=ACT.Silu)
         w1_rows = w1.rearrange("(p j) c -> p j c", j=PACK)
-        nc.sync.dma_start(out=w1_raw[:, 0:2, :], in_=w1_rows[:, 0:2, :])
+        nc.sync.dma_start(out=w1_raw[0][:], in_=w1_rows[:, 0:2, :])
         nc.sync.dma_start(out=xs[0:P:8, :].bitcast(I32), in_=x_scales[0].bitcast(I32))
         nc.sync.dma_start(offs_t[:], offs)
-        nc.sync.dma_start(out=w1_raw[:, 2:4, :], in_=w1_rows[:, 2:4, :])
         nc.sync.dma_start(out=xw[:].bitcast(I32), in_=x_words[0].rearrange("p n t -> p (n t)").bitcast(I32))
+        nc.sync.dma_start(out=w1_raw[1][:], in_=w1_rows[:, 2:4, :])
         nc.sync.dma_start(la_t[:], la)
         nc.sync.dma_start(lb_t[:], lb)
-        nc.sync.dma_start(out=gn_t[:], in_=gn.rearrange("(p t) o -> p (t o)", t=PACK))
 
-        xs_p = keep.tile([P, S], U8, name="xs_p", align_bytes=64)
+        xs_p = keep.tile([P, S], U8, name="xs_p", tag="stage2", align_bytes=64)
         nc.vector.tensor_copy(xs_p[:], xs[:].indirect(offs_t[:]))
         xs_g = keep.tile([P, S], U8, name="xs_g", align_bytes=64)
         nc.gpsimd.memset(xs_g[:].bitcast(I32), 0)
         for r in range(4):
             nc.sync.dma_start(out=xs_g[r:P:32, :].bitcast(I32), in_=xs_p[8 * r : P : 32, :].bitcast(I32))
-        w2_raw = keep.tile([P, PACK, N], F32, name="w2_raw", tag="stage", align_bytes=64)
-        nc.sync.dma_start(out=w2_raw[:], in_=w2.rearrange("(p j) c -> p j c", j=PACK))
+        w2_rows = w2.rearrange("(p j) c -> p j c", j=PACK)
+        w2_raw = [keep.tile([P, PACK, N // 2], F32, name=f"w2_raw{u}", tag=("stage", "stage2")[u], align_bytes=64) for u in range(2)]
+        for u in range(2):
+            nc.sync.dma_start(out=w2_raw[u][:], in_=w2_rows[:, :, u * (N // 2) : (u + 1) * (N // 2)])
 
         w1_g = [keep.tile([P, 2, P, PACK], BF16, name=f"w1_g{u}", align_bytes=64) for u in range(2)]
-        w1_by_t = w1_raw[:].rearrange("p j (m t) -> p m j t", t=PACK)
-        nc.vector.tensor_copy(out=w1_g[0][:].rearrange("p t m j -> p m j t"), in_=w1_by_t[:, :, :, 0:2])
-        nc.scalar.copy(out=w1_g[1][:].rearrange("p t m j -> p m j t"), in_=w1_by_t[:, :, :, 2:4])
+        xw_g = keep.tile([P, S], U32, name="xw_g", align_bytes=64)
+        for u in range(2):
+            w1_by_t = w1_raw[u][:].rearrange("p j (m t) -> p m j t", t=PACK)
+            slots = slice(2 * u, 2 * u + 2)
+            for lo, hi in ((0, 2),) if u == 0 else ((0, 1), (1, 2)):
+                nc.vector.tensor_copy(out=w1_g[0][:, lo:hi, :, slots].rearrange("p t m j -> p m j t"), in_=w1_by_t[:, :, :, lo:hi])
+            nc.scalar.copy(out=w1_g[1][:, :, :, slots].rearrange("p t m j -> p m j t"), in_=w1_by_t[:, :, :, 2:4])
+            if u == 0:
+                nc.vector.tensor_copy(xw_g[:], xw[:].indirect(offs_t[:]))
+        gn_t = keep.tile([P, PACK], F32, name="gn_t", tag="w1_raw0", align_bytes=64)
+        nc.sync.dma_start(out=gn_t[:], in_=gn.rearrange("(p t) o -> p (t o)", t=PACK))
         w1_codes = [keep.tile([P, P], U32, name=f"w1_codes{t}", align_bytes=64) for t in range(PACK)]
         w1_scales = [keep.tile([P, P], U8, name=f"w1_scales{t}", align_bytes=64) for t in range(PACK)]
         for t in ORDER:
             src = w1_g[t // 2][:, t % 2, :, :]
             nc.vector.quantize_mx(out=w1_codes[t][:].bitcast(FP8X4), scales=w1_scales[t][:], in_=src.rearrange("p m j -> p (m j)"))
 
-        xw_g = keep.tile([P, S], U32, name="xw_g", align_bytes=64)
-        for u in range(2):
-            nc.vector.tensor_copy(xw_g[:, u * HALF : (u + 1) * HALF], xw[:].indirect(offs_t[:, u * 16 : (u + 1) * 16]))
-
         def product1(t, bank, cols):
             nc.tensor.matmul_mx(out=bank, lhsT=w1_codes[t][:].bitcast(FP8X4), lhsT_scale=w1_scales[t][:],
                                 rhs=xw_g[:, cols].bitcast(FP8X4), rhs_scale=xs_g[:, cols], start=True, stop=True)
 
         hw = [keep.tile([P, S], F32, name=f"h{t}", align_bytes=64) for t in range(PACK)]
-        for n, (t, cols) in enumerate(((0, slice(0, HALF)), (1, slice(0, HALF)), (0, slice(HALF, S)), (1, slice(HALF, S)), (2, slice(0, S)), (3, slice(0, S)))):
+        for n, (t, cols) in enumerate(((0, slice(0, P)), (0, slice(P, 2 * P)), (0, slice(2 * P, 3 * P)), (0, slice(3 * P, S)), (1, slice(0, S)), (2, slice(0, S)), (3, slice(0, S)))):
             width = cols.stop - cols.start
             product1(t, banks[n][:, 0:width], cols)
-            nc.scalar.copy(out=hw[t][:, cols], in_=banks[n][:, 0:width])
+            if n in (0, 2):
+                nc.vector.tensor_copy(out=hw[t][:, cols], in_=banks[n][:, 0:width])
+            else:
+                nc.scalar.copy(out=hw[t][:, cols], in_=banks[n][:, 0:width])
 
         a_g = [keep.tile([P, V], F32, name=f"a_g{t}", tag=f"looked{t + 1}", align_bytes=64) for t in range(PACK)]
-        s_g = [keep.tile([P, V], F32, name=f"s_g{t}", align_bytes=64) for t in range(PACK)]
+        s_g = [keep.tile([P, V], F32, name=f"s_g{t}", align_bytes=64)[:] for t in range(2)]
         w2_g = keep.tile([P, N, PACK], BF16, name="w2_g", align_bytes=64)
         w2_codes = keep.tile([P, N], U32, name="w2_codes", align_bytes=64)
         w2_scales = keep.tile([P, N], U8, name="w2_scales", align_bytes=64)
@@ -103,22 +110,28 @@ def tile_picked_revcoup_none_p_kernel(tc, x_words, x_scales, w1, gn, w2, offs, l
         def w2_piece(c):
             cols = slice(c * P, (c + 1) * P)
             nc.scalar.copy(out=w2_g[:, cols, :].rearrange("p (b i) j -> p b j i", i=4),
-                           in_=w2_raw[:, :, cols].rearrange("p j (b i) -> p b j i", i=4))
+                           in_=w2_raw[c // 2][:, :, (c % 2) * P : (c % 2 + 1) * P].rearrange("p j (b i) -> p b j i", i=4))
 
         b_g = []
         for t in range(PACK):
             nc.vector.tensor_copy(a_g[t][:], hw[t][:].indirect(la_t[:]))
             if t == 0:
                 b_g.append(gather_b(0))
-        for t in range(PACK):
-            nc.scalar.activation(out=s_g[t][:], in_=a_g[t][:], func=ACT.Silu)
-        for c in range(4):
+        for t in range(2):
+            nc.scalar.activation(out=s_g[t], in_=a_g[t][:], func=ACT.Silu)
+        for c in range(2):
             w2_piece(c)
-        z_g = keep.tile([P, S, PACK], BF16, name="z_g", tag="stage", align_bytes=64)
+        s_late = keep.tile([P, 2, V], F32, name="s_late", tag="stage", align_bytes=64)
+        for t in range(2, PACK):
+            s_g.append(s_late[:, t - 2, :])
+            nc.scalar.activation(out=s_g[t], in_=a_g[t][:], func=ACT.Silu)
+        for c in range(2, 4):
+            w2_piece(c)
+        z_g = keep.tile([P, S, PACK], BF16, name="z_g", tag="stage2", align_bytes=64)
         for t in range(PACK):
             if t + 1 < PACK:
                 b_g.append(gather_b(t + 1))
-            nc.vector.tensor_tensor(hw[t][:].indirect(lb_t[:]), b_g[t][:], s_g[t][:], ALU.add)
+            nc.vector.tensor_tensor(hw[t][:].indirect(lb_t[:]), b_g[t][:], s_g[t], ALU.add)
             for lo, hi in CHUNKS if t == PACK - 1 else ((0, S),):
                 plane(t, lo, hi)
         nc.vector.quantize_mx(out=w2_codes[:].bitcast(FP8X4), scales=w2_scales[:], in_=w2_g[:].rearrange("p n j -> p (n j)"))

@@ -32,8 +32,8 @@ def tile_picked_revcoup_none_p_kernel(tc, x_words, x_scales, w1, gn, w2, offs, l
         offs_t = keep.tile([P, S // 16], U16, name="offs_t")
         la_t = keep.tile([P, V // 16], U16, name="la_t")
         lb_t = keep.tile([P, V // 16], U16, name="lb_t")
-        xw = keep.tile([P, T], U32, name="xw", align_bytes=64)
-        xs = keep.tile([P, T], U8, name="xs", tag="stage", align_bytes=64)
+        xw = keep.tile([P, T], U32, name="xw", tag="xw", align_bytes=64)
+        xs = keep.tile([P, T], U8, name="xs", align_bytes=64)
         w1_raw = [keep.tile([P, 2, H], F32, name=f"w1_raw{u}", tag=f"w1_raw{u}", align_bytes=64) for u in range(2)]
         banks = [psum.tile([P, 512], F32, name=f"bank{b}") for b in range(8)]
 
@@ -42,37 +42,42 @@ def tile_picked_revcoup_none_p_kernel(tc, x_words, x_scales, w1, gn, w2, offs, l
         nc.gpsimd.memset(warm[:, 0:1], 0.0)
         nc.scalar.activation(out=warm[:, 1:2], in_=warm[:, 0:1], func=ACT.Silu)
         w1_rows = w1.rearrange("(p j) c -> p j c", j=PACK)
-        nc.sync.dma_start(out=w1_raw[0][:], in_=w1_rows[:, 0:2, :])
+        x_rows = x_words[0].rearrange("p n t -> p (n t)").bitcast(I32)
+        nc.sync.dma_start(out=xw[:, 0 : T // 2].bitcast(I32), in_=x_rows[:, 0 : T // 2])
         nc.sync.dma_start(out=xs[0:P:8, :].bitcast(I32), in_=x_scales[0].bitcast(I32))
         nc.sync.dma_start(offs_t[:], offs)
-        nc.sync.dma_start(out=xw[:].bitcast(I32), in_=x_words[0].rearrange("p n t -> p (n t)").bitcast(I32))
-        nc.sync.dma_start(out=w1_raw[1][:], in_=w1_rows[:, 2:4, :])
+        nc.sync.dma_start(out=xw[:, T // 2 : T].bitcast(I32), in_=x_rows[:, T // 2 : T])
+        for u in range(2):
+            nc.sync.dma_start(out=w1_raw[u][:], in_=w1_rows[:, 2 * u : 2 * u + 2, :])
         nc.sync.dma_start(la_t[:], la)
         nc.sync.dma_start(lb_t[:], lb)
 
-        xs_p = keep.tile([P, S], U8, name="xs_p", tag="stage2", align_bytes=64)
+        xs_p = keep.tile([P, S], U8, name="xs_p", tag="stage", align_bytes=64)
         nc.vector.tensor_copy(xs_p[:], xs[:].indirect(offs_t[:]))
         xs_g = keep.tile([P, S], U8, name="xs_g", align_bytes=64)
         nc.gpsimd.memset(xs_g[:].bitcast(I32), 0)
         for r in range(4):
-            nc.sync.dma_start(out=xs_g[r:P:32, :].bitcast(I32), in_=xs_p[8 * r : P : 32, :].bitcast(I32))
-        w2_rows = w2.rearrange("(p j) c -> p j c", j=PACK)
-        w2_raw = [keep.tile([P, PACK, N // 2], F32, name=f"w2_raw{u}", tag=("stage", "stage2")[u], align_bytes=64) for u in range(2)]
-        for u in range(2):
-            nc.sync.dma_start(out=w2_raw[u][:], in_=w2_rows[:, :, u * (N // 2) : (u + 1) * (N // 2)])
+            nc.scalar.dma_start(out=xs_g[r:P:32, :].bitcast(I32), in_=xs_p[8 * r : P : 32, :].bitcast(I32))
 
         w1_g = [keep.tile([P, 2, P, PACK], BF16, name=f"w1_g{u}", align_bytes=64) for u in range(2)]
         xw_g = keep.tile([P, S], U32, name="xw_g", align_bytes=64)
         for u in range(2):
-            w1_by_t = w1_raw[u][:].rearrange("p j (m t) -> p m j t", t=PACK)
+            w1_by_t = w1_raw[u][:].rearrange("p j (b t i) -> p t b i j", t=PACK, i=8)
             slots = slice(2 * u, 2 * u + 2)
-            for lo, hi in ((0, 2),) if u == 0 else ((0, 1), (1, 2)):
-                nc.vector.tensor_copy(out=w1_g[0][:, lo:hi, :, slots].rearrange("p t m j -> p m j t"), in_=w1_by_t[:, :, :, lo:hi])
-            nc.scalar.copy(out=w1_g[1][:, :, :, slots].rearrange("p t m j -> p m j t"), in_=w1_by_t[:, :, :, 2:4])
             if u == 0:
                 nc.vector.tensor_copy(xw_g[:], xw[:].indirect(offs_t[:]))
-        gn_t = keep.tile([P, PACK], F32, name="gn_t", tag="w1_raw0", align_bytes=64)
-        nc.sync.dma_start(out=gn_t[:], in_=gn.rearrange("(p t) o -> p (t o)", t=PACK))
+            for lo, hi in ((0, 2),) if u == 0 else ((0, 1), (1, 2)):
+                nc.vector.tensor_copy(out=w1_g[0][:, lo:hi, :, slots].rearrange("p t (b i) j -> p t b i j", i=8), in_=w1_by_t[:, lo:hi])
+            nc.scalar.copy(out=w1_g[1][:, :, :, slots].rearrange("p t (b i) j -> p t b i j", i=8), in_=w1_by_t[:, 2:4])
+        w2_rows = w2.rearrange("(b j i) c -> j b i c", j=PACK, i=8)
+        w2_raw = [keep.tile([P, PACK, N // 2], F32, name=f"w2_raw{u}", tag=("stage", "w1_raw1")[u], align_bytes=64) for u in range(2)]
+        for u in range(2):
+            for j in range(PACK):
+                nc.sync.dma_start(out=w2_raw[u][:, j, :], in_=w2_rows[j][:, :, u * (N // 2) : (u + 1) * (N // 2)])
+        gn_t = keep.tile([P, PACK, 8], F32, name="gn_t", tag="xw", align_bytes=64)
+        with nc.allow_non_contiguous_dma(reason="one gain a partition and plane"):
+            for t in range(PACK):
+                nc.sync.dma_start(out=gn_t[:, t, 0:1], in_=gn.rearrange("(b t i) o -> t b i o", t=PACK, i=8)[t])
         w1_codes = [keep.tile([P, P], U32, name=f"w1_codes{t}", align_bytes=64) for t in range(PACK)]
         w1_scales = [keep.tile([P, P], U8, name=f"w1_scales{t}", align_bytes=64) for t in range(PACK)]
         for t in ORDER:
@@ -105,7 +110,7 @@ def tile_picked_revcoup_none_p_kernel(tc, x_words, x_scales, w1, gn, w2, offs, l
 
         def plane(t, lo, hi):
             src = hw[t][:, lo:hi]
-            nc.scalar.activation(out=z_g[:, lo:hi, t], in_=src, func=ACT.Copy, scale=gn_t[:, t : t + 1])
+            nc.scalar.activation(out=z_g[:, lo:hi, t], in_=src, func=ACT.Copy, scale=gn_t[:, t, 0:1])
 
         def w2_piece(c):
             cols = slice(c * P, (c + 1) * P)
@@ -127,7 +132,7 @@ def tile_picked_revcoup_none_p_kernel(tc, x_words, x_scales, w1, gn, w2, offs, l
             nc.scalar.activation(out=s_g[t], in_=a_g[t][:], func=ACT.Silu)
         for c in range(2, 4):
             w2_piece(c)
-        z_g = keep.tile([P, S, PACK], BF16, name="z_g", tag="stage2", align_bytes=64)
+        z_g = keep.tile([P, S, PACK], BF16, name="z_g", tag="w1_raw1", align_bytes=64)
         for t in range(PACK):
             if t + 1 < PACK:
                 b_g.append(gather_b(t + 1))
@@ -137,24 +142,25 @@ def tile_picked_revcoup_none_p_kernel(tc, x_words, x_scales, w1, gn, w2, offs, l
         nc.vector.quantize_mx(out=w2_codes[:].bitcast(FP8X4), scales=w2_scales[:], in_=w2_g[:].rearrange("p n j -> p (n j)"))
 
         n = 0
-        for lo, hi in CHUNKS:
+        for (lo, hi), groups in zip(CHUNKS, (((1, True), (1, True), (2, False)), ((2, True), (2, False)), ((1, True), (1, False), (1, True), (1, False)))):
             cols = slice(lo, hi)
             width = hi - lo
-            per_bank = HALF // width
             z_codes = ring.tile([P, width], U32, name="z_codes", align_bytes=64)
             z_scales = ring.tile([P, width], U8, name="z_scales", align_bytes=64)
             nc.vector.quantize_mx(out=z_codes[:].bitcast(FP8X4), scales=z_scales[:], in_=z_g[:, lo:hi, :].rearrange("p n j -> p (n j)"))
-            for m0 in range(0, 4, per_bank):
-                bank = banks[n]
-                for i in range(per_bank):
+            m0 = 0
+            for count, on_vector in groups:
+                bank = banks[n % 8]
+                for i in range(count):
                     rows = slice((m0 + i) * P, (m0 + i + 1) * P)
                     nc.tensor.matmul_mx(out=bank[:, i * width : (i + 1) * width], lhsT=w2_codes[:, rows].bitcast(FP8X4), lhsT_scale=w2_scales[:, rows],
                                         rhs=z_codes[:].bitcast(FP8X4), rhs_scale=z_scales[:], start=True, stop=True)
-                res = keep.tile([P, HALF], F32, name=f"res{n}", align_bytes=64)
-                if n % 2 == 0:
-                    nc.vector.tensor_copy(out=res[:], in_=bank[:, 0:HALF])
+                res = keep.tile([P, count * width], F32, name=f"res{n}", align_bytes=64)
+                if on_vector:
+                    nc.vector.tensor_copy(out=res[:], in_=bank[:, 0 : count * width])
                 else:
-                    nc.scalar.copy(out=res[:], in_=bank[:, 0:HALF])
-                nc.sync.dma_start(out=out[m0 * P : (m0 + per_bank) * P, cols].rearrange("(i p) c -> p i c", p=P),
-                                  in_=res[:].rearrange("p (i c) -> p i c", i=per_bank))
+                    nc.scalar.copy(out=res[:], in_=bank[:, 0 : count * width])
+                nc.sync.dma_start(out=out[m0 * P : (m0 + count) * P, cols].rearrange("(i p) c -> p i c", p=P),
+                                  in_=res[:].rearrange("p (i c) -> p i c", i=count))
+                m0 = m0 + count
                 n = n + 1

@@ -33,7 +33,7 @@ def tile_picked_revcoup_none_p_kernel(tc, x_words, x_scales, w1, gn, w2, offs, l
         la_t = keep.tile([P, V // 16], U16, name="la_t")
         lb_t = keep.tile([P, V // 16], U16, name="lb_t")
         xw = keep.tile([P, T], U32, name="xw", tag="xw", align_bytes=64)
-        xs = keep.tile([P, T], U8, name="xs", align_bytes=64)
+        xs = keep.tile([P, T], U8, name="xs", tag="stage", align_bytes=64)
         w1_raw = [keep.tile([P, 2, H], F32, name=f"w1_raw{u}", tag=f"w1_raw{u}", align_bytes=64) for u in range(2)]
         banks = [psum.tile([P, 512], F32, name=f"bank{b}") for b in range(8)]
 
@@ -52,12 +52,12 @@ def tile_picked_revcoup_none_p_kernel(tc, x_words, x_scales, w1, gn, w2, offs, l
         nc.sync.dma_start(la_t[:], la)
         nc.sync.dma_start(lb_t[:], lb)
 
-        xs_p = keep.tile([P, S], U8, name="xs_p", tag="stage", align_bytes=64)
+        xs_p = keep.tile([P, S], U8, name="xs_p", align_bytes=64)
         nc.vector.tensor_copy(xs_p[:], xs[:].indirect(offs_t[:]))
         xs_g = keep.tile([P, S], U8, name="xs_g", align_bytes=64)
         nc.gpsimd.memset(xs_g[:].bitcast(I32), 0)
         for r in range(4):
-            nc.scalar.dma_start(out=xs_g[r:P:32, :].bitcast(I32), in_=xs_p[8 * r : P : 32, :].bitcast(I32))
+            nc.sync.dma_start(out=xs_g[r:P:32, :].bitcast(I32), in_=xs_p[8 * r : P : 32, :].bitcast(I32))
 
         w1_g = [keep.tile([P, 2, P, PACK], BF16, name=f"w1_g{u}", align_bytes=64) for u in range(2)]
         xw_g = keep.tile([P, S], U32, name="xw_g", align_bytes=64)
@@ -70,11 +70,10 @@ def tile_picked_revcoup_none_p_kernel(tc, x_words, x_scales, w1, gn, w2, offs, l
                 nc.vector.tensor_copy(out=w1_g[0][:, lo:hi, :, slots].rearrange("p t (b i) j -> p t b i j", i=8), in_=w1_by_t[:, lo:hi])
             nc.scalar.copy(out=w1_g[1][:, :, :, slots].rearrange("p t (b i) j -> p t b i j", i=8), in_=w1_by_t[:, 2:4])
         w2_rows = w2.rearrange("(b j i) c -> j b i c", j=PACK, i=8)
-        w2_raw = [keep.tile([P, PACK, N // 2], F32, name=f"w2_raw{u}", tag=("stage", "w1_raw1")[u], align_bytes=64) for u in range(2)]
-        for u in range(2):
-            for j in range(PACK):
-                nc.sync.dma_start(out=w2_raw[u][:, j, :], in_=w2_rows[j][:, :, u * (N // 2) : (u + 1) * (N // 2)])
-        gn_t = keep.tile([P, PACK, 8], F32, name="gn_t", tag="xw", align_bytes=64)
+        w2_raw = keep.tile([P, PACK, N], F32, name="w2_raw", tag="stage", align_bytes=64)
+        for j in range(PACK):
+            nc.sync.dma_start(out=w2_raw[:, j, :], in_=w2_rows[j])
+        gn_t = keep.tile([P, PACK, 8], F32, name="gn_t", tag="w1_raw1", align_bytes=64)
         with nc.allow_non_contiguous_dma(reason="one gain a partition and plane"):
             for t in range(PACK):
                 nc.sync.dma_start(out=gn_t[:, t, 0:1], in_=gn.rearrange("(b t i) o -> t b i o", t=PACK, i=8)[t])
@@ -89,24 +88,37 @@ def tile_picked_revcoup_none_p_kernel(tc, x_words, x_scales, w1, gn, w2, offs, l
                                 rhs=xw_g[:, cols].bitcast(FP8X4), rhs_scale=xs_g[:, cols], start=True, stop=True)
 
         hw = [keep.tile([P, S], F32, name=f"h{t}", align_bytes=64) for t in range(PACK)]
-        for n, (t, cols) in enumerate(((0, slice(0, P)), (0, slice(P, 2 * P)), (0, slice(2 * P, 3 * P)), (0, slice(3 * P, S)), (1, slice(0, S)), (2, slice(0, S)), (3, slice(0, S)))):
-            width = cols.stop - cols.start
-            product1(t, banks[n][:, 0:width], cols)
-            if n in (0, 2):
-                nc.vector.tensor_copy(out=hw[t][:, cols], in_=banks[n][:, 0:width])
+        for n in range(4):
+            cols = slice(n * P, (n + 1) * P)
+            product1(0, banks[n][:, 0:P], cols)
+            if n % 2 == 0:
+                nc.vector.tensor_copy(out=hw[0][:, cols], in_=banks[n][:, 0:P])
             else:
-                nc.scalar.copy(out=hw[t][:, cols], in_=banks[n][:, 0:width])
+                nc.scalar.copy(out=hw[0][:, cols], in_=banks[n][:, 0:P])
+        for t in range(1, PACK):
+            product1(t, banks[3 + t][:], slice(0, S))
 
-        a_g = [keep.tile([P, V], F32, name=f"a_g{t}", tag=f"looked{t + 1}", align_bytes=64) for t in range(PACK)]
-        s_g = [keep.tile([P, V], F32, name=f"s_g{t}", align_bytes=64)[:] for t in range(2)]
         w2_g = keep.tile([P, N, PACK], BF16, name="w2_g", align_bytes=64)
-        w2_codes = keep.tile([P, N], U32, name="w2_codes", align_bytes=64)
         w2_scales = keep.tile([P, N], U8, name="w2_scales", align_bytes=64)
+        a_g, b_g, s_g = {}, {}, {}
 
-        def gather_b(t):
-            b = keep.tile([P, V], F32, name=f"b_g{t}", tag=f"looked{t}", align_bytes=64)
-            nc.vector.tensor_copy(b[:], hw[t][:].indirect(lb_t[:]))
-            return b
+        def y_out(t):
+            nc.scalar.copy(out=hw[t][:], in_=banks[3 + t][:])
+
+        def gather_a(t):
+            a_g[t] = keep.tile([P, V], F32, name=f"a_g{t}", tag=f"a_g{t}", align_bytes=64)
+            nc.vector.tensor_copy(a_g[t][:], hw[t][:].indirect(la_t[:]))
+
+        def gather_b(t, tag):
+            b_g[t] = keep.tile([P, V], F32, name=f"b_g{t}", tag=tag, align_bytes=64)
+            nc.vector.tensor_copy(b_g[t][:], hw[t][:].indirect(lb_t[:]))
+
+        def silu(t, dst):
+            s_g[t] = dst
+            nc.scalar.activation(out=dst, in_=a_g[t][:], func=ACT.Silu)
+
+        def scatter(t):
+            nc.vector.tensor_tensor(hw[t][:].indirect(lb_t[:]), b_g[t][:], s_g[t], ALU.add)
 
         def plane(t, lo, hi):
             src = hw[t][:, lo:hi]
@@ -115,30 +127,38 @@ def tile_picked_revcoup_none_p_kernel(tc, x_words, x_scales, w1, gn, w2, offs, l
         def w2_piece(c):
             cols = slice(c * P, (c + 1) * P)
             nc.scalar.copy(out=w2_g[:, cols, :].rearrange("p (b i) j -> p b j i", i=4),
-                           in_=w2_raw[c // 2][:, :, (c % 2) * P : (c % 2 + 1) * P].rearrange("p j (b i) -> p b j i", i=4))
+                           in_=w2_raw[:, :, cols].rearrange("p j (b i) -> p b j i", i=4))
 
-        b_g = []
-        for t in range(PACK):
-            nc.vector.tensor_copy(a_g[t][:], hw[t][:].indirect(la_t[:]))
-            if t == 0:
-                b_g.append(gather_b(0))
-        for t in range(2):
-            nc.scalar.activation(out=s_g[t], in_=a_g[t][:], func=ACT.Silu)
-        for c in range(2):
+        s_early = keep.tile([P, 2, V], F32, name="s_early", align_bytes=64)
+        gather_a(0)
+        gather_b(0, "b_g0")
+        y_out(1)
+        silu(0, s_early[:, 0, :])
+        gather_a(1)
+        gather_b(1, "b_g1")
+        y_out(2)
+        scatter(0)
+        y_out(3)
+        silu(1, s_early[:, 1, :])
+        gather_a(2)
+        gather_b(2, "b_g2")
+        gather_a(3)
+        scatter(1)
+        gather_b(3, "a_g1")
+        for c in range(4):
             w2_piece(c)
-        s_late = keep.tile([P, 2, V], F32, name="s_late", tag="stage", align_bytes=64)
+        late = keep.tile([P, S * PACK + 4 * V], BF16, name="late", tag="stage", align_bytes=64)
+        z_g = late[:, 0 : S * PACK].rearrange("p (n j) -> p n j", j=PACK)
         for t in range(2, PACK):
-            s_g.append(s_late[:, t - 2, :])
-            nc.scalar.activation(out=s_g[t], in_=a_g[t][:], func=ACT.Silu)
-        for c in range(2, 4):
-            w2_piece(c)
-        z_g = keep.tile([P, S, PACK], BF16, name="z_g", tag="w1_raw1", align_bytes=64)
-        for t in range(PACK):
-            if t + 1 < PACK:
-                b_g.append(gather_b(t + 1))
-            nc.vector.tensor_tensor(hw[t][:].indirect(lb_t[:]), b_g[t][:], s_g[t], ALU.add)
-            for lo, hi in CHUNKS if t == PACK - 1 else ((0, S),):
-                plane(t, lo, hi)
+            silu(t, late[:, S * PACK + 2 * V * (t - 2) : S * PACK + 2 * V * (t - 1)].bitcast(F32))
+        for t in range(2):
+            plane(t, 0, S)
+        scatter(2)
+        plane(2, 0, S)
+        scatter(3)
+        for lo, hi in CHUNKS:
+            plane(3, lo, hi)
+        w2_codes = keep.tile([P, N], U32, name="w2_codes", tag="a_g3", align_bytes=64)
         nc.vector.quantize_mx(out=w2_codes[:].bitcast(FP8X4), scales=w2_scales[:], in_=w2_g[:].rearrange("p n j -> p (n j)"))
 
         n = 0

@@ -69,6 +69,9 @@ def tile_picked_revcoup_none_p_kernel(tc, x_words, x_scales, w1, gn, w2, offs, l
             for lo, hi in ((0, 2),) if u == 0 else ((0, 1), (1, 2)):
                 nc.vector.tensor_copy(out=w1_g[0][:, lo:hi, :, slots].rearrange("p t (b i) j -> p t b i j", i=8), in_=w1_by_t[:, lo:hi])
             nc.scalar.copy(out=w1_g[1][:, :, :, slots].rearrange("p t (b i) j -> p t b i j", i=8), in_=w1_by_t[:, 2:4])
+        for n in range(2):
+            nc.tensor.matmul_mx(out=banks[7][:], lhsT=xw_g[:, 0:P].bitcast(FP8X4), lhsT_scale=xs_p[:, 0:P],
+                                rhs=xw_g[:].bitcast(FP8X4), rhs_scale=xs_p[:], start=True, stop=True)
         w2_rows = w2.rearrange("(b j i) c -> j b i c", j=PACK, i=8)
         w2_raw = keep.tile([P, PACK, N], F32, name="w2_raw", tag="stage", align_bytes=64)
         for j in range(PACK):

@@ -20,6 +20,7 @@ PACK = 4
 HALF = S // 2
 ORDER = (0, 1, 2, 3)
 CHUNKS = ((0, 128), (128, 256), (256, 512))
+SLOT = (2, 0, 1, 3)
 
 
 def tile_picked_revcoup_none_p_kernel(tc, x_words, x_scales, w1, gn, w2, offs, la, lb, out):
@@ -74,8 +75,8 @@ def tile_picked_revcoup_none_p_kernel(tc, x_words, x_scales, w1, gn, w2, offs, l
                                 rhs=xw_g[:].bitcast(FP8X4), rhs_scale=xs_p[:], start=True, stop=True)
         w2_rows = w2.rearrange("(b j i) c -> j b i c", j=PACK, i=8)
         w2_raw = keep.tile([P, PACK, N], F32, name="w2_raw", tag="stage", align_bytes=64)
-        for j in range(PACK):
-            nc.sync.dma_start(out=w2_raw[:, j, :], in_=w2_rows[j])
+        for t in range(PACK):
+            nc.sync.dma_start(out=w2_raw[:, SLOT[t], :], in_=w2_rows[t])
         gn_t = keep.tile([P, PACK, 8], F32, name="gn_t", tag="w1_raw1", align_bytes=64)
         with nc.allow_non_contiguous_dma(reason="one gain a partition and plane"):
             for t in range(PACK):
@@ -90,7 +91,7 @@ def tile_picked_revcoup_none_p_kernel(tc, x_words, x_scales, w1, gn, w2, offs, l
             nc.tensor.matmul_mx(out=bank, lhsT=w1_codes[t][:].bitcast(FP8X4), lhsT_scale=w1_scales[t][:],
                                 rhs=xw_g[:, cols].bitcast(FP8X4), rhs_scale=xs_g[:, cols], start=True, stop=True)
 
-        hw = [keep.tile([P, S], F32, name=f"h{t}", align_bytes=64) for t in range(PACK)]
+        hw = [keep.tile([P, S], F32, name=f"h{t}", tag=f"h{t}", align_bytes=64) for t in range(PACK)]
         for n in range(4):
             cols = slice(n * P, (n + 1) * P)
             product1(0, banks[n][:, 0:P], cols)
@@ -125,7 +126,7 @@ def tile_picked_revcoup_none_p_kernel(tc, x_words, x_scales, w1, gn, w2, offs, l
 
         def plane(t, lo, hi):
             src = hw[t][:, lo:hi]
-            nc.scalar.activation(out=z_g[:, lo:hi, t], in_=src, func=ACT.Copy, scale=gn_t[:, t, 0:1])
+            nc.scalar.activation(out=z_g[:, lo:hi, SLOT[t]], in_=src, func=ACT.Copy, scale=gn_t[:, t, 0:1])
 
         def w2_piece(c):
             cols = slice(c * P, (c + 1) * P)
@@ -152,17 +153,32 @@ def tile_picked_revcoup_none_p_kernel(tc, x_words, x_scales, w1, gn, w2, offs, l
             w2_piece(c)
         late = keep.tile([P, S * PACK + 4 * V], BF16, name="late", tag="stage", align_bytes=64)
         z_g = late[:, 0 : S * PACK].rearrange("p (n j) -> p n j", j=PACK)
-        for t in range(2, PACK):
+
+        def late_silu(t):
             silu(t, late[:, S * PACK + 2 * V * (t - 2) : S * PACK + 2 * V * (t - 1)].bitcast(F32))
-        for t in range(2):
-            plane(t, 0, S)
+
+        def plane_on_vector(lo, hi):
+            nc.vector.tensor_scalar(out=z_g[:, lo:hi, SLOT[3]], in0=hw[3][:, lo:hi], scalar1=gn_t[:, 3, 0:1], scalar2=None, op0=ALU.mult)
+
+        def w2_quantize(dst, lo, hi):
+            nc.vector.quantize_mx(out=dst.bitcast(FP8X4), scales=w2_scales[:, lo:hi], in_=w2_g[:, lo:hi, :].rearrange("p n j -> p (n j)"))
+
+        late_silu(2)
+        plane(0, 0, S)
+        late_silu(3)
+        plane(1, 0, S)
         scatter(2)
-        plane(2, 0, S)
+        plane(2, 0, S - 32)
         scatter(3)
-        for lo, hi in CHUNKS:
-            plane(3, lo, hi)
-        w2_codes = keep.tile([P, N], U32, name="w2_codes", tag="a_g3", align_bytes=64)
-        nc.vector.quantize_mx(out=w2_codes[:].bitcast(FP8X4), scales=w2_scales[:], in_=w2_g[:].rearrange("p n j -> p (n j)"))
+        plane_on_vector(0, 64)
+        plane(3, 64, P)
+        plane(2, S - 32, S)
+        plane(3, P, 2 * P)
+        plane(3, 2 * P, S - 64)
+        w2_first = keep.tile([P, P], U32, name="w2_first", tag="a_g3", align_bytes=64)
+        w2_quantize(w2_first[:], 0, P)
+        plane_on_vector(S - 64, S)
+        w2_codes = [w2_first[:]]
 
         n = 0
         for (lo, hi), groups in zip(CHUNKS, (((1, True), (1, True), (2, False)), ((2, True), (2, False)), ((1, True), (1, False), (1, True), (1, False)))):
@@ -171,12 +187,17 @@ def tile_picked_revcoup_none_p_kernel(tc, x_words, x_scales, w1, gn, w2, offs, l
             z_codes = ring.tile([P, width], U32, name="z_codes", align_bytes=64)
             z_scales = ring.tile([P, width], U8, name="z_scales", align_bytes=64)
             nc.vector.quantize_mx(out=z_codes[:].bitcast(FP8X4), scales=z_scales[:], in_=z_g[:, lo:hi, :].rearrange("p n j -> p (n j)"))
+            if lo == 0:
+                w2_rest = keep.tile([P, 3 * P], U32, name="w2_rest", tag="h2", align_bytes=64)
+                w2_quantize(w2_rest[:, 0:P], P, 2 * P)
+                w2_quantize(w2_rest[:, P : 3 * P], 2 * P, N)
+                w2_codes.extend(w2_rest[:, m * P : (m + 1) * P] for m in range(3))
             m0 = 0
             for count, on_vector in groups:
                 bank = banks[n % 8]
                 for i in range(count):
                     rows = slice((m0 + i) * P, (m0 + i + 1) * P)
-                    nc.tensor.matmul_mx(out=bank[:, i * width : (i + 1) * width], lhsT=w2_codes[:, rows].bitcast(FP8X4), lhsT_scale=w2_scales[:, rows],
+                    nc.tensor.matmul_mx(out=bank[:, i * width : (i + 1) * width], lhsT=w2_codes[m0 + i].bitcast(FP8X4), lhsT_scale=w2_scales[:, rows],
                                         rhs=z_codes[:].bitcast(FP8X4), rhs_scale=z_scales[:], start=True, stop=True)
                 res = keep.tile([P, count * width], F32, name=f"res{n}", align_bytes=64)
                 if on_vector:

@@ -174,11 +174,10 @@ def tile_picked_revcoup_none_p_kernel(tc, x_words, x_scales, w1, gn, w2, offs, l
         plane(3, 64, P)
         plane(2, S - 32, S)
         plane(3, P, 2 * P)
-        plane(3, 2 * P, S - 64)
-        w2_first = keep.tile([P, P], U32, name="w2_first", tag="a_g3", align_bytes=64)
-        w2_quantize(w2_first[:], 0, P)
-        plane_on_vector(S - 64, S)
-        w2_codes = [w2_first[:]]
+        plane(3, 2 * P, S)
+        w2_first = keep.tile([P, 2 * P], U32, name="w2_first", tag="a_g3", align_bytes=64)
+        w2_quantize(w2_first[:], 0, 2 * P)
+        w2_codes = [w2_first[:, m * P : (m + 1) * P] for m in range(2)]
 
         n = 0
         for (lo, hi), groups in zip(CHUNKS, (((1, True), (1, True), (2, False)), ((2, True), (2, False)), ((1, True), (1, False), (1, True), (1, False)))):
@@ -188,10 +187,9 @@ def tile_picked_revcoup_none_p_kernel(tc, x_words, x_scales, w1, gn, w2, offs, l
             z_scales = ring.tile([P, width], U8, name="z_scales", align_bytes=64)
             nc.vector.quantize_mx(out=z_codes[:].bitcast(FP8X4), scales=z_scales[:], in_=z_g[:, lo:hi, :].rearrange("p n j -> p (n j)"))
             if lo == 0:
-                w2_rest = keep.tile([P, 3 * P], U32, name="w2_rest", tag="h2", align_bytes=64)
-                w2_quantize(w2_rest[:, 0:P], P, 2 * P)
-                w2_quantize(w2_rest[:, P : 3 * P], 2 * P, N)
-                w2_codes.extend(w2_rest[:, m * P : (m + 1) * P] for m in range(3))
+                w2_rest = keep.tile([P, 2 * P], U32, name="w2_rest", tag="h2", align_bytes=64)
+                w2_quantize(w2_rest[:], 2 * P, N)
+                w2_codes.extend(w2_rest[:, m * P : (m + 1) * P] for m in range(2))
             m0 = 0
             for count, on_vector in groups:
                 bank = banks[n % 8]

@@ -17,192 +17,205 @@ ALU = mybir.AluOpType
 
 P = 128
 PACK = 4
-HALF = S // 2
-ORDER = (0, 1, 2, 3)
-CHUNKS = ((0, 128), (128, 256), (256, 512))
+LINE = 8
+LAST = PACK - 1
 SLOT = (2, 0, 1, 3)
+RANGES = ((0, 128), (128, 256), (256, 512))
+STORES = (((1, True), (1, True), (2, False)), ((2, True), (2, False)), ((1, True), (1, False), (1, True), (1, False)))
+SHARE = 64
+HELD = 32
 
 
 def tile_picked_revcoup_none_p_kernel(tc, x_words, x_scales, w1, gn, w2, offs, la, lb, out):
     nc = tc.nc
     with ExitStack() as ctx:
         keep = ctx.enter_context(tc.tile_pool(name="keep", bufs=1))
-        ring = ctx.enter_context(tc.tile_pool(name="ring", bufs=2))
         psum = ctx.enter_context(tc.psum_pool(name="psum", bufs=1))
 
         offs_t = keep.tile([P, S // 16], U16, name="offs_t")
         la_t = keep.tile([P, V // 16], U16, name="la_t")
         lb_t = keep.tile([P, V // 16], U16, name="lb_t")
-        xw = keep.tile([P, T], U32, name="xw", tag="xw", align_bytes=64)
-        xs = keep.tile([P, T], U8, name="xs", tag="stage", align_bytes=64)
+        x_all = keep.tile([P, T], U32, name="x_all", align_bytes=64)
+        xs_all = keep.tile([P, T], U8, name="xs_all", tag="stage", align_bytes=64)
         w1_raw = [keep.tile([P, 2, H], F32, name=f"w1_raw{u}", tag=f"w1_raw{u}", align_bytes=64) for u in range(2)]
         banks = [psum.tile([P, 512], F32, name=f"bank{b}") for b in range(8)]
 
-        nc.vector.memset(xs[:].bitcast(I32), 0)
+        nc.vector.memset(xs_all[:].bitcast(I32), 0)
         warm = keep.tile([P, 2], F32, name="warm")
-        nc.gpsimd.memset(warm[:, 0:1], 0.0)
+        nc.vector.memset(warm[:, 0:1], 0.0)
         nc.scalar.activation(out=warm[:, 1:2], in_=warm[:, 0:1], func=ACT.Silu)
         w1_rows = w1.rearrange("(p j) c -> p j c", j=PACK)
         x_rows = x_words[0].rearrange("p n t -> p (n t)").bitcast(I32)
-        nc.sync.dma_start(out=xw[:, 0 : T // 2].bitcast(I32), in_=x_rows[:, 0 : T // 2])
-        nc.sync.dma_start(out=xs[0:P:8, :].bitcast(I32), in_=x_scales[0].bitcast(I32))
+        nc.sync.dma_start(out=x_all[:, 0 : T // 2].bitcast(I32), in_=x_rows[:, 0 : T // 2])
+        nc.sync.dma_start(out=xs_all[0:P:LINE, :].bitcast(I32), in_=x_scales[0].bitcast(I32))
         nc.sync.dma_start(offs_t[:], offs)
-        nc.sync.dma_start(out=xw[:, T // 2 : T].bitcast(I32), in_=x_rows[:, T // 2 : T])
+        nc.sync.dma_start(out=x_all[:, T // 2 : T].bitcast(I32), in_=x_rows[:, T // 2 : T])
         for u in range(2):
             nc.sync.dma_start(out=w1_raw[u][:], in_=w1_rows[:, 2 * u : 2 * u + 2, :])
         nc.sync.dma_start(la_t[:], la)
         nc.sync.dma_start(lb_t[:], lb)
 
-        xs_p = keep.tile([P, S], U8, name="xs_p", align_bytes=64)
-        nc.vector.tensor_copy(xs_p[:], xs[:].indirect(offs_t[:]))
-        xs_g = keep.tile([P, S], U8, name="xs_g", align_bytes=64)
-        nc.gpsimd.memset(xs_g[:].bitcast(I32), 0)
+        xs_picked = keep.tile([P, S], U8, name="xs_picked", align_bytes=64)
+        nc.vector.tensor_copy(xs_picked[:], xs_all[:].indirect(offs_t[:]))
+        x_scale = keep.tile([P, S], U8, name="x_scale", align_bytes=64)
+        nc.gpsimd.memset(x_scale[:].bitcast(I32), 0)
         for r in range(4):
-            nc.sync.dma_start(out=xs_g[r:P:32, :].bitcast(I32), in_=xs_p[8 * r : P : 32, :].bitcast(I32))
+            nc.sync.dma_start(out=x_scale[r:P:32, :].bitcast(I32), in_=xs_picked[LINE * r : P : 32, :].bitcast(I32))
 
-        w1_g = [keep.tile([P, 2, P, PACK], BF16, name=f"w1_g{u}", align_bytes=64) for u in range(2)]
-        xw_g = keep.tile([P, S], U32, name="xw_g", align_bytes=64)
-        for u in range(2):
-            w1_by_t = w1_raw[u][:].rearrange("p j (b t i) -> p t b i j", t=PACK, i=8)
-            slots = slice(2 * u, 2 * u + 2)
-            if u == 0:
-                nc.vector.tensor_copy(xw_g[:], xw[:].indirect(offs_t[:]))
-            for lo, hi in ((0, 2),) if u == 0 else ((0, 1), (1, 2)):
-                nc.vector.tensor_copy(out=w1_g[0][:, lo:hi, :, slots].rearrange("p t (b i) j -> p t b i j", i=8), in_=w1_by_t[:, lo:hi])
-            nc.scalar.copy(out=w1_g[1][:, :, :, slots].rearrange("p t (b i) j -> p t b i j", i=8), in_=w1_by_t[:, 2:4])
+        x_codes = keep.tile([P, S], U32, name="x_codes", align_bytes=64)
+        w1_bf = [keep.tile([P, 2, P, PACK], BF16, name=f"w1_bf{e}", align_bytes=64) for e in range(2)]
+        nc.vector.tensor_copy(x_codes[:], x_all[:].indirect(offs_t[:]))
+        for u, vector_planes in enumerate((((0, 2),), ((0, 1), (1, 2)))):
+            by_plane = w1_raw[u][:].rearrange("p j (b t i) -> p t b i j", t=PACK, i=LINE)
+            pair = slice(2 * u, 2 * u + 2)
+            for lo, hi in vector_planes:
+                nc.vector.tensor_copy(out=w1_bf[0][:, lo:hi, :, pair].rearrange("p t (b i) j -> p t b i j", i=LINE), in_=by_plane[:, lo:hi])
+            nc.scalar.copy(out=w1_bf[1][:, :, :, pair].rearrange("p t (b i) j -> p t b i j", i=LINE), in_=by_plane[:, 2:4])
+
         for n in range(2):
-            nc.tensor.matmul_mx(out=banks[7][:], lhsT=xw_g[:, 0:P].bitcast(FP8X4), lhsT_scale=xs_p[:, 0:P],
-                                rhs=xw_g[:].bitcast(FP8X4), rhs_scale=xs_p[:], start=True, stop=True)
-        w2_rows = w2.rearrange("(b j i) c -> j b i c", j=PACK, i=8)
+            nc.tensor.matmul_mx(out=banks[7][:], lhsT=x_codes[:, 0:P].bitcast(FP8X4), lhsT_scale=xs_picked[:, 0:P],
+                                rhs=x_codes[:].bitcast(FP8X4), rhs_scale=xs_picked[:], start=True, stop=True)
+
+        w2_rows = w2.rearrange("(b t i) c -> t b i c", t=PACK, i=LINE)
         w2_raw = keep.tile([P, PACK, N], F32, name="w2_raw", tag="stage", align_bytes=64)
         for t in range(PACK):
             nc.sync.dma_start(out=w2_raw[:, SLOT[t], :], in_=w2_rows[t])
         gn_t = keep.tile([P, PACK, 8], F32, name="gn_t", tag="w1_raw1", align_bytes=64)
         with nc.allow_non_contiguous_dma(reason="one gain a partition and plane"):
             for t in range(PACK):
-                nc.sync.dma_start(out=gn_t[:, t, 0:1], in_=gn.rearrange("(b t i) o -> t b i o", t=PACK, i=8)[t])
+                nc.sync.dma_start(out=gn_t[:, t, 0:1], in_=gn.rearrange("(b t i) o -> t b i o", t=PACK, i=LINE)[t])
+
         w1_codes = [keep.tile([P, P], U32, name=f"w1_codes{t}", align_bytes=64) for t in range(PACK)]
         w1_scales = [keep.tile([P, P], U8, name=f"w1_scales{t}", align_bytes=64) for t in range(PACK)]
-        for t in ORDER:
-            src = w1_g[t // 2][:, t % 2, :, :]
-            nc.vector.quantize_mx(out=w1_codes[t][:].bitcast(FP8X4), scales=w1_scales[t][:], in_=src.rearrange("p m j -> p (m j)"))
+        for t in range(PACK):
+            nc.vector.quantize_mx(out=w1_codes[t][:].bitcast(FP8X4), scales=w1_scales[t][:],
+                                  in_=w1_bf[t // 2][:, t % 2, :, :].rearrange("p m j -> p (m j)"))
 
-        def product1(t, bank, cols):
-            nc.tensor.matmul_mx(out=bank, lhsT=w1_codes[t][:].bitcast(FP8X4), lhsT_scale=w1_scales[t][:],
-                                rhs=xw_g[:, cols].bitcast(FP8X4), rhs_scale=xs_g[:, cols], start=True, stop=True)
+        def first_product(t, dst, cols):
+            nc.tensor.matmul_mx(out=dst, lhsT=w1_codes[t][:].bitcast(FP8X4), lhsT_scale=w1_scales[t][:],
+                                rhs=x_codes[:, cols].bitcast(FP8X4), rhs_scale=x_scale[:, cols], start=True, stop=True)
 
-        hw = [keep.tile([P, S], F32, name=f"h{t}", tag=f"h{t}", align_bytes=64) for t in range(PACK)]
+        h = [keep.tile([P, S], F32, name=f"h{t}", tag=f"h{t}", align_bytes=64) for t in range(PACK)]
         for n in range(4):
             cols = slice(n * P, (n + 1) * P)
-            product1(0, banks[n][:, 0:P], cols)
+            first_product(0, banks[n][:, 0:P], cols)
             if n % 2 == 0:
-                nc.vector.tensor_copy(out=hw[0][:, cols], in_=banks[n][:, 0:P])
+                nc.vector.tensor_copy(out=h[0][:, cols], in_=banks[n][:, 0:P])
             else:
-                nc.scalar.copy(out=hw[0][:, cols], in_=banks[n][:, 0:P])
+                nc.scalar.copy(out=h[0][:, cols], in_=banks[n][:, 0:P])
+        halves = (slice(0, S // 2), slice(S // 2, S))
+        pieces = {1: ((banks[4][:, 0 : S // 2], halves[0]), (banks[7][:, 0 : S // 2], halves[1])),
+                  2: ((banks[5][:], slice(0, S)),), 3: ((banks[6][:], slice(0, S)),)}
         for t in range(1, PACK):
-            product1(t, banks[3 + t][:], slice(0, S))
+            for dst, cols in pieces[t]:
+                first_product(t, dst, cols)
 
-        w2_g = keep.tile([P, N, PACK], BF16, name="w2_g", align_bytes=64)
+        w2_bf = keep.tile([P, N, PACK], BF16, name="w2_bf", align_bytes=64)
         w2_scales = keep.tile([P, N], U8, name="w2_scales", align_bytes=64)
-        a_g, b_g, s_g = {}, {}, {}
+        a, b, gated = {}, {}, {}
 
-        def y_out(t):
-            nc.scalar.copy(out=hw[t][:], in_=banks[3 + t][:])
+        def leave_psum(t):
+            for src, cols in pieces[t]:
+                nc.scalar.copy(out=h[t][:, cols], in_=src)
 
         def gather_a(t):
-            a_g[t] = keep.tile([P, V], F32, name=f"a_g{t}", tag=f"a_g{t}", align_bytes=64)
-            nc.vector.tensor_copy(a_g[t][:], hw[t][:].indirect(la_t[:]))
+            a[t] = keep.tile([P, V], F32, name=f"a{t}", tag=f"a{t}", align_bytes=64)
+            nc.vector.tensor_copy(a[t][:], h[t][:].indirect(la_t[:]))
 
         def gather_b(t, tag):
-            b_g[t] = keep.tile([P, V], F32, name=f"b_g{t}", tag=tag, align_bytes=64)
-            nc.vector.tensor_copy(b_g[t][:], hw[t][:].indirect(lb_t[:]))
+            b[t] = keep.tile([P, V], F32, name=f"b{t}", tag=tag, align_bytes=64)
+            nc.vector.tensor_copy(b[t][:], h[t][:].indirect(lb_t[:]))
 
         def silu(t, dst):
-            s_g[t] = dst
-            nc.scalar.activation(out=dst, in_=a_g[t][:], func=ACT.Silu)
+            gated[t] = dst
+            nc.scalar.activation(out=dst, in_=a[t][:], func=ACT.Silu)
 
         def scatter(t):
-            nc.vector.tensor_tensor(hw[t][:].indirect(lb_t[:]), b_g[t][:], s_g[t], ALU.add)
+            nc.vector.tensor_tensor(h[t][:].indirect(lb_t[:]), b[t][:], gated[t], ALU.add)
 
-        def plane(t, lo, hi):
-            src = hw[t][:, lo:hi]
-            nc.scalar.activation(out=z_g[:, lo:hi, SLOT[t]], in_=src, func=ACT.Copy, scale=gn_t[:, t, 0:1])
-
-        def w2_piece(c):
-            cols = slice(c * P, (c + 1) * P)
-            nc.scalar.copy(out=w2_g[:, cols, :].rearrange("p (b i) j -> p b j i", i=4),
-                           in_=w2_raw[:, :, cols].rearrange("p j (b i) -> p b j i", i=4))
-
-        s_early = keep.tile([P, 2, V], F32, name="s_early", align_bytes=64)
+        gated_early = keep.tile([P, 2, V], F32, name="gated_early", align_bytes=64)
         gather_a(0)
-        gather_b(0, "b_g0")
-        y_out(1)
-        silu(0, s_early[:, 0, :])
+        gather_b(0, "b0")
+        leave_psum(1)
+        silu(0, gated_early[:, 0, :])
         gather_a(1)
-        gather_b(1, "b_g1")
-        y_out(2)
+        gather_b(1, "b1")
+        leave_psum(2)
         scatter(0)
-        y_out(3)
-        silu(1, s_early[:, 1, :])
+        leave_psum(3)
+        silu(1, gated_early[:, 1, :])
         gather_a(2)
-        gather_b(2, "b_g2")
+        gather_b(2, "b2")
         gather_a(3)
         scatter(1)
-        gather_b(3, "a_g1")
-        for c in range(4):
-            w2_piece(c)
+        gather_b(3, "a1")
+
+        for c in range(N // P):
+            cols = slice(c * P, (c + 1) * P)
+            nc.scalar.copy(out=w2_bf[:, cols, :].rearrange("p (g i) j -> p g j i", i=4),
+                           in_=w2_raw[:, :, cols].rearrange("p j (g i) -> p g j i", i=4))
+
         late = keep.tile([P, S * PACK + 4 * V], BF16, name="late", tag="stage", align_bytes=64)
-        z_g = late[:, 0 : S * PACK].rearrange("p (n j) -> p n j", j=PACK)
+        z_bf = late[:, 0 : S * PACK].rearrange("p (n j) -> p n j", j=PACK)
+        gated_late = late[:, S * PACK :].bitcast(F32)
 
-        def late_silu(t):
-            silu(t, late[:, S * PACK + 2 * V * (t - 2) : S * PACK + 2 * V * (t - 1)].bitcast(F32))
+        def z_on_scalar(t, lo, hi):
+            nc.scalar.activation(out=z_bf[:, lo:hi, SLOT[t]], in_=h[t][:, lo:hi], func=ACT.Copy, scale=gn_t[:, t, 0:1])
 
-        def plane_on_vector(lo, hi):
-            nc.vector.tensor_scalar(out=z_g[:, lo:hi, SLOT[3]], in0=hw[3][:, lo:hi], scalar1=gn_t[:, 3, 0:1], scalar2=None, op0=ALU.mult)
+        def z_on_vector(t, lo, hi):
+            nc.vector.tensor_scalar(out=z_bf[:, lo:hi, SLOT[t]], in0=h[t][:, lo:hi], scalar1=gn_t[:, t, 0:1], scalar2=None, op0=ALU.mult)
 
-        def w2_quantize(dst, lo, hi):
-            nc.vector.quantize_mx(out=dst.bitcast(FP8X4), scales=w2_scales[:, lo:hi], in_=w2_g[:, lo:hi, :].rearrange("p n j -> p (n j)"))
+        def quantize_w2(dst, lo, hi):
+            nc.vector.quantize_mx(out=dst.bitcast(FP8X4), scales=w2_scales[:, lo:hi], in_=w2_bf[:, lo:hi, :].rearrange("p n j -> p (n j)"))
 
-        late_silu(2)
-        plane(0, 0, S)
-        late_silu(3)
-        plane(1, 0, S)
+        silu(2, gated_late[:, 0:V])
+        z_on_scalar(0, 0, S)
+        silu(LAST, gated_late[:, V : 2 * V])
+        z_on_scalar(1, 0, S)
         scatter(2)
-        plane(2, 0, S - 32)
-        scatter(3)
-        plane_on_vector(0, 64)
-        plane(3, 64, P)
-        plane(2, S - 32, S)
-        plane(3, P, 2 * P)
-        plane(3, 2 * P, S)
-        w2_first = keep.tile([P, 2 * P], U32, name="w2_first", tag="a_g3", align_bytes=64)
-        w2_quantize(w2_first[:], 0, 2 * P)
-        w2_codes = [w2_first[:, m * P : (m + 1) * P] for m in range(2)]
+        z_on_scalar(2, 0, S - HELD)
+        scatter(LAST)
 
-        n = 0
-        for (lo, hi), groups in zip(CHUNKS, (((1, True), (1, True), (2, False)), ((2, True), (2, False)), ((1, True), (1, False), (1, True), (1, False)))):
-            cols = slice(lo, hi)
+        (first_lo, first_hi), (second_lo, second_hi), (third_lo, third_hi) = RANGES
+        w2_early = keep.tile([P, 2 * P], U32, name="w2_early", tag="a3", align_bytes=64)
+        quantize_w2(w2_early[:, 0:P], 0, P)
+        z_on_vector(LAST, first_lo, first_lo + SHARE)
+        z_on_scalar(LAST, first_lo + SHARE, first_hi)
+        z_on_scalar(2, S - HELD, S)
+        z_on_scalar(LAST, second_lo, second_hi)
+        z_on_scalar(LAST, third_lo + SHARE, third_hi)
+        quantize_w2(w2_early[:, P : 2 * P], P, 2 * P)
+        z_on_vector(LAST, third_lo, third_lo + SHARE)
+
+        def quantize_z(lo, hi):
+            codes = keep.tile([P, hi - lo], U32, name=f"z_codes{lo}", align_bytes=64)
+            scales = keep.tile([P, hi - lo], U8, name=f"z_scales{lo}", align_bytes=64)
+            nc.vector.quantize_mx(out=codes[:].bitcast(FP8X4), scales=scales[:], in_=z_bf[:, lo:hi, :].rearrange("p n j -> p (n j)"))
+            return codes, scales
+
+        z_first = quantize_z(first_lo, first_hi)
+        w2_late = keep.tile([P, 2 * P], U32, name="w2_late", tag="h2", align_bytes=64)
+        quantize_w2(w2_late[:], 2 * P, N)
+        w2_codes = [half[:, m * P : (m + 1) * P] for half in (w2_early, w2_late) for m in range(2)]
+
+        store = 0
+        for (lo, hi), groups in zip(RANGES, STORES):
             width = hi - lo
-            z_codes = ring.tile([P, width], U32, name="z_codes", align_bytes=64)
-            z_scales = ring.tile([P, width], U8, name="z_scales", align_bytes=64)
-            nc.vector.quantize_mx(out=z_codes[:].bitcast(FP8X4), scales=z_scales[:], in_=z_g[:, lo:hi, :].rearrange("p n j -> p (n j)"))
-            if lo == 0:
-                w2_rest = keep.tile([P, 2 * P], U32, name="w2_rest", tag="h2", align_bytes=64)
-                w2_quantize(w2_rest[:], 2 * P, N)
-                w2_codes.extend(w2_rest[:, m * P : (m + 1) * P] for m in range(2))
-            m0 = 0
+            z_codes, z_scales = z_first if lo == first_lo else quantize_z(lo, hi)
+            block = 0
             for count, on_vector in groups:
-                bank = banks[n % 8]
+                bank = banks[store % 8]
                 for i in range(count):
-                    rows = slice((m0 + i) * P, (m0 + i + 1) * P)
-                    nc.tensor.matmul_mx(out=bank[:, i * width : (i + 1) * width], lhsT=w2_codes[m0 + i].bitcast(FP8X4), lhsT_scale=w2_scales[:, rows],
+                    m = block + i
+                    nc.tensor.matmul_mx(out=bank[:, i * width : (i + 1) * width], lhsT=w2_codes[m].bitcast(FP8X4),
+                                        lhsT_scale=w2_scales[:, m * P : (m + 1) * P],
                                         rhs=z_codes[:].bitcast(FP8X4), rhs_scale=z_scales[:], start=True, stop=True)
-                res = keep.tile([P, count * width], F32, name=f"res{n}", align_bytes=64)
+                result = keep.tile([P, count * width], F32, name=f"result{store}", align_bytes=64)
                 if on_vector:
-                    nc.vector.tensor_copy(out=res[:], in_=bank[:, 0 : count * width])
+                    nc.vector.tensor_copy(out=result[:], in_=bank[:, 0 : count * width])
                 else:
-                    nc.scalar.copy(out=res[:], in_=bank[:, 0 : count * width])
-                nc.sync.dma_start(out=out[m0 * P : (m0 + count) * P, cols].rearrange("(i p) c -> p i c", p=P),
-                                  in_=res[:].rearrange("p (i c) -> p i c", i=count))
-                m0 = m0 + count
-                n = n + 1
+                    nc.scalar.copy(out=result[:], in_=bank[:, 0 : count * width])
+                nc.sync.dma_start(out=out[block * P : (block + count) * P, lo:hi].rearrange("(i p) c -> p i c", p=P),
+                                  in_=result[:].rearrange("p (i c) -> p i c", i=count))
+                block = block + count
+                store = store + 1

@@ -19,9 +19,9 @@ P = 128
 PACK = 4
 LINE = 8
 LAST = PACK - 1
-SLOT = (2, 0, 1, 3)
+SLOT = (0, 1, 2, 3)
 RANGES = ((0, 128), (128, 256), (256, 512))
-STORES = (((1, True), (1, True), (2, False)), ((2, True), (2, False)), ((1, True), (1, False), (1, True), (1, False)))
+STORES = (((1, False), (1, False), (2, False)), ((2, False), (2, False)), ((1, True), (1, False), (1, True), (1, False)))
 SHARE = 64
 HELD = 32
 
@@ -72,10 +72,6 @@ def tile_picked_revcoup_none_p_kernel(tc, x_words, x_scales, w1, gn, w2, offs, l
                 nc.vector.tensor_copy(out=w1_bf[0][:, lo:hi, :, pair].rearrange("p t (b i) j -> p t b i j", i=LINE), in_=by_plane[:, lo:hi])
             nc.scalar.copy(out=w1_bf[1][:, :, :, pair].rearrange("p t (b i) j -> p t b i j", i=LINE), in_=by_plane[:, 2:4])
 
-        for n in range(2):
-            nc.tensor.matmul_mx(out=banks[7][:], lhsT=x_codes[:, 0:P].bitcast(FP8X4), lhsT_scale=xs_picked[:, 0:P],
-                                rhs=x_codes[:].bitcast(FP8X4), rhs_scale=xs_picked[:], start=True, stop=True)
-
         w2_rows = w2.rearrange("(b t i) c -> t b i c", t=PACK, i=LINE)
         w2_raw = keep.tile([P, PACK, N], F32, name="w2_raw", tag="stage", align_bytes=64)
         for t in range(PACK):
@@ -110,82 +106,77 @@ def tile_picked_revcoup_none_p_kernel(tc, x_words, x_scales, w1, gn, w2, offs, l
             for dst, cols in pieces[t]:
                 first_product(t, dst, cols)
 
-        w2_bf = keep.tile([P, N, PACK], BF16, name="w2_bf", align_bytes=64)
-        w2_scales = keep.tile([P, N], U8, name="w2_scales", align_bytes=64)
         a, b, gated = {}, {}, {}
 
         def leave_psum(t):
             for src, cols in pieces[t]:
                 nc.scalar.copy(out=h[t][:, cols], in_=src)
 
+        def gather(dst, t, offsets):
+            if t == 0:
+                nc.vector.tensor_copy(dst[:], h[t][:].indirect(offsets[:]))
+            else:
+                nc.scalar.activation(out=dst[:], in_=h[t][:].indirect(offsets[:]), func=ACT.Copy)
+
         def gather_a(t):
             a[t] = keep.tile([P, V], F32, name=f"a{t}", tag=f"a{t}", align_bytes=64)
-            nc.vector.tensor_copy(a[t][:], h[t][:].indirect(la_t[:]))
+            gather(a[t], t, la_t)
 
-        def gather_b(t, tag):
-            b[t] = keep.tile([P, V], F32, name=f"b{t}", tag=tag, align_bytes=64)
-            nc.vector.tensor_copy(b[t][:], h[t][:].indirect(lb_t[:]))
+        def gather_b(t):
+            b[t] = keep.tile([P, V], F32, name=f"b{t}", align_bytes=64)
+            gather(b[t], t, lb_t)
 
-        def silu(t, dst):
-            gated[t] = dst
-            nc.scalar.activation(out=dst, in_=a[t][:], func=ACT.Silu)
+        def silu(t):
+            gated[t] = keep.tile([P, V], F32, name=f"gated{t}", align_bytes=64)
+            nc.scalar.activation(out=gated[t][:], in_=a[t][:], func=ACT.Silu)
 
         def scatter(t):
-            nc.vector.tensor_tensor(h[t][:].indirect(lb_t[:]), b[t][:], gated[t], ALU.add)
+            nc.vector.tensor_tensor(h[t][:].indirect(lb_t[:]), b[t][:], gated[t][:], ALU.add)
 
-        gated_early = keep.tile([P, 2, V], F32, name="gated_early", align_bytes=64)
-        gather_a(0)
-        gather_b(0, "b0")
         leave_psum(1)
-        silu(0, gated_early[:, 0, :])
-        gather_a(1)
-        gather_b(1, "b1")
-        leave_psum(2)
+        gather_a(0)
+        gather_b(0)
+        silu(0)
         scatter(0)
-        leave_psum(3)
-        silu(1, gated_early[:, 1, :])
-        gather_a(2)
-        gather_b(2, "b2")
-        gather_a(3)
+        gather_a(1)
+        leave_psum(2)
+        gather_b(1)
+        silu(1)
         scatter(1)
-        gather_b(3, "a1")
+        z_planes = keep.tile([P, PACK, S], BF16, name="z_planes", tag="a1", align_bytes=64)
 
-        for c in range(N // P):
-            cols = slice(c * P, (c + 1) * P)
+        def z_on_vector(t, lo, hi):
+            nc.vector.tensor_scalar(out=z_planes[:, t, lo:hi], in0=h[t][:, lo:hi], scalar1=gn_t[:, t, 0:1], scalar2=None, op0=ALU.mult)
+
+        z_on_vector(0, 0, S)
+        z_on_vector(1, 0, S)
+        gather_a(2)
+        leave_psum(3)
+        gather_b(2)
+        silu(2)
+        scatter(2)
+        gather_a(3)
+        gather_b(3)
+        silu(3)
+        scatter(3)
+
+        w2_bf = keep.tile([P, N, PACK], BF16, name="w2_bf", tag="a3", align_bytes=64)
+        w2_words = keep.tile([P, N], U32, name="w2_words", align_bytes=64)
+        w2_scales = keep.tile([P, N], U8, name="w2_scales", align_bytes=64)
+        z_bf = keep.tile([P, S, PACK], BF16, name="z_bf", align_bytes=64)
+
+        def cast_w2(m):
+            cols = slice(m * P, (m + 1) * P)
             nc.scalar.copy(out=w2_bf[:, cols, :].rearrange("p (g i) j -> p g j i", i=4),
                            in_=w2_raw[:, :, cols].rearrange("p j (g i) -> p g j i", i=4))
 
-        late = keep.tile([P, S * PACK + 4 * V], BF16, name="late", tag="stage", align_bytes=64)
-        z_bf = late[:, 0 : S * PACK].rearrange("p (n j) -> p n j", j=PACK)
-        gated_late = late[:, S * PACK :].bitcast(F32)
+        def quantize_w2(m):
+            cols = slice(m * P, (m + 1) * P)
+            nc.vector.quantize_mx(out=w2_words[:, cols].bitcast(FP8X4), scales=w2_scales[:, cols], in_=w2_bf[:, cols, :].rearrange("p n j -> p (n j)"))
 
-        def z_on_scalar(t, lo, hi):
-            nc.scalar.activation(out=z_bf[:, lo:hi, SLOT[t]], in_=h[t][:, lo:hi], func=ACT.Copy, scale=gn_t[:, t, 0:1])
-
-        def z_on_vector(t, lo, hi):
-            nc.vector.tensor_scalar(out=z_bf[:, lo:hi, SLOT[t]], in0=h[t][:, lo:hi], scalar1=gn_t[:, t, 0:1], scalar2=None, op0=ALU.mult)
-
-        def quantize_w2(dst, lo, hi):
-            nc.vector.quantize_mx(out=dst.bitcast(FP8X4), scales=w2_scales[:, lo:hi], in_=w2_bf[:, lo:hi, :].rearrange("p n j -> p (n j)"))
-
-        silu(2, gated_late[:, 0:V])
-        z_on_scalar(0, 0, S)
-        silu(LAST, gated_late[:, V : 2 * V])
-        z_on_scalar(1, 0, S)
-        scatter(2)
-        z_on_scalar(2, 0, S - HELD)
-        scatter(LAST)
-
-        (first_lo, first_hi), (second_lo, second_hi), (third_lo, third_hi) = RANGES
-        w2_early = keep.tile([P, 2 * P], U32, name="w2_early", tag="a3", align_bytes=64)
-        quantize_w2(w2_early[:, 0:P], 0, P)
-        z_on_vector(LAST, first_lo, first_lo + SHARE)
-        z_on_scalar(LAST, first_lo + SHARE, first_hi)
-        z_on_scalar(2, S - HELD, S)
-        z_on_scalar(LAST, second_lo, second_hi)
-        z_on_scalar(LAST, third_lo + SHARE, third_hi)
-        quantize_w2(w2_early[:, P : 2 * P], P, 2 * P)
-        z_on_vector(LAST, third_lo, third_lo + SHARE)
+        def interleave(lo, hi):
+            nc.vector.tensor_copy(out=z_bf[:, lo:hi, :].rearrange("p (g i) j -> p g j i", i=4),
+                                  in_=z_planes[:, :, lo:hi].rearrange("p j (g i) -> p g j i", i=4))
 
         def quantize_z(lo, hi):
             codes = keep.tile([P, hi - lo], U32, name=f"z_codes{lo}", align_bytes=64)
@@ -193,15 +184,30 @@ def tile_picked_revcoup_none_p_kernel(tc, x_words, x_scales, w1, gn, w2, offs, l
             nc.vector.quantize_mx(out=codes[:].bitcast(FP8X4), scales=scales[:], in_=z_bf[:, lo:hi, :].rearrange("p n j -> p (n j)"))
             return codes, scales
 
-        z_first = quantize_z(first_lo, first_hi)
-        w2_late = keep.tile([P, 2 * P], U32, name="w2_late", tag="h2", align_bytes=64)
-        quantize_w2(w2_late[:], 2 * P, N)
-        w2_codes = [half[:, m * P : (m + 1) * P] for half in (w2_early, w2_late) for m in range(2)]
+        cast_w2(0)
+        nc.scalar.activation(out=z_planes[:, 2, :], in_=h[2][:], func=ACT.Copy, scale=gn_t[:, 2, 0:1])
+        for m in range(1, PACK):
+            cast_w2(m)
+        first, second, third = RANGES
+        z_quantized = {}
+        z_on_vector(LAST, *first)
+        quantize_w2(0)
+        interleave(*first)
+        z_on_vector(LAST, second[0], S)
+        z_quantized[first] = quantize_z(*first)
+        quantize_w2(1)
+        interleave(*second)
+        quantize_w2(2)
+        z_quantized[second] = quantize_z(*second)
+        interleave(*third)
+        quantize_w2(3)
+        z_quantized[third] = quantize_z(*third)
+        w2_codes = [w2_words[:, m * P : (m + 1) * P] for m in range(PACK)]
 
         store = 0
         for (lo, hi), groups in zip(RANGES, STORES):
             width = hi - lo
-            z_codes, z_scales = z_first if lo == first_lo else quantize_z(lo, hi)
+            z_codes, z_scales = z_quantized[(lo, hi)]
             block = 0
             for count, on_vector in groups:
                 bank = banks[store % 8]

@@ -19,7 +19,7 @@ P = 128
 PACK = 4
 LINE = 8
 LAST = PACK - 1
-SLOT = (0, 1, 2, 3)
+SLOT = (2, 0, 1, 3)
 RANGES = ((0, 128), (128, 256), (256, 512))
 STORES = (((1, False), (1, False), (2, False)), ((2, False), (2, False)), ((1, True), (1, False), (1, True), (1, False)))
 SHARE = 64
@@ -91,6 +91,7 @@ def tile_picked_revcoup_none_p_kernel(tc, x_words, x_scales, w1, gn, w2, offs, l
             nc.tensor.matmul_mx(out=dst, lhsT=w1_codes[t][:].bitcast(FP8X4), lhsT_scale=w1_scales[t][:],
                                 rhs=x_codes[:, cols].bitcast(FP8X4), rhs_scale=x_scale[:, cols], start=True, stop=True)
 
+        a = [keep.tile([P, V], F32, name=f"a{t}", tag=f"a{t}", align_bytes=64) for t in range(PACK)]
         h = [keep.tile([P, S], F32, name=f"h{t}", tag=f"h{t}", align_bytes=64) for t in range(PACK)]
         for n in range(4):
             cols = slice(n * P, (n + 1) * P)
@@ -99,129 +100,129 @@ def tile_picked_revcoup_none_p_kernel(tc, x_words, x_scales, w1, gn, w2, offs, l
                 nc.vector.tensor_copy(out=h[0][:, cols], in_=banks[n][:, 0:P])
             else:
                 nc.scalar.copy(out=h[0][:, cols], in_=banks[n][:, 0:P])
-        halves = (slice(0, S // 2), slice(S // 2, S))
-        pieces = {1: ((banks[4][:, 0 : S // 2], halves[0]), (banks[7][:, 0 : S // 2], halves[1])),
-                  2: ((banks[5][:], slice(0, S)),), 3: ((banks[6][:], slice(0, S)),)}
         for t in range(1, PACK):
-            for dst, cols in pieces[t]:
-                first_product(t, dst, cols)
+            first_product(t, banks[3 + t][:], slice(0, S))
+        b = [keep.tile([P, V], F32, name=f"b{t}", tag=f"b{t}", align_bytes=64) for t in range(PACK)]
+        gated = [keep.tile([P, V], F32, name=f"gated{t}", align_bytes=64) for t in range(PACK)]
 
-        a, b, gated = {}, {}, {}
-
-        def leave_psum(t):
-            for src, cols in pieces[t]:
-                nc.scalar.copy(out=h[t][:, cols], in_=src)
-
-        def gather(dst, t, offsets):
-            if t == 0:
-                nc.vector.tensor_copy(dst[:], h[t][:].indirect(offsets[:]))
+        def gather(dst, t, offsets, lo=0, hi=V, on_vector=False):
+            window = h[t][:].indirect(offsets[:, lo // 16 : hi // 16])
+            if on_vector:
+                nc.vector.tensor_copy(dst[t][:, lo:hi], window)
             else:
-                nc.scalar.activation(out=dst[:], in_=h[t][:].indirect(offsets[:]), func=ACT.Copy)
-
-        def gather_a(t):
-            a[t] = keep.tile([P, V], F32, name=f"a{t}", tag=f"a{t}", align_bytes=64)
-            gather(a[t], t, la_t)
-
-        def gather_b(t):
-            b[t] = keep.tile([P, V], F32, name=f"b{t}", align_bytes=64)
-            gather(b[t], t, lb_t)
+                nc.scalar.activation(out=dst[t][:, lo:hi], in_=window, func=ACT.Copy)
 
         def silu(t):
-            gated[t] = keep.tile([P, V], F32, name=f"gated{t}", align_bytes=64)
             nc.scalar.activation(out=gated[t][:], in_=a[t][:], func=ACT.Silu)
 
         def scatter(t):
             nc.vector.tensor_tensor(h[t][:].indirect(lb_t[:]), b[t][:], gated[t][:], ALU.add)
 
-        leave_psum(1)
-        gather_a(0)
-        gather_b(0)
-        silu(0)
-        scatter(0)
-        gather_a(1)
-        leave_psum(2)
-        gather_b(1)
-        silu(1)
-        scatter(1)
-        z_planes = keep.tile([P, PACK, S], BF16, name="z_planes", tag="a1", align_bytes=64)
+        def leave_psum(t):
+            nc.scalar.copy(out=h[t][:], in_=banks[3 + t][:])
 
-        def z_on_vector(t, lo, hi):
-            nc.vector.tensor_scalar(out=z_planes[:, t, lo:hi], in0=h[t][:, lo:hi], scalar1=gn_t[:, t, 0:1], scalar2=None, op0=ALU.mult)
-
-        z_on_vector(0, 0, S)
-        z_on_vector(1, 0, S)
-        gather_a(2)
-        leave_psum(3)
-        gather_b(2)
-        silu(2)
-        scatter(2)
-        gather_a(3)
-        gather_b(3)
-        silu(3)
-        scatter(3)
-
-        w2_bf = keep.tile([P, N, PACK], BF16, name="w2_bf", tag="a3", align_bytes=64)
-        w2_words = keep.tile([P, N], U32, name="w2_words", align_bytes=64)
+        w2_bf = keep.tile([P, N, PACK], BF16, name="w2_bf", tag="a1", align_bytes=64)
         w2_scales = keep.tile([P, N], U8, name="w2_scales", align_bytes=64)
-        z_bf = keep.tile([P, S, PACK], BF16, name="z_bf", align_bytes=64)
 
         def cast_w2(m):
             cols = slice(m * P, (m + 1) * P)
             nc.scalar.copy(out=w2_bf[:, cols, :].rearrange("p (g i) j -> p g j i", i=4),
                            in_=w2_raw[:, :, cols].rearrange("p j (g i) -> p g j i", i=4))
 
+        gather(a, 0, la_t, on_vector=True)
+        gather(b, 0, lb_t, on_vector=True)
+        leave_psum(1)
+        silu(0)
+        gather(a, 1, la_t, on_vector=True)
+        scatter(0)
+        leave_psum(2)
+        gather(b, 1, lb_t)
+        silu(1)
+        scatter(1)
+        gather(a, 2, la_t)
+        gather(b, 2, lb_t)
+        leave_psum(3)
+        silu(2)
+        scatter(2)
+
+        z_early = keep.tile([P, S * PACK], BF16, name="z_early", tag="a2", align_bytes=64)
+        z_first = z_early[:, 0 : P * PACK]
+        z_pairs = z_early[:, P * PACK :].rearrange("p (u n e) -> p u n e", u=2, e=2)
+        pair_words = z_early[:, P * PACK :].bitcast(I32).rearrange("p (u n) -> p n u", u=2)
+
+        def z_plane(t, lo, hi):
+            if lo == 0:
+                dst = z_first.rearrange("p (n j) -> p n j", j=PACK)[:, :, SLOT[t]]
+            else:
+                dst = z_pairs[:, SLOT[t] // 2, lo - P : hi - P, SLOT[t] % 2]
+            if t in (0, LAST):
+                nc.vector.tensor_scalar(out=dst, in0=h[t][:, lo:hi], scalar1=gn_t[:, t, 0:1], scalar2=None, op0=ALU.mult)
+            else:
+                nc.scalar.activation(out=dst, in_=h[t][:, lo:hi], func=ACT.Copy, scale=gn_t[:, t, 0:1])
+
+        z_plane(0, 0, P)
+        z_plane(0, P, S)
+        gather(a, 3, la_t)
+        gather(b, 3, lb_t)
+        cast_w2(0)
+        silu(3)
+        scatter(3)
+        z_plane(1, 0, P)
+        z_plane(2, 0, P)
+        cast_w2(1)
+        z_plane(1, P, 2 * P)
+        z_plane(2, P, 2 * P)
+        cast_w2(2)
+        cast_w2(3)
+        z_plane(1, 2 * P, S)
+        z_plane(2, 2 * P, S)
+
+        w2_words = keep.tile([P, N], U32, name="w2_words", tag="a3", align_bytes=64)
+
         def quantize_w2(m):
             cols = slice(m * P, (m + 1) * P)
             nc.vector.quantize_mx(out=w2_words[:, cols].bitcast(FP8X4), scales=w2_scales[:, cols], in_=w2_bf[:, cols, :].rearrange("p n j -> p (n j)"))
 
-        def interleave(lo, hi):
-            nc.vector.tensor_copy(out=z_bf[:, lo:hi, :].rearrange("p (g i) j -> p g j i", i=4),
-                                  in_=z_planes[:, :, lo:hi].rearrange("p j (g i) -> p g j i", i=4))
+        z_bf, z_codes, z_scales = {0: z_first}, {}, {}
 
-        def quantize_z(lo, hi):
-            codes = keep.tile([P, hi - lo], U32, name=f"z_codes{lo}", align_bytes=64)
-            scales = keep.tile([P, hi - lo], U8, name=f"z_scales{lo}", align_bytes=64)
-            nc.vector.quantize_mx(out=codes[:].bitcast(FP8X4), scales=scales[:], in_=z_bf[:, lo:hi, :].rearrange("p n j -> p (n j)"))
-            return codes, scales
+        def interleave(r):
+            tile = keep.tile([P, P * PACK], BF16, name=f"z_bf{r}", align_bytes=64)
+            z_bf[r] = tile[:]
+            nc.vector.tensor_copy(out=tile[:].bitcast(I32).rearrange("p (n u) -> p n u", u=2), in_=pair_words[:, (r - 1) * P : r * P, :])
 
-        cast_w2(0)
-        nc.scalar.activation(out=z_planes[:, 2, :], in_=h[2][:], func=ACT.Copy, scale=gn_t[:, 2, 0:1])
-        for m in range(1, PACK):
-            cast_w2(m)
-        first, second, third = RANGES
-        z_quantized = {}
-        z_on_vector(LAST, *first)
+        def quantize_z(r):
+            z_codes[r] = keep.tile([P, P], U32, name=f"z_codes{r}", align_bytes=64)
+            z_scales[r] = keep.tile([P, P], U8, name=f"z_scales{r}", align_bytes=64)
+            nc.vector.quantize_mx(out=z_codes[r][:].bitcast(FP8X4), scales=z_scales[r][:], in_=z_bf[r])
+
         quantize_w2(0)
-        interleave(*first)
-        z_on_vector(LAST, second[0], S)
-        z_quantized[first] = quantize_z(*first)
+        z_plane(LAST, 0, P)
         quantize_w2(1)
-        interleave(*second)
+        z_plane(LAST, P, 2 * P)
+        quantize_z(0)
+        interleave(1)
+        z_plane(LAST, 2 * P, S)
+        quantize_z(1)
         quantize_w2(2)
-        z_quantized[second] = quantize_z(*second)
-        interleave(*third)
         quantize_w2(3)
-        z_quantized[third] = quantize_z(*third)
-        w2_codes = [w2_words[:, m * P : (m + 1) * P] for m in range(PACK)]
+        interleave(2)
+        interleave(3)
+        quantize_z(2)
+        quantize_z(3)
 
-        store = 0
-        for (lo, hi), groups in zip(RANGES, STORES):
-            width = hi - lo
-            z_codes, z_scales = z_quantized[(lo, hi)]
-            block = 0
-            for count, on_vector in groups:
-                bank = banks[store % 8]
-                for i in range(count):
-                    m = block + i
-                    nc.tensor.matmul_mx(out=bank[:, i * width : (i + 1) * width], lhsT=w2_codes[m].bitcast(FP8X4),
-                                        lhsT_scale=w2_scales[:, m * P : (m + 1) * P],
-                                        rhs=z_codes[:].bitcast(FP8X4), rhs_scale=z_scales[:], start=True, stop=True)
-                result = keep.tile([P, count * width], F32, name=f"result{store}", align_bytes=64)
-                if on_vector:
-                    nc.vector.tensor_copy(out=result[:], in_=bank[:, 0 : count * width])
-                else:
-                    nc.scalar.copy(out=result[:], in_=bank[:, 0 : count * width])
-                nc.sync.dma_start(out=out[block * P : (block + count) * P, lo:hi].rearrange("(i p) c -> p i c", p=P),
-                                  in_=result[:].rearrange("p (i c) -> p i c", i=count))
-                block = block + count
-                store = store + 1
+        def multiply_and_store(m, ranges, bank, on_vector=False):
+            width = len(ranges) * P
+            for i, r in enumerate(ranges):
+                nc.tensor.matmul_mx(out=bank[:, i * P : (i + 1) * P], lhsT=w2_words[:, m * P : (m + 1) * P].bitcast(FP8X4),
+                                    lhsT_scale=w2_scales[:, m * P : (m + 1) * P],
+                                    rhs=z_codes[r][:].bitcast(FP8X4), rhs_scale=z_scales[r][:], start=True, stop=True)
+            result = keep.tile([P, width], F32, name=f"result{m}{ranges[0]}", align_bytes=64)
+            if on_vector:
+                nc.vector.tensor_copy(out=result[:], in_=bank[:, 0:width])
+            else:
+                nc.scalar.copy(out=result[:], in_=bank[:, 0:width])
+            nc.sync.dma_start(out=out[m * P : (m + 1) * P, ranges[0] * P : ranges[0] * P + width], in_=result[:])
+
+        steps = [(m, (r,)) for r in range(2) for m in range(2)] + [(m, (0, 1)) for m in range(2, PACK)] + [(m, (2, 3)) for m in range(PACK)]
+        for n, (m, ranges) in enumerate(steps):
+            multiply_and_store(m, ranges, banks[n % 8], on_vector=ranges[0] == 2 and m % 2 == 0)

@@ -19,11 +19,8 @@ P = 128
 PACK = 4
 LINE = 8
 LAST = PACK - 1
-SLOT = (2, 0, 1, 3)
-RANGES = ((0, 128), (128, 256), (256, 512))
-STORES = (((1, False), (1, False), (2, False)), ((2, False), (2, False)), ((1, True), (1, False), (1, True), (1, False)))
-SHARE = 64
-HELD = 32
+SLOT = (0, 2, 3, 1)
+SPLIT = 96
 
 
 def tile_picked_revcoup_none_p_kernel(tc, x_words, x_scales, w1, gn, w2, offs, la, lb, out):
@@ -58,34 +55,37 @@ def tile_picked_revcoup_none_p_kernel(tc, x_words, x_scales, w1, gn, w2, offs, l
         xs_picked = keep.tile([P, S], U8, name="xs_picked", align_bytes=64)
         nc.vector.tensor_copy(xs_picked[:], xs_all[:].indirect(offs_t[:]))
         x_scale = keep.tile([P, S], U8, name="x_scale", align_bytes=64)
-        nc.gpsimd.memset(x_scale[:].bitcast(I32), 0)
-        for r in range(4):
+        nc.vector.tensor_copy(out=x_scale[:].bitcast(I32), in_=xs_picked[:].bitcast(I32))
+        for r in range(1, 4):
             nc.sync.dma_start(out=x_scale[r:P:32, :].bitcast(I32), in_=xs_picked[LINE * r : P : 32, :].bitcast(I32))
 
         x_codes = keep.tile([P, S], U32, name="x_codes", align_bytes=64)
         w1_bf = [keep.tile([P, 2, P, PACK], BF16, name=f"w1_bf{e}", align_bytes=64) for e in range(2)]
         nc.vector.tensor_copy(x_codes[:], x_all[:].indirect(offs_t[:]))
-        for u, vector_planes in enumerate((((0, 2),), ((0, 1), (1, 2)))):
-            by_plane = w1_raw[u][:].rearrange("p j (b t i) -> p t b i j", t=PACK, i=LINE)
+        for u in range(2):
+            by_byte = w1_raw[u][:].rearrange("p j (m e f) -> p f m e j", e=2, f=2)
             pair = slice(2 * u, 2 * u + 2)
-            for lo, hi in vector_planes:
-                nc.vector.tensor_copy(out=w1_bf[0][:, lo:hi, :, pair].rearrange("p t (b i) j -> p t b i j", i=LINE), in_=by_plane[:, lo:hi])
-            nc.scalar.copy(out=w1_bf[1][:, :, :, pair].rearrange("p t (b i) j -> p t b i j", i=LINE), in_=by_plane[:, 2:4])
+            if u == 0:
+                nc.vector.tensor_copy(out=w1_bf[0][:, :, :, pair].rearrange("p e m j -> p m e j"), in_=by_byte[:, 0])
+            else:
+                nc.vector.tensor_copy(out=w1_bf[0][:, 0, 0:SPLIT, pair], in_=by_byte[:, 0, 0:SPLIT, 0, :])
+                nc.scalar.copy(out=w1_bf[0][:, 0, SPLIT:P, pair], in_=by_byte[:, 0, SPLIT:P, 0, :])
+                nc.vector.tensor_copy(out=w1_bf[0][:, 1, :, pair], in_=by_byte[:, 0, :, 1, :])
+            nc.scalar.copy(out=w1_bf[1][:, :, :, pair].rearrange("p e m j -> p m e j"), in_=by_byte[:, 1])
 
-        w2_rows = w2.rearrange("(b t i) c -> t b i c", t=PACK, i=LINE)
-        w2_raw = keep.tile([P, PACK, N], F32, name="w2_raw", tag="stage", align_bytes=64)
-        for t in range(PACK):
-            nc.sync.dma_start(out=w2_raw[:, SLOT[t], :], in_=w2_rows[t])
-        gn_t = keep.tile([P, PACK, 8], F32, name="gn_t", tag="w1_raw1", align_bytes=64)
-        with nc.allow_non_contiguous_dma(reason="one gain a partition and plane"):
-            for t in range(PACK):
-                nc.sync.dma_start(out=gn_t[:, t, 0:1], in_=gn.rearrange("(b t i) o -> t b i o", t=PACK, i=LINE)[t])
+        w2_rows = w2.rearrange("(p j) c -> p j c", j=PACK)
+        w2_first = keep.tile([P, PACK, P], F32, name="w2_first", tag="stage", align_bytes=64)
+        nc.sync.dma_start(out=w2_first[:], in_=w2_rows[:, :, 0:P])
+        w2_rest = keep.tile([P, PACK, N - P], F32, name="w2_rest", tag="w1_raw0", align_bytes=64)
+        nc.sync.dma_start(out=w2_rest[:], in_=w2_rows[:, :, P:N])
+        gn_t = keep.tile([P, PACK], F32, name="gn_t", tag="w1_raw1", align_bytes=64)
+        nc.sync.dma_start(out=gn_t[:], in_=gn.rearrange("(p j) o -> p (j o)", j=PACK))
 
         w1_codes = [keep.tile([P, P], U32, name=f"w1_codes{t}", align_bytes=64) for t in range(PACK)]
         w1_scales = [keep.tile([P, P], U8, name=f"w1_scales{t}", align_bytes=64) for t in range(PACK)]
         for t in range(PACK):
             nc.vector.quantize_mx(out=w1_codes[t][:].bitcast(FP8X4), scales=w1_scales[t][:],
-                                  in_=w1_bf[t // 2][:, t % 2, :, :].rearrange("p m j -> p (m j)"))
+                                  in_=w1_bf[SLOT[t] % 2][:, SLOT[t] // 2, :, :].rearrange("p m j -> p (m j)"))
 
         def first_product(t, dst, cols):
             nc.tensor.matmul_mx(out=dst, lhsT=w1_codes[t][:].bitcast(FP8X4), lhsT_scale=w1_scales[t][:],
@@ -96,14 +96,14 @@ def tile_picked_revcoup_none_p_kernel(tc, x_words, x_scales, w1, gn, w2, offs, l
         for n in range(4):
             cols = slice(n * P, (n + 1) * P)
             first_product(0, banks[n][:, 0:P], cols)
-            if n % 2 == 0:
+            if n < 2:
                 nc.vector.tensor_copy(out=h[0][:, cols], in_=banks[n][:, 0:P])
             else:
                 nc.scalar.copy(out=h[0][:, cols], in_=banks[n][:, 0:P])
         for t in range(1, PACK):
             first_product(t, banks[3 + t][:], slice(0, S))
         b = [keep.tile([P, V], F32, name=f"b{t}", tag=f"b{t}", align_bytes=64) for t in range(PACK)]
-        gated = [keep.tile([P, V], F32, name=f"gated{t}", align_bytes=64) for t in range(PACK)]
+        gated = [keep.tile([P, V], F32, name=f"gated{t}", tag=f"gated{t}", align_bytes=64) for t in range(PACK)]
 
         def gather(dst, t, offsets, lo=0, hi=V, on_vector=False):
             window = h[t][:].indirect(offsets[:, lo // 16 : hi // 16])
@@ -118,24 +118,37 @@ def tile_picked_revcoup_none_p_kernel(tc, x_words, x_scales, w1, gn, w2, offs, l
         def scatter(t):
             nc.vector.tensor_tensor(h[t][:].indirect(lb_t[:]), b[t][:], gated[t][:], ALU.add)
 
-        def leave_psum(t):
-            nc.scalar.copy(out=h[t][:], in_=banks[3 + t][:])
+        def leave_psum(t, lo=0, hi=S):
+            nc.scalar.copy(out=h[t][:, lo:hi], in_=banks[3 + t][:, lo:hi])
 
-        w2_bf = keep.tile([P, N, PACK], BF16, name="w2_bf", tag="a1", align_bytes=64)
+        w2_bf_first = keep.tile([P, P, PACK], BF16, name="w2_bf_first", align_bytes=64)
+        w2_bf_rest = keep.tile([P, N - P, PACK], BF16, name="w2_bf_rest", tag="gated2", align_bytes=64)
+
+        def w2_bf(m):
+            return w2_bf_first[:] if m == 0 else w2_bf_rest[:, (m - 1) * P : m * P, :]
+
         w2_scales = keep.tile([P, N], U8, name="w2_scales", align_bytes=64)
 
         def cast_w2(m):
-            cols = slice(m * P, (m + 1) * P)
-            nc.scalar.copy(out=w2_bf[:, cols, :].rearrange("p (g i) j -> p g j i", i=4),
-                           in_=w2_raw[:, :, cols].rearrange("p j (g i) -> p g j i", i=4))
+            raw = w2_first[:] if m == 0 else w2_rest[:, :, (m - 1) * P : m * P]
+            copy = nc.vector.tensor_copy if m == 0 else nc.scalar.copy
+            copy(out=w2_bf(m).rearrange("p (g i) j -> p g j i", i=4), in_=raw.rearrange("p j (g i) -> p g j i", i=4))
 
+        w2_words = keep.tile([P, N], U32, name="w2_words", tag="a3", align_bytes=64)
+
+        def quantize_w2(m):
+            cols = slice(m * P, (m + 1) * P)
+            nc.vector.quantize_mx(out=w2_words[:, cols].bitcast(FP8X4), scales=w2_scales[:, cols], in_=w2_bf(m).rearrange("p n j -> p (n j)"))
+
+        cast_w2(0)
         gather(a, 0, la_t, on_vector=True)
         gather(b, 0, lb_t, on_vector=True)
         leave_psum(1)
+        leave_psum(2, 0, S // 2)
         silu(0)
         gather(a, 1, la_t, on_vector=True)
         scatter(0)
-        leave_psum(2)
+        leave_psum(2, S // 2, S)
         gather(b, 1, lb_t)
         silu(1)
         scatter(1)
@@ -150,21 +163,21 @@ def tile_picked_revcoup_none_p_kernel(tc, x_words, x_scales, w1, gn, w2, offs, l
         z_pairs = z_early[:, P * PACK :].rearrange("p (u n e) -> p u n e", u=2, e=2)
         pair_words = z_early[:, P * PACK :].bitcast(I32).rearrange("p (u n) -> p n u", u=2)
 
-        def z_plane(t, lo, hi):
+        def z_plane(t, lo, hi, on_vector=False):
             if lo == 0:
                 dst = z_first.rearrange("p (n j) -> p n j", j=PACK)[:, :, SLOT[t]]
             else:
                 dst = z_pairs[:, SLOT[t] // 2, lo - P : hi - P, SLOT[t] % 2]
-            if t in (0, LAST):
-                nc.vector.tensor_scalar(out=dst, in0=h[t][:, lo:hi], scalar1=gn_t[:, t, 0:1], scalar2=None, op0=ALU.mult)
+            if on_vector:
+                nc.vector.tensor_scalar(out=dst, in0=h[t][:, lo:hi], scalar1=gn_t[:, SLOT[t] : SLOT[t] + 1], scalar2=None, op0=ALU.mult)
             else:
-                nc.scalar.activation(out=dst, in_=h[t][:, lo:hi], func=ACT.Copy, scale=gn_t[:, t, 0:1])
+                nc.scalar.activation(out=dst, in_=h[t][:, lo:hi], func=ACT.Copy, scale=gn_t[:, SLOT[t] : SLOT[t] + 1])
 
-        z_plane(0, 0, P)
-        z_plane(0, P, S)
+        z_plane(0, 2 * P, S, on_vector=True)
+        z_plane(0, P, 2 * P)
         gather(a, 3, la_t)
         gather(b, 3, lb_t)
-        cast_w2(0)
+        z_plane(0, 0, P)
         silu(3)
         scatter(3)
         z_plane(1, 0, P)
@@ -176,12 +189,6 @@ def tile_picked_revcoup_none_p_kernel(tc, x_words, x_scales, w1, gn, w2, offs, l
         cast_w2(3)
         z_plane(1, 2 * P, S)
         z_plane(2, 2 * P, S)
-
-        w2_words = keep.tile([P, N], U32, name="w2_words", tag="a3", align_bytes=64)
-
-        def quantize_w2(m):
-            cols = slice(m * P, (m + 1) * P)
-            nc.vector.quantize_mx(out=w2_words[:, cols].bitcast(FP8X4), scales=w2_scales[:, cols], in_=w2_bf[:, cols, :].rearrange("p n j -> p (n j)"))
 
         z_bf, z_codes, z_scales = {0: z_first}, {}, {}
 
@@ -196,12 +203,12 @@ def tile_picked_revcoup_none_p_kernel(tc, x_words, x_scales, w1, gn, w2, offs, l
             nc.vector.quantize_mx(out=z_codes[r][:].bitcast(FP8X4), scales=z_scales[r][:], in_=z_bf[r])
 
         quantize_w2(0)
-        z_plane(LAST, 0, P)
+        z_plane(LAST, 0, P, on_vector=True)
         quantize_w2(1)
-        z_plane(LAST, P, 2 * P)
+        z_plane(LAST, P, 2 * P, on_vector=True)
         quantize_z(0)
         interleave(1)
-        z_plane(LAST, 2 * P, S)
+        z_plane(LAST, 2 * P, S, on_vector=True)
         quantize_z(1)
         quantize_w2(2)
         quantize_w2(3)

@@ -52,7 +52,7 @@ def tile_picked_revcoup_none_p_kernel(tc, x_words, x_scales, w1, gn, w2, offs, l
         nc.sync.dma_start(la_t[:], la)
         nc.sync.dma_start(lb_t[:], lb)
 
-        xs_picked = keep.tile([P, S], U8, name="xs_picked", align_bytes=64)
+        xs_picked = keep.tile([P, S], U8, name="xs_picked", tag="picked", align_bytes=64)
         nc.vector.tensor_copy(xs_picked[:], xs_all[:].indirect(offs_t[:]))
         x_scale = keep.tile([P, S], U8, name="x_scale", align_bytes=64)
         nc.vector.tensor_copy(out=x_scale[:].bitcast(I32), in_=xs_picked[:].bitcast(I32))
@@ -76,9 +76,11 @@ def tile_picked_revcoup_none_p_kernel(tc, x_words, x_scales, w1, gn, w2, offs, l
         w2_rows = w2.rearrange("(p j) c -> p j c", j=PACK)
         w2_first = keep.tile([P, PACK, P], F32, name="w2_first", tag="stage", align_bytes=64)
         nc.sync.dma_start(out=w2_first[:], in_=w2_rows[:, :, 0:P])
-        w2_rest = keep.tile([P, PACK, N - P], F32, name="w2_rest", tag="w1_raw0", align_bytes=64)
-        nc.sync.dma_start(out=w2_rest[:], in_=w2_rows[:, :, P:N])
-        gn_t = keep.tile([P, PACK], F32, name="gn_t", tag="w1_raw1", align_bytes=64)
+        w2_second = keep.tile([P, PACK, P], F32, name="w2_second", tag="w1_raw0", align_bytes=64)
+        nc.sync.dma_start(out=w2_second[:], in_=w2_rows[:, :, P : 2 * P])
+        w2_rest = keep.tile([P, PACK, N // 2], F32, name="w2_rest", tag="w1_raw1", align_bytes=64)
+        nc.sync.dma_start(out=w2_rest[:], in_=w2_rows[:, :, N // 2 : N])
+        gn_t = keep.tile([P, PACK], F32, name="gn_t", tag="picked", align_bytes=64)
         nc.sync.dma_start(out=gn_t[:], in_=gn.rearrange("(p j) o -> p (j o)", j=PACK))
 
         w1_codes = [keep.tile([P, P], U32, name=f"w1_codes{t}", align_bytes=64) for t in range(PACK)]
@@ -122,15 +124,16 @@ def tile_picked_revcoup_none_p_kernel(tc, x_words, x_scales, w1, gn, w2, offs, l
             nc.scalar.copy(out=h[t][:, lo:hi], in_=banks[3 + t][:, lo:hi])
 
         w2_bf_first = keep.tile([P, P, PACK], BF16, name="w2_bf_first", align_bytes=64)
-        w2_bf_rest = keep.tile([P, N - P, PACK], BF16, name="w2_bf_rest", tag="gated2", align_bytes=64)
+        w2_bf_second = keep.tile([P, P, PACK], BF16, name="w2_bf_second", tag="stage", align_bytes=64)
+        w2_bf_rest = keep.tile([P, N // 2, PACK], BF16, name="w2_bf_rest", tag="gated2", align_bytes=64)
 
         def w2_bf(m):
-            return w2_bf_first[:] if m == 0 else w2_bf_rest[:, (m - 1) * P : m * P, :]
+            return (w2_bf_first, w2_bf_second)[m][:] if m < 2 else w2_bf_rest[:, (m - 2) * P : (m - 1) * P, :]
 
         w2_scales = keep.tile([P, N], U8, name="w2_scales", align_bytes=64)
 
         def cast_w2(m):
-            raw = w2_first[:] if m == 0 else w2_rest[:, :, (m - 1) * P : m * P]
+            raw = w2_first[:] if m == 0 else w2_rest[:, :, (m - 2) * P : (m - 1) * P]
             copy = nc.vector.tensor_copy if m == 0 else nc.scalar.copy
             copy(out=w2_bf(m).rearrange("p (g i) j -> p g j i", i=4), in_=raw.rearrange("p j (g i) -> p g j i", i=4))
 
@@ -141,6 +144,7 @@ def tile_picked_revcoup_none_p_kernel(tc, x_words, x_scales, w1, gn, w2, offs, l
             nc.vector.quantize_mx(out=w2_words[:, cols].bitcast(FP8X4), scales=w2_scales[:, cols], in_=w2_bf(m).rearrange("p n j -> p (n j)"))
 
         cast_w2(0)
+        nc.gpsimd.tensor_scalar(out=w2_bf(1), in0=w2_second[:].rearrange("p j n -> p n j"), scalar1=1.0, scalar2=0.0, op0=ALU.mult, op1=ALU.add)
         gather(a, 0, la_t, on_vector=True)
         gather(b, 0, lb_t, on_vector=True)
         leave_psum(1)
@@ -182,7 +186,6 @@ def tile_picked_revcoup_none_p_kernel(tc, x_words, x_scales, w1, gn, w2, offs, l
         scatter(3)
         z_plane(1, 0, P)
         z_plane(2, 0, P)
-        cast_w2(1)
         z_plane(1, P, 2 * P)
         z_plane(2, P, 2 * P)
         cast_w2(2)

@@ -76,10 +76,11 @@ def tile_picked_revcoup_none_p_kernel(tc, x_words, x_scales, w1, gn, w2, offs, l
         w2_rows = w2.rearrange("(p j) c -> p j c", j=PACK)
         w2_first = keep.tile([P, PACK, P], F32, name="w2_first", tag="stage", align_bytes=64)
         nc.sync.dma_start(out=w2_first[:], in_=w2_rows[:, :, 0:P])
-        w2_second = keep.tile([P, PACK, P], F32, name="w2_second", tag="w1_raw0", align_bytes=64)
-        nc.sync.dma_start(out=w2_second[:], in_=w2_rows[:, :, P : 2 * P])
-        w2_rest = keep.tile([P, PACK, N // 2], F32, name="w2_rest", tag="w1_raw1", align_bytes=64)
-        nc.sync.dma_start(out=w2_rest[:], in_=w2_rows[:, :, N // 2 : N])
+        w2_second = keep.tile([P, 2, PACK, P], F32, name="w2_second", tag="w1_raw0", align_bytes=64)
+        for m in range(1, 3):
+            nc.sync.dma_start(out=w2_second[:, m - 1], in_=w2_rows[:, :, m * P : (m + 1) * P])
+        w2_rest = keep.tile([P, PACK, P], F32, name="w2_rest", tag="w1_raw1", align_bytes=64)
+        nc.sync.dma_start(out=w2_rest[:], in_=w2_rows[:, :, 3 * P : N])
         gn_t = keep.tile([P, PACK], F32, name="gn_t", tag="picked", align_bytes=64)
         nc.sync.dma_start(out=gn_t[:], in_=gn.rearrange("(p j) o -> p (j o)", j=PACK))
 
@@ -124,16 +125,16 @@ def tile_picked_revcoup_none_p_kernel(tc, x_words, x_scales, w1, gn, w2, offs, l
             nc.scalar.copy(out=h[t][:, lo:hi], in_=banks[3 + t][:, lo:hi])
 
         w2_bf_first = keep.tile([P, P, PACK], BF16, name="w2_bf_first", align_bytes=64)
-        w2_bf_second = keep.tile([P, P, PACK], BF16, name="w2_bf_second", tag="stage", align_bytes=64)
-        w2_bf_rest = keep.tile([P, N // 2, PACK], BF16, name="w2_bf_rest", tag="gated2", align_bytes=64)
+        w2_bf_second = keep.tile([P, 2, P, PACK], BF16, name="w2_bf_second", tag="stage", align_bytes=64)
+        w2_bf_rest = keep.tile([P, P, PACK], BF16, name="w2_bf_rest", tag="gated2", align_bytes=64)
 
         def w2_bf(m):
-            return (w2_bf_first, w2_bf_second)[m][:] if m < 2 else w2_bf_rest[:, (m - 2) * P : (m - 1) * P, :]
+            return (w2_bf_first[:], w2_bf_second[:, 0], w2_bf_second[:, 1], w2_bf_rest[:])[m]
 
         w2_scales = keep.tile([P, N], U8, name="w2_scales", align_bytes=64)
 
         def cast_w2(m):
-            raw = w2_first[:] if m == 0 else w2_rest[:, :, (m - 2) * P : (m - 1) * P]
+            raw = w2_first[:] if m == 0 else w2_rest[:]
             copy = nc.vector.tensor_copy if m == 0 else nc.scalar.copy
             copy(out=w2_bf(m).rearrange("p (g i) j -> p g j i", i=4), in_=raw.rearrange("p j (g i) -> p g j i", i=4))
 
@@ -144,7 +145,9 @@ def tile_picked_revcoup_none_p_kernel(tc, x_words, x_scales, w1, gn, w2, offs, l
             nc.vector.quantize_mx(out=w2_words[:, cols].bitcast(FP8X4), scales=w2_scales[:, cols], in_=w2_bf(m).rearrange("p n j -> p (n j)"))
 
         cast_w2(0)
-        nc.gpsimd.tensor_scalar(out=w2_bf(1), in0=w2_second[:].rearrange("p j n -> p n j"), scalar1=1.0, scalar2=0.0, op0=ALU.mult, op1=ALU.add)
+        for m in range(1, 3):
+            nc.gpsimd.tensor_scalar(out=w2_bf(m), in0=w2_second[:, m - 1].rearrange("p j n -> p n j"),
+                                    scalar1=1.0, scalar2=0.0, op0=ALU.mult, op1=ALU.add)
         gather(a, 0, la_t, on_vector=True)
         gather(b, 0, lb_t, on_vector=True)
         leave_psum(1)
@@ -188,7 +191,6 @@ def tile_picked_revcoup_none_p_kernel(tc, x_words, x_scales, w1, gn, w2, offs, l
         z_plane(2, 0, P)
         z_plane(1, P, 2 * P)
         z_plane(2, P, 2 * P)
-        cast_w2(2)
         cast_w2(3)
         z_plane(1, 2 * P, S)
         z_plane(2, 2 * P, S)

@@ -32,7 +32,7 @@ def tile_picked_revcoup_none_p_kernel(tc, x_words, x_scales, w1, gn, w2, offs, l
         offs_t = keep.tile([P, S // 16], U16, name="offs_t")
         la_t = keep.tile([P, V // 16], U16, name="la_t")
         lb_t = keep.tile([P, V // 16], U16, name="lb_t")
-        x_all = keep.tile([P, T], U32, name="x_all", align_bytes=64)
+        x_all = keep.tile([P, T], U32, name="x_all", tag="words", align_bytes=64)
         xs_all = keep.tile([P, T], U8, name="xs_all", tag="stage", align_bytes=64)
         w1_raw = [keep.tile([P, 2, H], F32, name=f"w1_raw{u}", tag=f"w1_raw{u}", align_bytes=64) for u in range(2)]
         banks = [psum.tile([P, 512], F32, name=f"bank{b}") for b in range(8)]
@@ -52,7 +52,7 @@ def tile_picked_revcoup_none_p_kernel(tc, x_words, x_scales, w1, gn, w2, offs, l
         nc.sync.dma_start(la_t[:], la)
         nc.sync.dma_start(lb_t[:], lb)
 
-        xs_picked = keep.tile([P, S], U8, name="xs_picked", tag="picked", align_bytes=64)
+        xs_picked = keep.tile([P, S], U8, name="xs_picked", align_bytes=64)
         nc.vector.tensor_copy(xs_picked[:], xs_all[:].indirect(offs_t[:]))
         x_scale = keep.tile([P, S], U8, name="x_scale", align_bytes=64)
         nc.vector.tensor_copy(out=x_scale[:].bitcast(I32), in_=xs_picked[:].bitcast(I32))
@@ -76,12 +76,12 @@ def tile_picked_revcoup_none_p_kernel(tc, x_words, x_scales, w1, gn, w2, offs, l
         w2_rows = w2.rearrange("(p j) c -> p j c", j=PACK)
         w2_first = keep.tile([P, PACK, P], F32, name="w2_first", tag="stage", align_bytes=64)
         nc.sync.dma_start(out=w2_first[:], in_=w2_rows[:, :, 0:P])
-        w2_second = keep.tile([P, 2, PACK, P], F32, name="w2_second", tag="w1_raw0", align_bytes=64)
+        w2_second = keep.tile([P, 2, PACK, P], F32, name="w2_second", tag="words", align_bytes=64)
         for m in range(1, 3):
             nc.sync.dma_start(out=w2_second[:, m - 1], in_=w2_rows[:, :, m * P : (m + 1) * P])
-        w2_rest = keep.tile([P, PACK, P], F32, name="w2_rest", tag="w1_raw1", align_bytes=64)
+        w2_rest = keep.tile([P, PACK, P], F32, name="w2_rest", tag="w1_raw0", align_bytes=64)
         nc.sync.dma_start(out=w2_rest[:], in_=w2_rows[:, :, 3 * P : N])
-        gn_t = keep.tile([P, PACK], F32, name="gn_t", tag="picked", align_bytes=64)
+        gn_t = keep.tile([P, PACK], F32, name="gn_t", tag="w1_raw1", align_bytes=64)
         nc.sync.dma_start(out=gn_t[:], in_=gn.rearrange("(p j) o -> p (j o)", j=PACK))
 
         w1_codes = [keep.tile([P, P], U32, name=f"w1_codes{t}", align_bytes=64) for t in range(PACK)]
@@ -94,12 +94,35 @@ def tile_picked_revcoup_none_p_kernel(tc, x_words, x_scales, w1, gn, w2, offs, l
             nc.tensor.matmul_mx(out=dst, lhsT=w1_codes[t][:].bitcast(FP8X4), lhsT_scale=w1_scales[t][:],
                                 rhs=x_codes[:, cols].bitcast(FP8X4), rhs_scale=x_scale[:, cols], start=True, stop=True)
 
+        w2_bf_first = keep.tile([P, P, PACK], BF16, name="w2_bf_first", align_bytes=64)
+        w2_bf_second = keep.tile([P, 2, P, PACK], BF16, name="w2_bf_second", tag="stage", align_bytes=64)
+
+        def w2_bf(m):
+            return w2_bf_rest[:] if m == LAST else (w2_bf_first[:], w2_bf_second[:, 0], w2_bf_second[:, 1])[m]
+
+        w2_scales = keep.tile([P, N], U8, name="w2_scales", align_bytes=64)
+
+        def cast_w2(m):
+            raw = w2_first[:] if m == 0 else w2_rest[:]
+            copy = nc.vector.tensor_copy if m == 0 else nc.scalar.copy
+            copy(out=w2_bf(m).rearrange("p (g i) j -> p g j i", i=4), in_=raw.rearrange("p j (g i) -> p g j i", i=4))
+
+
+        def quantize_w2(m):
+            cols = slice(m * P, (m + 1) * P)
+            nc.vector.quantize_mx(out=w2_words[:, cols].bitcast(FP8X4), scales=w2_scales[:, cols], in_=w2_bf(m).rearrange("p n j -> p (n j)"))
+
+        cast_w2(0)
+        for m in range(1, 3):
+            nc.gpsimd.tensor_scalar(out=w2_bf(m), in0=w2_second[:, m - 1].rearrange("p j n -> p n j"),
+                                    scalar1=1.0, scalar2=0.0, op0=ALU.mult, op1=ALU.add)
+
         a = [keep.tile([P, V], F32, name=f"a{t}", tag=f"a{t}", align_bytes=64) for t in range(PACK)]
         h = [keep.tile([P, S], F32, name=f"h{t}", tag=f"h{t}", align_bytes=64) for t in range(PACK)]
         for n in range(4):
             cols = slice(n * P, (n + 1) * P)
             first_product(0, banks[n][:, 0:P], cols)
-            if n < 2:
+            if n == 2:
                 nc.vector.tensor_copy(out=h[0][:, cols], in_=banks[n][:, 0:P])
             else:
                 nc.scalar.copy(out=h[0][:, cols], in_=banks[n][:, 0:P])
@@ -107,6 +130,10 @@ def tile_picked_revcoup_none_p_kernel(tc, x_words, x_scales, w1, gn, w2, offs, l
             first_product(t, banks[3 + t][:], slice(0, S))
         b = [keep.tile([P, V], F32, name=f"b{t}", tag=f"b{t}", align_bytes=64) for t in range(PACK)]
         gated = [keep.tile([P, V], F32, name=f"gated{t}", tag=f"gated{t}", align_bytes=64) for t in range(PACK)]
+
+        w2_bf_rest = keep.tile([P, P, PACK], BF16, name="w2_bf_rest", tag="gated2", align_bytes=64)
+
+        w2_words = keep.tile([P, N], U32, name="w2_words", tag="a3", align_bytes=64)
 
         def gather(dst, t, offsets, lo=0, hi=V, on_vector=False):
             window = h[t][:].indirect(offsets[:, lo // 16 : hi // 16])
@@ -124,30 +151,6 @@ def tile_picked_revcoup_none_p_kernel(tc, x_words, x_scales, w1, gn, w2, offs, l
         def leave_psum(t, lo=0, hi=S):
             nc.scalar.copy(out=h[t][:, lo:hi], in_=banks[3 + t][:, lo:hi])
 
-        w2_bf_first = keep.tile([P, P, PACK], BF16, name="w2_bf_first", align_bytes=64)
-        w2_bf_second = keep.tile([P, 2, P, PACK], BF16, name="w2_bf_second", tag="stage", align_bytes=64)
-        w2_bf_rest = keep.tile([P, P, PACK], BF16, name="w2_bf_rest", tag="gated2", align_bytes=64)
-
-        def w2_bf(m):
-            return (w2_bf_first[:], w2_bf_second[:, 0], w2_bf_second[:, 1], w2_bf_rest[:])[m]
-
-        w2_scales = keep.tile([P, N], U8, name="w2_scales", align_bytes=64)
-
-        def cast_w2(m):
-            raw = w2_first[:] if m == 0 else w2_rest[:]
-            copy = nc.vector.tensor_copy if m == 0 else nc.scalar.copy
-            copy(out=w2_bf(m).rearrange("p (g i) j -> p g j i", i=4), in_=raw.rearrange("p j (g i) -> p g j i", i=4))
-
-        w2_words = keep.tile([P, N], U32, name="w2_words", tag="a3", align_bytes=64)
-
-        def quantize_w2(m):
-            cols = slice(m * P, (m + 1) * P)
-            nc.vector.quantize_mx(out=w2_words[:, cols].bitcast(FP8X4), scales=w2_scales[:, cols], in_=w2_bf(m).rearrange("p n j -> p (n j)"))
-
-        cast_w2(0)
-        for m in range(1, 3):
-            nc.gpsimd.tensor_scalar(out=w2_bf(m), in0=w2_second[:, m - 1].rearrange("p j n -> p n j"),
-                                    scalar1=1.0, scalar2=0.0, op0=ALU.mult, op1=ALU.add)
         gather(a, 0, la_t, on_vector=True)
         gather(b, 0, lb_t, on_vector=True)
         leave_psum(1)
@@ -192,8 +195,8 @@ def tile_picked_revcoup_none_p_kernel(tc, x_words, x_scales, w1, gn, w2, offs, l
         z_plane(1, P, 2 * P)
         z_plane(2, P, 2 * P)
         cast_w2(3)
-        z_plane(1, 2 * P, S)
-        z_plane(2, 2 * P, S)
+        for t in range(1, PACK):
+            z_plane(t, 2 * P, S)
 
         z_bf, z_codes, z_scales = {0: z_first}, {}, {}
 
@@ -213,9 +216,8 @@ def tile_picked_revcoup_none_p_kernel(tc, x_words, x_scales, w1, gn, w2, offs, l
         z_plane(LAST, P, 2 * P, on_vector=True)
         quantize_z(0)
         interleave(1)
-        z_plane(LAST, 2 * P, S, on_vector=True)
-        quantize_z(1)
         quantize_w2(2)
+        quantize_z(1)
         quantize_w2(3)
         interleave(2)
         interleave(3)

@@ -94,35 +94,12 @@ def tile_picked_revcoup_none_p_kernel(tc, x_words, x_scales, w1, gn, w2, offs, l
             nc.tensor.matmul_mx(out=dst, lhsT=w1_codes[t][:].bitcast(FP8X4), lhsT_scale=w1_scales[t][:],
                                 rhs=x_codes[:, cols].bitcast(FP8X4), rhs_scale=x_scale[:, cols], start=True, stop=True)
 
-        w2_bf_first = keep.tile([P, P, PACK], BF16, name="w2_bf_first", align_bytes=64)
-        w2_bf_second = keep.tile([P, 2, P, PACK], BF16, name="w2_bf_second", tag="stage", align_bytes=64)
-
-        def w2_bf(m):
-            return w2_bf_rest[:] if m == LAST else (w2_bf_first[:], w2_bf_second[:, 0], w2_bf_second[:, 1])[m]
-
-        w2_scales = keep.tile([P, N], U8, name="w2_scales", align_bytes=64)
-
-        def cast_w2(m):
-            raw = w2_first[:] if m == 0 else w2_rest[:]
-            copy = nc.vector.tensor_copy if m == 0 else nc.scalar.copy
-            copy(out=w2_bf(m).rearrange("p (g i) j -> p g j i", i=4), in_=raw.rearrange("p j (g i) -> p g j i", i=4))
-
-
-        def quantize_w2(m):
-            cols = slice(m * P, (m + 1) * P)
-            nc.vector.quantize_mx(out=w2_words[:, cols].bitcast(FP8X4), scales=w2_scales[:, cols], in_=w2_bf(m).rearrange("p n j -> p (n j)"))
-
-        cast_w2(0)
-        for m in range(1, 3):
-            nc.gpsimd.tensor_scalar(out=w2_bf(m), in0=w2_second[:, m - 1].rearrange("p j n -> p n j"),
-                                    scalar1=1.0, scalar2=0.0, op0=ALU.mult, op1=ALU.add)
-
         a = [keep.tile([P, V], F32, name=f"a{t}", tag=f"a{t}", align_bytes=64) for t in range(PACK)]
         h = [keep.tile([P, S], F32, name=f"h{t}", tag=f"h{t}", align_bytes=64) for t in range(PACK)]
         for n in range(4):
             cols = slice(n * P, (n + 1) * P)
             first_product(0, banks[n][:, 0:P], cols)
-            if n == 2:
+            if n == 0:
                 nc.vector.tensor_copy(out=h[0][:, cols], in_=banks[n][:, 0:P])
             else:
                 nc.scalar.copy(out=h[0][:, cols], in_=banks[n][:, 0:P])
@@ -130,10 +107,6 @@ def tile_picked_revcoup_none_p_kernel(tc, x_words, x_scales, w1, gn, w2, offs, l
             first_product(t, banks[3 + t][:], slice(0, S))
         b = [keep.tile([P, V], F32, name=f"b{t}", tag=f"b{t}", align_bytes=64) for t in range(PACK)]
         gated = [keep.tile([P, V], F32, name=f"gated{t}", tag=f"gated{t}", align_bytes=64) for t in range(PACK)]
-
-        w2_bf_rest = keep.tile([P, P, PACK], BF16, name="w2_bf_rest", tag="gated2", align_bytes=64)
-
-        w2_words = keep.tile([P, N], U32, name="w2_words", tag="a3", align_bytes=64)
 
         def gather(dst, t, offsets, lo=0, hi=V, on_vector=False):
             window = h[t][:].indirect(offsets[:, lo // 16 : hi // 16])
@@ -151,6 +124,30 @@ def tile_picked_revcoup_none_p_kernel(tc, x_words, x_scales, w1, gn, w2, offs, l
         def leave_psum(t, lo=0, hi=S):
             nc.scalar.copy(out=h[t][:, lo:hi], in_=banks[3 + t][:, lo:hi])
 
+        w2_bf_first = keep.tile([P, P, PACK], BF16, name="w2_bf_first", align_bytes=64)
+        w2_bf_second = keep.tile([P, 2, P, PACK], BF16, name="w2_bf_second", tag="stage", align_bytes=64)
+        w2_bf_rest = keep.tile([P, P, PACK], BF16, name="w2_bf_rest", tag="gated2", align_bytes=64)
+
+        def w2_bf(m):
+            return (w2_bf_first[:], w2_bf_second[:, 0], w2_bf_second[:, 1], w2_bf_rest[:])[m]
+
+        w2_scales = keep.tile([P, N], U8, name="w2_scales", align_bytes=64)
+
+        def cast_w2(m):
+            raw = w2_first[:] if m == 0 else w2_rest[:]
+            copy = nc.vector.tensor_copy if m == 0 else nc.scalar.copy
+            copy(out=w2_bf(m).rearrange("p (g i) j -> p g j i", i=4), in_=raw.rearrange("p j (g i) -> p g j i", i=4))
+
+        w2_words = keep.tile([P, N], U32, name="w2_words", tag="a3", align_bytes=64)
+
+        def quantize_w2(m):
+            cols = slice(m * P, (m + 1) * P)
+            nc.vector.quantize_mx(out=w2_words[:, cols].bitcast(FP8X4), scales=w2_scales[:, cols], in_=w2_bf(m).rearrange("p n j -> p (n j)"))
+
+        cast_w2(0)
+        for m in range(1, 3):
+            nc.gpsimd.tensor_scalar(out=w2_bf(m), in0=w2_second[:, m - 1].rearrange("p j n -> p n j"),
+                                    scalar1=1.0, scalar2=0.0, op0=ALU.mult, op1=ALU.add)
         gather(a, 0, la_t, on_vector=True)
         gather(b, 0, lb_t, on_vector=True)
         leave_psum(1)

@@ -221,19 +221,31 @@ def tile_picked_revcoup_none_p_kernel(tc, x_words, x_scales, w1, gn, w2, offs, l
         quantize_z(2)
         quantize_z(3)
 
-        def multiply_and_store(m, ranges, bank, on_vector=False):
-            width = len(ranges) * P
+        def multiply(m, ranges, dst):
             for i, r in enumerate(ranges):
-                nc.tensor.matmul_mx(out=bank[:, i * P : (i + 1) * P], lhsT=w2_words[:, m * P : (m + 1) * P].bitcast(FP8X4),
+                nc.tensor.matmul_mx(out=dst[:, i * P : (i + 1) * P], lhsT=w2_words[:, m * P : (m + 1) * P].bitcast(FP8X4),
                                     lhsT_scale=w2_scales[:, m * P : (m + 1) * P],
                                     rhs=z_codes[r][:].bitcast(FP8X4), rhs_scale=z_scales[r][:], start=True, stop=True)
-            result = keep.tile([P, width], F32, name=f"result{m}{ranges[0]}", align_bytes=64)
-            if on_vector:
-                nc.vector.tensor_copy(out=result[:], in_=bank[:, 0:width])
-            else:
-                nc.scalar.copy(out=result[:], in_=bank[:, 0:width])
-            nc.sync.dma_start(out=out[m * P : (m + 1) * P, ranges[0] * P : ranges[0] * P + width], in_=result[:])
 
-        steps = [(m, (r,)) for r in range(2) for m in range(2)] + [(m, (0, 1)) for m in range(2, PACK)] + [(m, (2, 3)) for m in range(PACK)]
-        for n, (m, ranges) in enumerate(steps):
-            multiply_and_store(m, ranges, banks[n % 8], on_vector=ranges[0] == 2 and m % 2 == 0)
+        out_blocks = out.rearrange("(m p) c -> p m c", p=P)
+
+        def store(blocks, ranges, first_bank, on_vector=False):
+            width = len(ranges) * P
+            result = keep.tile([P, len(blocks), width], F32, name=f"result{blocks[0]}{ranges[0]}", align_bytes=64)
+            copy = nc.vector.tensor_copy if on_vector else nc.scalar.copy
+            if width == P:
+                for i, m in enumerate(blocks):
+                    multiply(m, ranges, banks[first_bank][:, i * P : (i + 1) * P])
+                copy(out=result[:].rearrange("p m c -> p (m c)"), in_=banks[first_bank][:, 0 : len(blocks) * P])
+            else:
+                for i, m in enumerate(blocks):
+                    multiply(m, ranges, banks[first_bank + i])
+                    copy(out=result[:, i, :], in_=banks[first_bank + i][:, 0:width])
+            nc.sync.dma_start(out=out_blocks[:, blocks[0] : blocks[-1] + 1, ranges[0] * P : ranges[0] * P + width], in_=result[:])
+
+        for r in range(2):
+            store((0, 1), (r,), r)
+        for m in range(2, PACK):
+            store((m,), (0, 1), m)
+        for m in range(PACK):
+            store((m,), (2, 3), PACK + m, on_vector=m % 2 == 0)

@@ -229,23 +229,25 @@ def tile_picked_revcoup_none_p_kernel(tc, x_words, x_scales, w1, gn, w2, offs, l
 
         out_blocks = out.rearrange("(m p) c -> p m c", p=P)
 
-        def store(blocks, ranges, first_bank, on_vector=False):
+        def store(blocks, ranges, first_bank, on_vector=()):
             width = len(ranges) * P
             result = keep.tile([P, len(blocks), width], F32, name=f"result{blocks[0]}{ranges[0]}", align_bytes=64)
-            copy = nc.vector.tensor_copy if on_vector else nc.scalar.copy
             if width == P:
                 for i, m in enumerate(blocks):
                     multiply(m, ranges, banks[first_bank][:, i * P : (i + 1) * P])
-                copy(out=result[:].rearrange("p m c -> p (m c)"), in_=banks[first_bank][:, 0 : len(blocks) * P])
+                nc.scalar.copy(out=result[:].rearrange("p m c -> p (m c)"), in_=banks[first_bank][:, 0 : len(blocks) * P])
             else:
                 for i, m in enumerate(blocks):
                     multiply(m, ranges, banks[first_bank + i])
+                    copy = nc.vector.tensor_copy if m in on_vector else nc.scalar.copy
                     copy(out=result[:, i, :], in_=banks[first_bank + i][:, 0:width])
             nc.sync.dma_start(out=out_blocks[:, blocks[0] : blocks[-1] + 1, ranges[0] * P : ranges[0] * P + width], in_=result[:])
 
-        for r in range(2):
-            store((0, 1), (r,), r)
+        store((0, 1), (0,), 0)
+        for m in range(2):
+            store((m,), (1,), m + 1)
         for m in range(2, PACK):
-            store((m,), (0, 1), m)
-        for m in range(PACK):
-            store((m,), (2, 3), PACK + m, on_vector=m % 2 == 0)
+            store((m,), (0, 1), m + 1)
+        store((0,), (2, 3), 5, on_vector=(0,))
+        store((1, 2), (2, 3), 6, on_vector=(2,))
+        store((3,), (2, 3), 0)

@@ -105,72 +105,64 @@ def tile_picked_revcoup_none_p_kernel(tc, x_words, x_scales, w1, gn, w2, offs, l
                 nc.scalar.copy(out=h[0][:, cols], in_=banks[n][:, 0:P])
         for t in range(1, PACK):
             first_product(t, banks[3 + t][:], slice(0, S))
+        ON_SCALAR = (0, 1, 2)
         b = [keep.tile([P, V], F32, name=f"b{t}", tag=f"b{t}", align_bytes=64) for t in range(PACK)]
         gated = [keep.tile([P, V], F32, name=f"gated{t}", tag=f"gated{t}", align_bytes=64) for t in range(PACK)]
 
-        def gather(dst, t, offsets, lo=0, hi=V, on_vector=False):
-            window = h[t][:].indirect(offsets[:, lo // 16 : hi // 16])
+        total = keep.tile([P, V], F32, name="total", align_bytes=64)
+
+        def gather(dst, t, offsets, on_vector=False):
+            window = h[t][:].indirect(offsets[:])
             if on_vector:
-                nc.vector.tensor_copy(dst[t][:, lo:hi], window)
+                nc.vector.tensor_copy(dst[t][:], window)
             else:
-                nc.scalar.activation(out=dst[t][:, lo:hi], in_=window, func=ACT.Copy)
+                nc.scalar.activation(out=dst[t][:], in_=window, func=ACT.Copy)
 
         def silu(t):
             nc.scalar.activation(out=gated[t][:], in_=a[t][:], func=ACT.Silu)
 
-        def scatter(t):
-            nc.vector.tensor_tensor(h[t][:].indirect(lb_t[:]), b[t][:], gated[t][:], ALU.add)
+        def gather_and_add(t):
+            nc.vector.tensor_tensor(b[t][:], h[t][:].indirect(lb_t[:]), gated[t][:], ALU.add)
 
-        def leave_psum(t, lo=0, hi=S):
-            nc.scalar.copy(out=h[t][:, lo:hi], in_=banks[3 + t][:, lo:hi])
+        def add(t):
+            nc.vector.tensor_tensor(total[:], b[t][:], gated[t][:], ALU.add)
+
+        def scatter(t):
+            if t in ON_SCALAR:
+                nc.scalar.activation(out=h[t][:].indirect(lb_t[:]), in_=(total if t == 0 else b[t])[:], func=ACT.Copy)
+            else:
+                nc.vector.tensor_tensor(h[t][:].indirect(lb_t[:]), b[t][:], gated[t][:], ALU.add)
+
+        def leave_psum(t):
+            nc.scalar.copy(out=h[t][:], in_=banks[3 + t][:])
 
         w2_bf_first = keep.tile([P, P, PACK], BF16, name="w2_bf_first", align_bytes=64)
         w2_bf_second = keep.tile([P, 2, P, PACK], BF16, name="w2_bf_second", tag="stage", align_bytes=64)
         w2_bf_rest = keep.tile([P, P, PACK], BF16, name="w2_bf_rest", tag="gated2", align_bytes=64)
-
-        def w2_bf(m):
-            return (w2_bf_first[:], w2_bf_second[:, 0], w2_bf_second[:, 1], w2_bf_rest[:])[m]
-
-        w2_scales = keep.tile([P, N], U8, name="w2_scales", align_bytes=64)
+        w2_codes = {0: keep.tile([P, P], U32, name="w2_codes0", tag="b3", align_bytes=64),
+                    1: keep.tile([P, 2 * P], U32, name="w2_codes1", tag="gated3", align_bytes=64),
+                    3: keep.tile([P, P], U32, name="w2_codes3", align_bytes=64)}
+        w2_scales = {m: keep.tile([P, w * P], U8, name=f"w2_scales{m}", align_bytes=64) for m, w in ((0, 1), (1, 2), (3, 1))}
 
         def cast_w2(m):
-            raw = w2_first[:] if m == 0 else w2_rest[:]
-            copy = nc.vector.tensor_copy if m == 0 else nc.scalar.copy
-            copy(out=w2_bf(m).rearrange("p (g i) j -> p g j i", i=4), in_=raw.rearrange("p j (g i) -> p g j i", i=4))
-
-        w2_words = keep.tile([P, N], U32, name="w2_words", tag="a3", align_bytes=64)
+            raw, dst = (w2_first, w2_bf_first) if m == 0 else (w2_rest, w2_bf_rest)
+            nc.vector.tensor_copy(out=dst[:].rearrange("p (g i) j -> p g j i", i=4), in_=raw[:].rearrange("p j (g i) -> p g j i", i=4))
 
         def quantize_w2(m):
-            cols = slice(m * P, (m + 1) * P)
-            nc.vector.quantize_mx(out=w2_words[:, cols].bitcast(FP8X4), scales=w2_scales[:, cols], in_=w2_bf(m).rearrange("p n j -> p (n j)"))
+            src = {0: w2_bf_first[:].rearrange("p n j -> p (n j)"), 1: w2_bf_second[:].rearrange("p m n j -> p (m n j)"),
+                   3: w2_bf_rest[:].rearrange("p n j -> p (n j)")}[m]
+            nc.vector.quantize_mx(out=w2_codes[m][:].bitcast(FP8X4), scales=w2_scales[m][:], in_=src)
 
-        cast_w2(0)
-        for m in range(1, 3):
-            nc.gpsimd.tensor_scalar(out=w2_bf(m), in0=w2_second[:, m - 1].rearrange("p j n -> p n j"),
-                                    scalar1=1.0, scalar2=0.0, op0=ALU.mult, op1=ALU.add)
-        gather(a, 0, la_t, on_vector=True)
-        gather(b, 0, lb_t, on_vector=True)
-        leave_psum(1)
-        leave_psum(2, 0, S // 2)
-        silu(0)
-        gather(a, 1, la_t, on_vector=True)
-        scatter(0)
-        leave_psum(2, S // 2, S)
-        gather(b, 1, lb_t)
-        silu(1)
-        scatter(1)
-        gather(a, 2, la_t)
-        gather(b, 2, lb_t)
-        leave_psum(3)
-        silu(2)
-        scatter(2)
+        def w2_operand(m):
+            key, lo = (1, (m - 1) * P) if m in (1, 2) else (m, 0)
+            return w2_codes[key][:, lo : lo + P].bitcast(FP8X4), w2_scales[key][:, lo : lo + P]
 
-        z_early = keep.tile([P, S * PACK], BF16, name="z_early", tag="a2", align_bytes=64)
+        z_early = keep.tile([P, S * PACK], BF16, name="z_early", tag="a3", align_bytes=64)
         z_first = z_early[:, 0 : P * PACK]
         z_pairs = z_early[:, P * PACK :].rearrange("p (u n e) -> p u n e", u=2, e=2)
         pair_words = z_early[:, P * PACK :].bitcast(I32).rearrange("p (u n) -> p n u", u=2)
 
-        def z_plane(t, lo, hi, on_vector=False):
+        def z_plane(t, lo, hi, on_vector=True):
             if lo == 0:
                 dst = z_first.rearrange("p (n j) -> p n j", j=PACK)[:, :, SLOT[t]]
             else:
@@ -180,51 +172,23 @@ def tile_picked_revcoup_none_p_kernel(tc, x_words, x_scales, w1, gn, w2, offs, l
             else:
                 nc.scalar.activation(out=dst, in_=h[t][:, lo:hi], func=ACT.Copy, scale=gn_t[:, SLOT[t] : SLOT[t] + 1])
 
-        z_plane(0, 2 * P, S, on_vector=True)
-        z_plane(0, P, 2 * P)
-        gather(a, 3, la_t)
-        gather(b, 3, lb_t)
-        z_plane(0, 0, P)
-        silu(3)
-        scatter(3)
-        z_plane(1, 0, P)
-        z_plane(2, 0, P)
-        z_plane(1, P, 2 * P)
-        z_plane(2, P, 2 * P)
-        cast_w2(3)
-        for t in range(1, PACK):
-            z_plane(t, 2 * P, S)
-
         z_bf, z_codes, z_scales = {0: z_first}, {}, {}
 
-        def interleave(r):
-            tile = keep.tile([P, P * PACK], BF16, name=f"z_bf{r}", align_bytes=64)
-            z_bf[r] = tile[:]
-            nc.vector.tensor_copy(out=tile[:].bitcast(I32).rearrange("p (n u) -> p n u", u=2), in_=pair_words[:, (r - 1) * P : r * P, :])
+        def interleave(r, count=1):
+            tile = keep.tile([P, count * P * PACK], BF16, name=f"z_bf{r}", align_bytes=64)
+            for i in range(count):
+                z_bf[r + i] = tile[:, i * P * PACK : (i + 1) * P * PACK]
+            nc.vector.tensor_copy(out=tile[:].bitcast(I32).rearrange("p (n u) -> p n u", u=2), in_=pair_words[:, (r - 1) * P : (r - 1 + count) * P, :])
 
         def quantize_z(r):
             z_codes[r] = keep.tile([P, P], U32, name=f"z_codes{r}", align_bytes=64)
             z_scales[r] = keep.tile([P, P], U8, name=f"z_scales{r}", align_bytes=64)
             nc.vector.quantize_mx(out=z_codes[r][:].bitcast(FP8X4), scales=z_scales[r][:], in_=z_bf[r])
 
-        quantize_w2(0)
-        z_plane(LAST, 0, P, on_vector=True)
-        quantize_w2(1)
-        z_plane(LAST, P, 2 * P, on_vector=True)
-        quantize_z(0)
-        interleave(1)
-        quantize_w2(2)
-        quantize_z(1)
-        quantize_w2(3)
-        interleave(2)
-        interleave(3)
-        quantize_z(2)
-        quantize_z(3)
-
         def multiply(m, ranges, dst):
+            codes, scales = w2_operand(m)
             for i, r in enumerate(ranges):
-                nc.tensor.matmul_mx(out=dst[:, i * P : (i + 1) * P], lhsT=w2_words[:, m * P : (m + 1) * P].bitcast(FP8X4),
-                                    lhsT_scale=w2_scales[:, m * P : (m + 1) * P],
+                nc.tensor.matmul_mx(out=dst[:, i * P : (i + 1) * P], lhsT=codes, lhsT_scale=scales,
                                     rhs=z_codes[r][:].bitcast(FP8X4), rhs_scale=z_scales[r][:], start=True, stop=True)
 
         out_blocks = out.rearrange("(m p) c -> p m c", p=P)
@@ -243,11 +207,59 @@ def tile_picked_revcoup_none_p_kernel(tc, x_words, x_scales, w1, gn, w2, offs, l
                     copy(out=result[:, i, :], in_=banks[first_bank + i][:, 0:width])
             nc.sync.dma_start(out=out_blocks[:, blocks[0] : blocks[-1] + 1, ranges[0] * P : ranges[0] * P + width], in_=result[:])
 
-        store((0, 1), (0,), 0)
+        cast_w2(0)
         for m in range(2):
-            store((m,), (1,), m + 1)
-        for m in range(2, PACK):
-            store((m,), (0, 1), m + 1)
+            nc.gpsimd.tensor_scalar(out=w2_bf_second[:, m], in0=w2_second[:, m].rearrange("p j n -> p n j"),
+                                    scalar1=1.0, scalar2=0.0, op0=ALU.mult, op1=ALU.add)
+        gather(a, 0, la_t, on_vector=True)
+        gather(b, 0, lb_t, on_vector=True)
+        leave_psum(1)
+        silu(0)
+        leave_psum(2)
+        leave_psum(3)
+        gather(a, 1, la_t, on_vector=True)
+        add(0)
+        silu(1)
+        gather(a, 2, la_t, on_vector=True)
+        gather_and_add(1)
+        gather(a, 3, la_t, on_vector=True)
+        gather(b, 3, lb_t, on_vector=True)
+        scatter(0)
+        silu(2)
+        silu(3)
+        gather_and_add(2)
+        scatter(3)
+        scatter(1)
+        scatter(2)
+        for lo, hi in ((P, 2 * P), (2 * P, S)):
+            for t in (1, 2):
+                z_plane(t, lo, hi, on_vector=False)
+
+        z_plane(0, 0, P)
+        z_plane(1, 0, P)
+        z_plane(3, 0, P)
+        cast_w2(3)
+        quantize_w2(0)
+        z_plane(2, 0, P)
+        z_plane(0, P, 2 * P)
+        z_plane(3, P, 2 * P)
+        quantize_z(0)
+        interleave(1)
+        quantize_w2(1)
+        quantize_z(1)
+        z_plane(0, 2 * P, S)
+        z_plane(3, 2 * P, S)
+        quantize_w2(3)
+        interleave(2)
+        interleave(3)
+        quantize_z(2)
+        quantize_z(3)
+
+        store((0,), (0,), 0)
+        store((1, 2), (0,), 1)
+        store((0, 1), (1,), 2)
+        store((2,), (1,), 3)
+        store((3,), (0, 1), 4)
         store((0,), (2, 3), 5, on_vector=(0,))
         store((1, 2), (2, 3), 6, on_vector=(2,))
         store((3,), (2, 3), 0)

@@ -75,12 +75,12 @@ def tile_picked_revcoup_none_p_kernel(tc, x_words, x_scales, w1, gn, w2, offs, l
 
         w2_rows = w2.rearrange("(p j) c -> p j c", j=PACK)
         w2_first = keep.tile([P, PACK, P], F32, name="w2_first", tag="stage", align_bytes=64)
-        nc.sync.dma_start(out=w2_first[:], in_=w2_rows[:, :, 0:P])
+        nc.sync.dma_start(out=w2_first[:], in_=w2_rows[:, :, 3 * P : N])
         w2_second = keep.tile([P, 2, PACK, P], F32, name="w2_second", tag="words", align_bytes=64)
-        for m in range(1, 3):
-            nc.sync.dma_start(out=w2_second[:, m - 1], in_=w2_rows[:, :, m * P : (m + 1) * P])
+        for m in range(2):
+            nc.sync.dma_start(out=w2_second[:, m], in_=w2_rows[:, :, m * P : (m + 1) * P])
         w2_rest = keep.tile([P, PACK, P], F32, name="w2_rest", tag="w1_raw0", align_bytes=64)
-        nc.sync.dma_start(out=w2_rest[:], in_=w2_rows[:, :, 3 * P : N])
+        nc.sync.dma_start(out=w2_rest[:], in_=w2_rows[:, :, 2 * P : 3 * P])
         gn_t = keep.tile([P, PACK], F32, name="gn_t", tag="w1_raw1", align_bytes=64)
         nc.sync.dma_start(out=gn_t[:], in_=gn.rearrange("(p j) o -> p (j o)", j=PACK))
 
@@ -111,21 +111,18 @@ def tile_picked_revcoup_none_p_kernel(tc, x_words, x_scales, w1, gn, w2, offs, l
 
         total = keep.tile([P, V], F32, name="total", align_bytes=64)
 
-        def gather(dst, t, offsets, on_vector=False):
-            window = h[t][:].indirect(offsets[:])
+        def gather(dst, t, offsets, lo=0, hi=V, on_vector=False):
+            window = h[t][:].indirect(offsets[:, lo // 16 : hi // 16])
             if on_vector:
-                nc.vector.tensor_copy(dst[t][:], window)
+                nc.vector.tensor_copy(dst[t][:, lo:hi], window)
             else:
-                nc.scalar.activation(out=dst[t][:], in_=window, func=ACT.Copy)
+                nc.scalar.activation(out=dst[t][:, lo:hi], in_=window, func=ACT.Copy)
 
         def silu(t):
             nc.scalar.activation(out=gated[t][:], in_=a[t][:], func=ACT.Silu)
 
         def gather_and_add(t):
             nc.vector.tensor_tensor(b[t][:], h[t][:].indirect(lb_t[:]), gated[t][:], ALU.add)
-
-        def add(t):
-            nc.vector.tensor_tensor(total[:], b[t][:], gated[t][:], ALU.add)
 
         def scatter(t):
             if t in ON_SCALAR:
@@ -137,24 +134,21 @@ def tile_picked_revcoup_none_p_kernel(tc, x_words, x_scales, w1, gn, w2, offs, l
             nc.scalar.copy(out=h[t][:], in_=banks[3 + t][:])
 
         w2_bf_first = keep.tile([P, P, PACK], BF16, name="w2_bf_first", align_bytes=64)
-        w2_bf_second = keep.tile([P, 2, P, PACK], BF16, name="w2_bf_second", tag="stage", align_bytes=64)
-        w2_bf_rest = keep.tile([P, P, PACK], BF16, name="w2_bf_rest", tag="gated2", align_bytes=64)
-        w2_codes = {0: keep.tile([P, P], U32, name="w2_codes0", tag="b3", align_bytes=64),
-                    1: keep.tile([P, 2 * P], U32, name="w2_codes1", tag="gated3", align_bytes=64),
-                    3: keep.tile([P, P], U32, name="w2_codes3", align_bytes=64)}
-        w2_scales = {m: keep.tile([P, w * P], U8, name=f"w2_scales{m}", align_bytes=64) for m, w in ((0, 1), (1, 2), (3, 1))}
+        w2_bf_second = keep.tile([P, 3, P, PACK], BF16, name="w2_bf_second", tag="stage", align_bytes=64)
+        w2_codes = [keep.tile([P, P], U32, name="w2_codes0", tag="b3", align_bytes=64),
+                    keep.tile([P, 3 * P], U32, name="w2_codes1", tag="gated3", align_bytes=64)]
+        w2_scales = [keep.tile([P, w * P], U8, name=f"w2_scales{w}", align_bytes=64) for w in (1, 3)]
 
-        def cast_w2(m):
-            raw, dst = (w2_first, w2_bf_first) if m == 0 else (w2_rest, w2_bf_rest)
-            nc.vector.tensor_copy(out=dst[:].rearrange("p (g i) j -> p g j i", i=4), in_=raw[:].rearrange("p j (g i) -> p g j i", i=4))
-
-        def quantize_w2(m):
-            src = {0: w2_bf_first[:].rearrange("p n j -> p (n j)"), 1: w2_bf_second[:].rearrange("p m n j -> p (m n j)"),
-                   3: w2_bf_rest[:].rearrange("p n j -> p (n j)")}[m]
-            nc.vector.quantize_mx(out=w2_codes[m][:].bitcast(FP8X4), scales=w2_scales[m][:], in_=src)
+        def quantize_w2(lo, hi):
+            if lo == 3:
+                nc.vector.quantize_mx(out=w2_codes[0][:].bitcast(FP8X4), scales=w2_scales[0][:], in_=w2_bf_first[:].rearrange("p n j -> p (n j)"))
+            else:
+                cols = slice(lo * P, hi * P)
+                nc.vector.quantize_mx(out=w2_codes[1][:, cols].bitcast(FP8X4), scales=w2_scales[1][:, cols],
+                                      in_=w2_bf_second[:, lo:hi].rearrange("p m n j -> p (m n j)"))
 
         def w2_operand(m):
-            key, lo = (1, (m - 1) * P) if m in (1, 2) else (m, 0)
+            key, lo = (0, 0) if m == 3 else (1, m * P)
             return w2_codes[key][:, lo : lo + P].bitcast(FP8X4), w2_scales[key][:, lo : lo + P]
 
         z_early = keep.tile([P, S * PACK], BF16, name="z_early", tag="a3", align_bytes=64)
@@ -207,27 +201,33 @@ def tile_picked_revcoup_none_p_kernel(tc, x_words, x_scales, w1, gn, w2, offs, l
                     copy(out=result[:, i, :], in_=banks[first_bank + i][:, 0:width])
             nc.sync.dma_start(out=out_blocks[:, blocks[0] : blocks[-1] + 1, ranges[0] * P : ranges[0] * P + width], in_=result[:])
 
-        cast_w2(0)
-        for m in range(2):
-            nc.gpsimd.tensor_scalar(out=w2_bf_second[:, m], in0=w2_second[:, m].rearrange("p j n -> p n j"),
+        nc.vector.tensor_copy(out=w2_bf_first[:].rearrange("p (g i) j -> p g j i", i=4), in_=w2_first[:].rearrange("p j (g i) -> p g j i", i=4))
+
+        def round_w2(m):
+            raw = w2_rest[:] if m == 2 else w2_second[:, m]
+            nc.gpsimd.tensor_scalar(out=w2_bf_second[:, m], in0=raw.rearrange("p j n -> p n j"),
                                     scalar1=1.0, scalar2=0.0, op0=ALU.mult, op1=ALU.add)
+
+        round_w2(0)
+        round_w2(1)
         gather(a, 0, la_t, on_vector=True)
         gather(b, 0, lb_t, on_vector=True)
         leave_psum(1)
         silu(0)
+        nc.gpsimd.tensor_tensor(total[:], b[0][:], gated[0][:], ALU.add)
+        round_w2(2)
         leave_psum(2)
         leave_psum(3)
         gather(a, 1, la_t, on_vector=True)
-        add(0)
-        silu(1)
         gather(a, 2, la_t, on_vector=True)
-        gather_and_add(1)
         gather(a, 3, la_t, on_vector=True)
         gather(b, 3, lb_t, on_vector=True)
-        scatter(0)
+        silu(1)
         silu(2)
-        silu(3)
+        gather_and_add(1)
         gather_and_add(2)
+        scatter(0)
+        silu(3)
         scatter(3)
         scatter(1)
         scatter(2)
@@ -238,18 +238,17 @@ def tile_picked_revcoup_none_p_kernel(tc, x_words, x_scales, w1, gn, w2, offs, l
         z_plane(0, 0, P)
         z_plane(1, 0, P)
         z_plane(3, 0, P)
-        cast_w2(3)
-        quantize_w2(0)
+        quantize_w2(0, 1)
         z_plane(2, 0, P)
         z_plane(0, P, 2 * P)
         z_plane(3, P, 2 * P)
         quantize_z(0)
         interleave(1)
-        quantize_w2(1)
+        quantize_w2(1, 3)
         quantize_z(1)
         z_plane(0, 2 * P, S)
         z_plane(3, 2 * P, S)
-        quantize_w2(3)
+        quantize_w2(3, 4)
         interleave(2)
         interleave(3)
         quantize_z(2)

@@ -32,9 +32,9 @@ def tile_picked_revcoup_none_p_kernel(tc, x_words, x_scales, w1, gn, w2, offs, l
         offs_t = keep.tile([P, S // 16], U16, name="offs_t")
         la_t = keep.tile([P, V // 16], U16, name="la_t")
         lb_t = keep.tile([P, V // 16], U16, name="lb_t")
-        x_all = keep.tile([P, T], U32, name="x_all", tag="words", align_bytes=64)
-        xs_all = keep.tile([P, T], U8, name="xs_all", tag="stage", align_bytes=64)
-        w1_raw = [keep.tile([P, 2, H], F32, name=f"w1_raw{u}", tag=f"w1_raw{u}", align_bytes=64) for u in range(2)]
+        x_all = keep.tile([P, T], U32, name="x_all", tag="words", align_bytes=256)
+        xs_all = keep.tile([P, T], U8, name="xs_all", tag="stage", align_bytes=256)
+        w1_raw = [keep.tile([P, 2, H], F32, name=f"w1_raw{u}", tag=f"w1_raw{u}", align_bytes=256) for u in range(2)]
         banks = [psum.tile([P, 512], F32, name=f"bank{b}") for b in range(8)]
 
         nc.vector.memset(xs_all[:].bitcast(I32), 0)
@@ -74,14 +74,14 @@ def tile_picked_revcoup_none_p_kernel(tc, x_words, x_scales, w1, gn, w2, offs, l
             nc.scalar.copy(out=w1_bf[1][:, :, :, pair].rearrange("p e m j -> p m e j"), in_=by_byte[:, 1])
 
         w2_rows = w2.rearrange("(p j) c -> p j c", j=PACK)
-        w2_first = keep.tile([P, PACK, P], F32, name="w2_first", tag="stage", align_bytes=64)
+        w2_first = keep.tile([P, PACK, P], F32, name="w2_first", tag="stage", align_bytes=256)
         nc.sync.dma_start(out=w2_first[:], in_=w2_rows[:, :, 3 * P : N])
-        w2_second = keep.tile([P, 2, PACK, P], F32, name="w2_second", tag="words", align_bytes=64)
+        w2_second = keep.tile([P, 2, PACK, P], F32, name="w2_second", tag="words", align_bytes=256)
         for m in range(2):
             nc.sync.dma_start(out=w2_second[:, m], in_=w2_rows[:, :, m * P : (m + 1) * P])
-        w2_rest = keep.tile([P, PACK, P], F32, name="w2_rest", tag="w1_raw0", align_bytes=64)
+        w2_rest = keep.tile([P, PACK, P], F32, name="w2_rest", tag="w1_raw0", align_bytes=256)
         nc.sync.dma_start(out=w2_rest[:], in_=w2_rows[:, :, 2 * P : 3 * P])
-        gn_t = keep.tile([P, PACK], F32, name="gn_t", tag="w1_raw1", align_bytes=64)
+        gn_t = keep.tile([P, PACK], F32, name="gn_t", tag="w1_raw1", align_bytes=256)
         nc.sync.dma_start(out=gn_t[:], in_=gn.rearrange("(p j) o -> p (j o)", j=PACK))
 
         w1_codes = [keep.tile([P, P], U32, name=f"w1_codes{t}", align_bytes=64) for t in range(PACK)]
@@ -134,7 +134,7 @@ def tile_picked_revcoup_none_p_kernel(tc, x_words, x_scales, w1, gn, w2, offs, l
             nc.scalar.copy(out=h[t][:], in_=banks[3 + t][:])
 
         w2_bf_first = keep.tile([P, P, PACK], BF16, name="w2_bf_first", align_bytes=64)
-        w2_bf_second = keep.tile([P, 3, P, PACK], BF16, name="w2_bf_second", tag="stage", align_bytes=64)
+        w2_bf_second = keep.tile([P, 3, P, PACK], BF16, name="w2_bf_second", tag="stage", align_bytes=256)
         w2_codes = [keep.tile([P, P], U32, name="w2_codes0", tag="b3", align_bytes=64),
                     keep.tile([P, 3 * P], U32, name="w2_codes1", tag="gated3", align_bytes=64)]
         w2_scales = [keep.tile([P, w * P], U8, name=f"w2_scales{w}", align_bytes=64) for w in (1, 3)]
@@ -189,7 +189,7 @@ def tile_picked_revcoup_none_p_kernel(tc, x_words, x_scales, w1, gn, w2, offs, l
 
         def store(blocks, ranges, first_bank, on_vector=()):
             width = len(ranges) * P
-            result = keep.tile([P, len(blocks), width], F32, name=f"result{blocks[0]}{ranges[0]}", align_bytes=64)
+            result = keep.tile([P, len(blocks), width], F32, name=f"result{blocks[0]}{ranges[0]}", align_bytes=256)
             if width == P:
                 for i, m in enumerate(blocks):
                     multiply(m, ranges, banks[first_bank][:, i * P : (i + 1) * P])

@@ -21,6 +21,7 @@ LINE = 8
 LAST = PACK - 1
 SLOT = (0, 2, 3, 1)
 SPLIT = 96
+AHEAD = 3 * T // 8
 
 
 def tile_picked_revcoup_none_p_kernel(tc, x_words, x_scales, w1, gn, w2, offs, la, lb, out):
@@ -43,10 +44,10 @@ def tile_picked_revcoup_none_p_kernel(tc, x_words, x_scales, w1, gn, w2, offs, l
         nc.scalar.activation(out=warm[:, 1:2], in_=warm[:, 0:1], func=ACT.Silu)
         w1_rows = w1.rearrange("(p j) c -> p j c", j=PACK)
         x_rows = x_words[0].rearrange("p n t -> p (n t)").bitcast(I32)
-        nc.sync.dma_start(out=x_all[:, 0 : T // 2].bitcast(I32), in_=x_rows[:, 0 : T // 2])
+        nc.sync.dma_start(out=x_all[:, 0:AHEAD].bitcast(I32), in_=x_rows[:, 0:AHEAD])
         nc.sync.dma_start(out=xs_all[0:P:LINE, :].bitcast(I32), in_=x_scales[0].bitcast(I32))
         nc.sync.dma_start(offs_t[:], offs)
-        nc.sync.dma_start(out=x_all[:, T // 2 : T].bitcast(I32), in_=x_rows[:, T // 2 : T])
+        nc.sync.dma_start(out=x_all[:, AHEAD:T].bitcast(I32), in_=x_rows[:, AHEAD:T])
         for u in range(2):
             nc.sync.dma_start(out=w1_raw[u][:], in_=w1_rows[:, 2 * u : 2 * u + 2, :])
         nc.sync.dma_start(la_t[:], la)

@@ -45,8 +45,8 @@ def tile_picked_revcoup_none_p_kernel(tc, x_words, x_scales, w1, gn, w2, offs, l
         w1_rows = w1.rearrange("(p j) c -> p j c", j=PACK)
         x_rows = x_words[0].rearrange("p n t -> p (n t)").bitcast(I32)
         nc.sync.dma_start(out=x_all[:, 0:AHEAD].bitcast(I32), in_=x_rows[:, 0:AHEAD])
-        nc.sync.dma_start(out=xs_all[0:P:LINE, :].bitcast(I32), in_=x_scales[0].bitcast(I32))
         nc.sync.dma_start(offs_t[:], offs)
+        nc.sync.dma_start(out=xs_all[0:P:LINE, :].bitcast(I32), in_=x_scales[0].bitcast(I32))
         nc.sync.dma_start(out=x_all[:, AHEAD:T].bitcast(I32), in_=x_rows[:, AHEAD:T])
         for u in range(2):
             nc.sync.dma_start(out=w1_raw[u][:], in_=w1_rows[:, 2 * u : 2 * u + 2, :])

from contextlib import ExitStack

import concourse.mybir as mybir

K, T, S, V, N, H = 512, 2048, 512, 256, 512, 512
FLOPS = 2 * K * H * S + 2 * H * N * S

F32 = mybir.dt.float32
BF16 = mybir.dt.bfloat16
I32 = mybir.dt.int32
U32 = mybir.dt.uint32
U16 = mybir.dt.uint16
U8 = mybir.dt.uint8
FP8X4 = mybir.dt.float8_e4m3fn_x4
ACT = mybir.ActivationFunctionType
ALU = mybir.AluOpType

P = 128
PACK = 4
LINE = 8
LAST = PACK - 1
SLOT = (0, 2, 3, 1)
SPLIT = 96
AHEAD = 3 * T // 8


def tile_picked_revcoup_none_p_kernel(tc, x_words, x_scales, w1, gn, w2, offs, la, lb, out):
    nc = tc.nc
    with ExitStack() as ctx:
        keep = ctx.enter_context(tc.tile_pool(name="keep", bufs=1))
        psum = ctx.enter_context(tc.psum_pool(name="psum", bufs=1))

        offs_t = keep.tile([P, S // 16], U16, name="offs_t")
        la_t = keep.tile([P, V // 16], U16, name="la_t")
        lb_t = keep.tile([P, V // 16], U16, name="lb_t")
        x_all = keep.tile([P, T], U32, name="x_all", tag="words", align_bytes=256)
        xs_all = keep.tile([P, T], U8, name="xs_all", tag="stage", align_bytes=256)
        w1_raw = [keep.tile([P, 2, H], F32, name=f"w1_raw{u}", tag=f"w1_raw{u}", align_bytes=256) for u in range(2)]
        banks = [psum.tile([P, 512], F32, name=f"bank{b}") for b in range(8)]

        nc.vector.memset(xs_all[:].bitcast(I32), 0)
        warm = keep.tile([P, 2], F32, name="warm")
        nc.vector.memset(warm[:, 0:1], 0.0)
        nc.scalar.activation(out=warm[:, 1:2], in_=warm[:, 0:1], func=ACT.Silu)
        w1_rows = w1.rearrange("(p j) c -> p j c", j=PACK)
        x_rows = x_words[0].rearrange("p n t -> p (n t)").bitcast(I32)
        nc.sync.dma_start(out=x_all[:, 0:AHEAD].bitcast(I32), in_=x_rows[:, 0:AHEAD])
        nc.sync.dma_start(offs_t[:], offs)
        nc.sync.dma_start(out=xs_all[0:P:LINE, :].bitcast(I32), in_=x_scales[0].bitcast(I32))
        nc.sync.dma_start(out=x_all[:, AHEAD:T].bitcast(I32), in_=x_rows[:, AHEAD:T])
        for u in range(2):
            nc.sync.dma_start(out=w1_raw[u][:], in_=w1_rows[:, 2 * u : 2 * u + 2, :])
        nc.sync.dma_start(la_t[:], la)
        nc.sync.dma_start(lb_t[:], lb)

        xs_picked = keep.tile([P, S], U8, name="xs_picked", align_bytes=64)
        nc.vector.tensor_copy(xs_picked[:], xs_all[:].indirect(offs_t[:]))
        x_scale = keep.tile([P, S], U8, name="x_scale", align_bytes=64)
        nc.vector.tensor_copy(out=x_scale[:].bitcast(I32), in_=xs_picked[:].bitcast(I32))
        for r in range(1, 4):
            nc.sync.dma_start(out=x_scale[r:P:32, :].bitcast(I32), in_=xs_picked[LINE * r : P : 32, :].bitcast(I32))

        x_codes = keep.tile([P, S], U32, name="x_codes", align_bytes=64)
        w1_bf = [keep.tile([P, 2, P, PACK], BF16, name=f"w1_bf{e}", align_bytes=64) for e in range(2)]
        nc.vector.tensor_copy(x_codes[:], x_all[:].indirect(offs_t[:]))
        for u in range(2):
            by_byte = w1_raw[u][:].rearrange("p j (m e f) -> p f m e j", e=2, f=2)
            pair = slice(2 * u, 2 * u + 2)
            if u == 0:
                nc.vector.tensor_copy(out=w1_bf[0][:, :, :, pair].rearrange("p e m j -> p m e j"), in_=by_byte[:, 0])
            else:
                nc.vector.tensor_copy(out=w1_bf[0][:, 0, 0:SPLIT, pair], in_=by_byte[:, 0, 0:SPLIT, 0, :])
                nc.scalar.copy(out=w1_bf[0][:, 0, SPLIT:P, pair], in_=by_byte[:, 0, SPLIT:P, 0, :])
                nc.vector.tensor_copy(out=w1_bf[0][:, 1, :, pair], in_=by_byte[:, 0, :, 1, :])
            nc.scalar.copy(out=w1_bf[1][:, :, :, pair].rearrange("p e m j -> p m e j"), in_=by_byte[:, 1])

        w2_rows = w2.rearrange("(p j) c -> p j c", j=PACK)
        w2_first = keep.tile([P, PACK, P], F32, name="w2_first", tag="stage", align_bytes=256)
        nc.sync.dma_start(out=w2_first[:], in_=w2_rows[:, :, 3 * P : N])
        w2_second = keep.tile([P, 2, PACK, P], F32, name="w2_second", tag="words", align_bytes=256)
        for m in range(2):
            nc.sync.dma_start(out=w2_second[:, m], in_=w2_rows[:, :, m * P : (m + 1) * P])
        w2_rest = keep.tile([P, PACK, P], F32, name="w2_rest", tag="w1_raw0", align_bytes=256)
        nc.sync.dma_start(out=w2_rest[:], in_=w2_rows[:, :, 2 * P : 3 * P])
        gn_t = keep.tile([P, PACK], F32, name="gn_t", tag="w1_raw1", align_bytes=256)
        nc.sync.dma_start(out=gn_t[:], in_=gn.rearrange("(p j) o -> p (j o)", j=PACK))

        w1_codes = [keep.tile([P, P], U32, name=f"w1_codes{t}", align_bytes=64) for t in range(PACK)]
        w1_scales = [keep.tile([P, P], U8, name=f"w1_scales{t}", align_bytes=64) for t in range(PACK)]
        for t in range(PACK):
            nc.vector.quantize_mx(out=w1_codes[t][:].bitcast(FP8X4), scales=w1_scales[t][:],
                                  in_=w1_bf[SLOT[t] % 2][:, SLOT[t] // 2, :, :].rearrange("p m j -> p (m j)"))

        def first_product(t, dst, cols):
            nc.tensor.matmul_mx(out=dst, lhsT=w1_codes[t][:].bitcast(FP8X4), lhsT_scale=w1_scales[t][:],
                                rhs=x_codes[:, cols].bitcast(FP8X4), rhs_scale=x_scale[:, cols], start=True, stop=True)

        a = [keep.tile([P, V], F32, name=f"a{t}", tag=f"a{t}", align_bytes=64) for t in range(PACK)]
        h = [keep.tile([P, S], F32, name=f"h{t}", tag=f"h{t}", align_bytes=64) for t in range(PACK)]
        for n in range(4):
            cols = slice(n * P, (n + 1) * P)
            first_product(0, banks[n][:, 0:P], cols)
            if n == 0:
                nc.vector.tensor_copy(out=h[0][:, cols], in_=banks[n][:, 0:P])
            else:
                nc.scalar.copy(out=h[0][:, cols], in_=banks[n][:, 0:P])
        for t in range(1, PACK):
            first_product(t, banks[3 + t][:], slice(0, S))
        ON_SCALAR = (0, 1, 2)
        b = [keep.tile([P, V], F32, name=f"b{t}", tag=f"b{t}", align_bytes=64) for t in range(PACK)]
        gated = [keep.tile([P, V], F32, name=f"gated{t}", tag=f"gated{t}", align_bytes=64) for t in range(PACK)]

        total = keep.tile([P, V], F32, name="total", align_bytes=64)

        def gather(dst, t, offsets, lo=0, hi=V, on_vector=False):
            window = h[t][:].indirect(offsets[:, lo // 16 : hi // 16])
            if on_vector:
                nc.vector.tensor_copy(dst[t][:, lo:hi], window)
            else:
                nc.scalar.activation(out=dst[t][:, lo:hi], in_=window, func=ACT.Copy)

        def silu(t):
            nc.scalar.activation(out=gated[t][:], in_=a[t][:], func=ACT.Silu)

        def gather_and_add(t):
            nc.vector.tensor_tensor(b[t][:], h[t][:].indirect(lb_t[:]), gated[t][:], ALU.add)

        def scatter(t):
            if t in ON_SCALAR:
                nc.scalar.activation(out=h[t][:].indirect(lb_t[:]), in_=(total if t == 0 else b[t])[:], func=ACT.Copy)
            else:
                nc.vector.tensor_tensor(h[t][:].indirect(lb_t[:]), b[t][:], gated[t][:], ALU.add)

        def leave_psum(t):
            nc.scalar.copy(out=h[t][:], in_=banks[3 + t][:])

        w2_bf_first = keep.tile([P, P, PACK], BF16, name="w2_bf_first", align_bytes=64)
        w2_bf_second = keep.tile([P, 3, P, PACK], BF16, name="w2_bf_second", tag="stage", align_bytes=256)
        w2_codes = [keep.tile([P, P], U32, name="w2_codes0", tag="b3", align_bytes=64),
                    keep.tile([P, 3 * P], U32, name="w2_codes1", tag="gated3", align_bytes=64)]
        w2_scales = [keep.tile([P, w * P], U8, name=f"w2_scales{w}", align_bytes=64) for w in (1, 3)]

        def quantize_w2(lo, hi):
            if lo == 3:
                nc.vector.quantize_mx(out=w2_codes[0][:].bitcast(FP8X4), scales=w2_scales[0][:], in_=w2_bf_first[:].rearrange("p n j -> p (n j)"))
            else:
                cols = slice(lo * P, hi * P)
                nc.vector.quantize_mx(out=w2_codes[1][:, cols].bitcast(FP8X4), scales=w2_scales[1][:, cols],
                                      in_=w2_bf_second[:, lo:hi].rearrange("p m n j -> p (m n j)"))

        def w2_operand(m):
            key, lo = (0, 0) if m == 3 else (1, m * P)
            return w2_codes[key][:, lo : lo + P].bitcast(FP8X4), w2_scales[key][:, lo : lo + P]

        z_early = keep.tile([P, S * PACK], BF16, name="z_early", tag="a3", align_bytes=64)
        z_first = z_early[:, 0 : P * PACK]
        z_pairs = z_early[:, P * PACK :].rearrange("p (u n e) -> p u n e", u=2, e=2)
        pair_words = z_early[:, P * PACK :].bitcast(I32).rearrange("p (u n) -> p n u", u=2)

        def z_plane(t, lo, hi, on_vector=True):
            if lo == 0:
                dst = z_first.rearrange("p (n j) -> p n j", j=PACK)[:, :, SLOT[t]]
            else:
                dst = z_pairs[:, SLOT[t] // 2, lo - P : hi - P, SLOT[t] % 2]
            if on_vector:
                nc.vector.tensor_scalar(out=dst, in0=h[t][:, lo:hi], scalar1=gn_t[:, SLOT[t] : SLOT[t] + 1], scalar2=None, op0=ALU.mult)
            else:
                nc.scalar.activation(out=dst, in_=h[t][:, lo:hi], func=ACT.Copy, scale=gn_t[:, SLOT[t] : SLOT[t] + 1])

        z_bf, z_codes, z_scales = {0: z_first}, {}, {}

        def interleave(r, count=1):
            tile = keep.tile([P, count * P * PACK], BF16, name=f"z_bf{r}", align_bytes=64)
            for i in range(count):
                z_bf[r + i] = tile[:, i * P * PACK : (i + 1) * P * PACK]
            nc.vector.tensor_copy(out=tile[:].bitcast(I32).rearrange("p (n u) -> p n u", u=2), in_=pair_words[:, (r - 1) * P : (r - 1 + count) * P, :])

        def quantize_z(r):
            z_codes[r] = keep.tile([P, P], U32, name=f"z_codes{r}", align_bytes=64)
            z_scales[r] = keep.tile([P, P], U8, name=f"z_scales{r}", align_bytes=64)
            nc.vector.quantize_mx(out=z_codes[r][:].bitcast(FP8X4), scales=z_scales[r][:], in_=z_bf[r])

        def multiply(m, ranges, dst):
            codes, scales = w2_operand(m)
            for i, r in enumerate(ranges):
                nc.tensor.matmul_mx(out=dst[:, i * P : (i + 1) * P], lhsT=codes, lhsT_scale=scales,
                                    rhs=z_codes[r][:].bitcast(FP8X4), rhs_scale=z_scales[r][:], start=True, stop=True)

        out_blocks = out.rearrange("(m p) c -> p m c", p=P)

        def store(blocks, ranges, first_bank, on_vector=()):
            width = len(ranges) * P
            result = keep.tile([P, len(blocks), width], F32, name=f"result{blocks[0]}{ranges[0]}", align_bytes=256)
            if width == P:
                for i, m in enumerate(blocks):
                    multiply(m, ranges, banks[first_bank][:, i * P : (i + 1) * P])
                nc.scalar.copy(out=result[:].rearrange("p m c -> p (m c)"), in_=banks[first_bank][:, 0 : len(blocks) * P])
            else:
                for i, m in enumerate(blocks):
                    multiply(m, ranges, banks[first_bank + i])
                    copy = nc.vector.tensor_copy if m in on_vector else nc.scalar.copy
                    copy(out=result[:, i, :], in_=banks[first_bank + i][:, 0:width])
            nc.sync.dma_start(out=out_blocks[:, blocks[0] : blocks[-1] + 1, ranges[0] * P : ranges[0] * P + width], in_=result[:])

        nc.vector.tensor_copy(out=w2_bf_first[:].rearrange("p (g i) j -> p g j i", i=4), in_=w2_first[:].rearrange("p j (g i) -> p g j i", i=4))

        def round_w2(m):
            raw = w2_rest[:] if m == 2 else w2_second[:, m]
            nc.gpsimd.tensor_scalar(out=w2_bf_second[:, m], in0=raw.rearrange("p j n -> p n j"),
                                    scalar1=1.0, scalar2=0.0, op0=ALU.mult, op1=ALU.add)

        round_w2(0)
        round_w2(1)
        gather(a, 0, la_t, on_vector=True)
        gather(b, 0, lb_t, on_vector=True)
        leave_psum(1)
        silu(0)
        nc.gpsimd.tensor_tensor(total[:], b[0][:], gated[0][:], ALU.add)
        round_w2(2)
        leave_psum(2)
        leave_psum(3)
        gather(a, 1, la_t, on_vector=True)
        gather(a, 2, la_t, on_vector=True)
        gather(a, 3, la_t, on_vector=True)
        gather(b, 3, lb_t, on_vector=True)
        silu(1)
        silu(2)
        gather_and_add(1)
        gather_and_add(2)
        scatter(0)
        silu(3)
        scatter(3)
        scatter(1)
        scatter(2)
        for lo, hi in ((P, 2 * P), (2 * P, S)):
            for t in (1, 2):
                z_plane(t, lo, hi, on_vector=False)

        z_plane(0, 0, P)
        z_plane(1, 0, P)
        z_plane(3, 0, P)
        quantize_w2(0, 1)
        z_plane(2, 0, P)
        z_plane(0, P, 2 * P)
        z_plane(3, P, 2 * P)
        quantize_z(0)
        interleave(1)
        quantize_w2(1, 3)
        quantize_z(1)
        z_plane(0, 2 * P, S)
        z_plane(3, 2 * P, S)
        quantize_w2(3, 4)
        interleave(2)
        interleave(3)
        quantize_z(2)
        quantize_z(3)

        store((0,), (0,), 0)
        store((1, 2), (0,), 1)
        store((0, 1), (1,), 2)
        store((2,), (1,), 3)
        store((3,), (0, 1), 4)
        store((0,), (2, 3), 5, on_vector=(0,))
        store((1, 2), (2, 3), 6, on_vector=(2,))
        store((3,), (2, 3), 0)
